import numpy as np
import ml_dtypes


def mxq(x, axis, fmt="e4m3"):
    dtype, down = {"e4m3": (ml_dtypes.float8_e4m3fn, 7), "e5m2": (ml_dtypes.float8_e5m2, 14)}[fmt]
    v = np.moveaxis(np.asarray(x, np.float32).astype(ml_dtypes.bfloat16).astype(np.float64), axis, -1)
    blocks = v.reshape(v.shape[:-1] + (-1, 32))
    amax = np.abs(blocks).max(-1, keepdims=True)
    byte = np.maximum(np.where(amax > 0, np.frexp(amax)[1] - 1 + 127, 0) - down, 1)
    scale = np.exp2(byte - 127.0)
    codes = (blocks / scale).astype(np.float32).astype(dtype).astype(np.float64)
    return np.moveaxis((codes * scale).reshape(v.shape), -1, axis)


WIDE = False


def mx_kscale(k):
    if not WIDE:
        return np.ones(k)
    levels = np.array([18, -18])
    if k % 512:
        return np.exp2(np.random.permutation(np.resize(levels, k // 32))).repeat(32)
    a = np.empty((k // 512, 16))
    for p in range(k // 512):
        a[p, :8] = np.random.permutation(np.resize(levels, 8))
        for g in range(8):
            far = levels[np.abs(levels - a[p, g]) >= 10]
            a[p, g + 8] = far[np.random.randint(len(far))]
    return np.exp2(a.ravel()).repeat(32)


def f64(x):
    return np.asarray(x).astype(np.float64)


def striped(idx):
    return np.tile(np.asarray(idx).reshape(-1, 16).T, (8, 1)).astype(np.uint16)


def unstriped(offs):
    return offs[:16].T.reshape(-1).astype(np.int64)


def setup_inputs():
    n = np.random.standard_normal
    uni = np.random.uniform
    idx = np.random.permutation(2048)[:512]
    f_d = mx_kscale(512)
    f_r = mx_kscale(512)
    return {
        "vT": (n((512, 2048)) * f_d[:, None]).astype(np.float32),
        "x": (n((512, 512)) / np.sqrt(512) * f_r[:, None] / f_d[None, :]).astype(np.float32),
        "cs": np.tile(uni(0.75, 1.3, 512) / f_d, (128, 1)).astype(np.float32),
        "gl": np.tile(uni(10.0, 30.0, 2048), (128, 1)).astype(np.float32),
        "y": (n((512, 512))).astype(np.float32),
        "us": (uni(0.75, 1.3, (512, 1)) / f_r[:, None]).astype(np.float32),
        "wt": (uni(0.75, 1.3, (512, 1)) / np.sqrt(512)).astype(np.float32),
        "offs": striped(idx),
    }


def reference(vT, x, cs, gl, y, us, wt, offs):
    idx = unstriped(offs)
    vT_i = f64(vT)[:, idx]
    gl_i = f64(gl)[:1][:, idx]
    gc = gl_i.T
    vt = vT_i.T
    nn = (np.square(f64(cs)[:1] * vt)).sum(-1, keepdims=True)
    len = np.sqrt(nn)
    lr = len.T
    a = mxq(f64(x), 1, "e4m3") @ mxq(vT_i, 0, "e4m3")
    g = f64(wt) * f64(us) * (f64(us) * gl_i * a / lr - f64(y))
    b = mxq(g, 0, "e5m2").T @ mxq(f64(x), 0, "e4m3")
    dg = (b * vt).sum(-1, keepdims=True)
    dvt = gc / len * (b - dg / nn * np.square(f64(cs)[:1]) * vt)
    dvd = dvt.T
    out_0 = np.zeros((512, 2048))
    out_0[:, idx] = dvd
    gg = dg / len
    out_1 = gg.T
    return out_0, out_1

@@ -1,0 +1,310 @@
+from contextlib import ExitStack
+
+import concourse.mybir as mybir
+from concourse.masks import make_identity
+
+D, R, N, T = 512, 512, 512, 2048
+FLOPS = 2 * 2 * D * R * N
+
+F32 = mybir.dt.float32
+BF16 = mybir.dt.bfloat16
+U32 = mybir.dt.uint32
+U16 = mybir.dt.uint16
+U8 = mybir.dt.uint8
+E4M3 = mybir.dt.float8_e4m3fn_x4
+E5M2 = mybir.dt.float8_e5m2_x4
+ACT = mybir.ActivationFunctionType
+ALU = mybir.AluOpType
+
+P = 128
+PACK = 4
+CHUNKS = N // P
+COLS = P // 16
+KV_ON_VECTOR = (0, 1, 2, 3)
+
+
+def tile_attend_gwnorm_vg_kernel(tc, vT, x, cs, gl, y, us, wt, offs, out_0, out_1):
+    nc = tc.nc
+    with ExitStack() as ctx:
+        keep = ctx.enter_context(tc.tile_pool(name="keep", bufs=1))
+        ring = ctx.enter_context(tc.tile_pool(name="ring", bufs=2))
+        psum = ctx.enter_context(tc.psum_pool(name="psum", bufs=2))
+
+        def turn(dst, src, start=True, stop=True):
+            nc.tensor.matmul(dst, src, ident[:], start=start, stop=stop, is_transpose=True)
+
+        def slots(c0, c1):
+            return offsets[:, c0 * COLS : c1 * COLS]
+
+        offsets = keep.tile([P, N // 16], U16, name="offsets")
+        gl_row = keep.tile([1, T], F32, name="gl_row")
+        nc.sync.dma_start(gl_row[:], gl[0:1, :])
+        xs = keep.tile([P, PACK, D], F32, name="xs")
+        nc.sync.dma_start(xs[:], x.rearrange("(p t) d -> p t d", t=PACK))
+        nc.sync.dma_start(offsets[:], offs)
+        cs4 = keep.tile([P, PACK], F32, name="cs4")
+        nc.sync.dma_start(cs4[:], cs[0:1, :].rearrange("o (p j) -> p (o j)", j=PACK))
+        us4 = keep.tile([P, PACK], F32, name="us4")
+        nc.sync.dma_start(us4[:], us.rearrange("(p t) o -> p (t o)", t=PACK))
+        wt4 = keep.tile([P, PACK], F32, name="wt4")
+        nc.sync.dma_start(wt4[:], wt.rearrange("(p t) o -> p (t o)", t=PACK))
+        v_planes = vT.rearrange("(p j) n -> p j n", j=PACK)
+        gl_win = keep.tile([P, T], F32, name="gl_win")
+        nc.vector.memset(gl_win[:], 0.0)
+        nc.scalar.activation(gl_win[0:1, :], gl_row[:], ACT.Copy)
+        v_win = []
+        for j in range(PACK):
+            w = keep.tile([P, T], F32, name=f"v_win{j}")
+            nc.sync.dma_start(w[:], v_planes[:, j, :])
+            v_win.append(w)
+        y_rows = y.rearrange("(p t) i -> p t i", t=PACK)
+        ys = []
+        for h in range(2):
+            yh = keep.tile([P, PACK, N // 2], F32, name=f"ys{h}")
+            nc.sync.dma_start(yh[:], y_rows[:, :, h * (N // 2) : (h + 1) * (N // 2)])
+            ys.append(yh)
+
+
+        ident = keep.tile([P, P], F32, name="ident")
+        make_identity(nc, ident[:])
+        gg = keep.tile([P, P], F32, name="gg")
+        nc.gpsimd.memset(gg[:], 0.0)
+        out_win = []
+        for j in range(PACK):
+            w = keep.tile([P, T], F32, name=f"out_win{j}")
+            (nc.vector if j == 0 else nc.gpsimd).memset(w[:], 0.0)
+            out_win.append(w)
+
+        c2n = keep.tile([P, PACK], F32, name="c2n")
+        nc.vector.scalar_tensor_tensor(c2n[:], wt4[:], -1.0, us4[:], ALU.mult, ALU.mult)
+        c1 = keep.tile([P, PACK], F32, name="c1")
+        nc.vector.scalar_tensor_tensor(c1[:], c2n[:], -1.0, us4[:], ALU.mult, ALU.mult)
+        cs2 = keep.tile([P, PACK], F32, name="cs2")
+        nc.vector.tensor_tensor(cs2[:], cs4[:], cs4[:], ALU.mult)
+
+        x_by_j = xs[:].rearrange("p t (m j) -> p t j m", j=PACK)
+        xd = keep.tile([P, PACK, P, PACK], BF16, name="xd", align_bytes=64)
+        for t in range(PACK):
+            bank = psum.tile([P, PACK, P], F32, name="x_bank", tag="ac"[t // 2])
+            for j in range(PACK):
+                turn(bank[:, j, :], x_by_j[:, t, j, :])
+            nc.scalar.copy(xd[:, t, :, :], bank[:].rearrange("m j p -> m p j"))
+        xd_codes = keep.tile([P, R], U32, name="xd_codes", align_bytes=64)
+        xd_scales = keep.tile([P, R], U8, name="xd_scales", align_bytes=64)
+        xr = keep.tile([P, PACK, P, PACK], BF16, name="xr", align_bytes=64)
+        xr_codes = keep.tile([P, D], U32, name="xr_codes", align_bytes=64)
+        xr_scales = keep.tile([P, D], U8, name="xr_scales", align_bytes=64)
+
+        vg = keep.tile([P, PACK, N], F32, name="vg")
+        vt = keep.tile([P, CHUNKS, PACK, P], F32, name="vt")
+        nn_bank = [psum.tile([P, 2, P], F32, name=f"nn_bank{h}", tag=f"n{h}", bufs=1) for h in range(2)]
+
+        def plane(j, pieces):
+            sq = ring.tile([P, N], F32, name="sq")
+            step = CHUNKS // pieces
+            for c0 in range(0, CHUNKS, step):
+                cols = slice(c0 * P, (c0 + step) * P)
+                nc.vector.tensor_copy(vg[:, j, cols], v_win[j][:].indirect(slots(c0, c0 + step)))
+                nc.scalar.activation(sq[:, cols], vg[:, j, cols], ACT.Square, scale=cs4[:, j : j + 1])
+                for c in range(c0, c0 + step):
+                    turn(nn_bank[c // 2][:, c % 2, :], sq[:, c * P : (c + 1) * P],
+                         start=(j == 0 and c % 2 == 0), stop=(j == PACK - 1 and c % 2 == 1))
+
+        def plane_turned(j):
+            if j < PACK - 1:
+                bank = psum.tile([P, CHUNKS, P], F32, name="v_bank", tag="b")
+            else:
+                bank = psum.tile([P, CHUNKS, P], F32, name="v_bank", tag="n1", bufs=1)
+            for c in range(CHUNKS):
+                turn(bank[:, c, :], vg[:, j, c * P : (c + 1) * P])
+            nc.scalar.copy(vt[:, :, j, :], bank[:])
+
+        gl_g = keep.tile([P, N], F32, name="gl_g")
+        nc.vector.tensor_copy(gl_g[:], gl_win[:].indirect(offsets[:]))
+        bank = psum.tile([P, CHUNKS, P], F32, name="gl_bank", tag="b")
+        for c in range(CHUNKS):
+            turn(bank[:, c, :], gl_g[:, c * P : (c + 1) * P])
+        gl_col = keep.tile([P, CHUNKS], F32, name="gl_col")
+        nc.scalar.copy(gl_col[:], bank[:, :, 0])
+        plane(0, 1)
+        plane_turned(0)
+        nc.vector.quantize_mx(xd_codes[:].bitcast(E4M3), xd_scales[:], xd[:].rearrange("m t p j -> m (t p j)"))
+        plane(1, 1)
+        plane_turned(1)
+        nc.vector.tensor_copy(xr[:].rearrange("p j m t -> p m t j"), xs[:].rearrange("p t (m j) -> p m t j", j=PACK))
+        plane(2, 1)
+        plane_turned(2)
+        nc.vector.quantize_mx(xr_codes[:].bitcast(E4M3), xr_scales[:], xr[:].rearrange("p j m t -> p (j m t)"))
+        plane(3, 2)
+
+        vi = keep.tile([P, N, PACK], BF16, name="vi", align_bytes=64)
+        v_codes = [keep.tile([P, N // 2], U32, name=f"v_codes{h}", tag=f"late{h}", align_bytes=64) for h in range(2)]
+        v_scales = keep.tile([P, N], U8, name="v_scales", align_bytes=64)
+        nn = keep.tile([P, CHUNKS], F32, name="nn")
+        half = N // 2
+
+        def v_interleave(h):
+            cols = slice(h * half, (h + 1) * half)
+            (nc.scalar.copy if h else nc.vector.tensor_copy)(vi[:, cols, :].rearrange("p (c i) j -> p c j i", i=4),
+                                  vg[:, :, cols].rearrange("p j (c i) -> p c j i", i=4))
+
+        def v_quantise(h):
+            cols = slice(h * half, (h + 1) * half)
+            nc.vector.quantize_mx(v_codes[h][:].bitcast(E4M3), v_scales[:, cols],
+                                  vi[:, cols, :].rearrange("p i j -> p (i j)"))
+
+        length = keep.tile([P, CHUNKS], F32, name="length")
+        rl = keep.tile([P, CHUNKS], F32, name="rl")
+        s = keep.tile([P, CHUNKS], F32, name="s")
+        m2 = keep.tile([P, CHUNKS], F32, name="m2")
+        s_row, a_banks, gb, gi, b_banks, sb, kv = {}, {}, {}, {}, {}, {}, {}
+
+        us_ = {}
+
+        def lengths(h):
+            two = slice(2 * h, 2 * h + 2)
+            nc.vector.tensor_reduce(nn[:, two], nn_bank[h][:], mybir.AxisListType.X, ALU.add)
+            nc.vector.reciprocal(length[:, two], nn[:, two])
+            nc.scalar.activation(rl[:, two], length[:, two], ACT.Sqrt)
+            for c in range(2 * h, 2 * h + 2):
+                nc.scalar.activation(s[:, c : c + 1], rl[:, c : c + 1], ACT.Copy, scale=gl_col[:, c : c + 1])
+            bank = psum.tile([P, 2, P], F32, name="s_bank", tag=f"n{h}", bufs=1)
+            for e in range(2):
+                turn(bank[:, e, :], s[:, 2 * h + e : 2 * h + e + 1].to_broadcast([P, P]))
+            s_row[h] = keep.tile([P, half], F32, name=f"s_row{h}")
+            nc.scalar.copy(s_row[h][:], bank[:].rearrange("p e i -> p (e i)"))
+
+        def scores(h):
+            cols = slice(h * half, (h + 1) * half)
+            for t in range(PACK):
+                if t % 2 == 0:
+                    if h == 1 and t == 0:
+                        bank = psum.tile([P, 2, half], F32, name="a_bank", tag="n0", bufs=1)
+                    else:
+                        bank = psum.tile([P, 2, half], F32, name="a_bank", tag="ab"[h])
+                a_banks[h, t] = bank[:, t % 2, :]
+                rows = slice(t * P, (t + 1) * P)
+                nc.tensor.matmul_mx(a_banks[h, t], xd_codes[:, rows].bitcast(E4M3), xd_scales[:, rows],
+                                    v_codes[h][:].bitcast(E4M3), v_scales[:, cols], start=True, stop=True)
+
+        def scaled(h):
+            us_[h] = ring.tile([P, PACK, half], F32, name="u")
+            for t in range(PACK):
+                nc.vector.scalar_tensor_tensor(us_[h][:, t, :], a_banks[h, t], c1[:, t : t + 1], s_row[h][:], ALU.mult, ALU.mult)
+
+        def targets(h):
+            gb[h] = keep.tile([P, PACK, half], F32, name=f"y2_{h}", tag="late1" if h else "y2", align_bytes=64)
+            for t in range(PACK):
+                if h == 0:
+                    nc.vector.tensor_scalar(gb[h][:, t, :], ys[h][:, t, :], c2n[:, t : t + 1], None, ALU.mult)
+                else:
+                    nc.scalar.activation(gb[h][:, t, :], ys[h][:, t, :], ACT.Copy, scale=c2n[:, t : t + 1])
+
+        def gradient(h):
+            u = us_[h]
+            for e in range(2):
+                c = 2 * h + e
+                gi[c] = keep.tile([P, P, PACK], BF16, name=f"gi{c}", align_bytes=64)
+                nc.vector.tensor_tensor(gi[c][:].rearrange("p (c i) t -> p c t i", i=4),
+                                        u[:, :, e * P : (e + 1) * P].rearrange("p t (c i) -> p c t i", i=4),
+                                        gb[h][:, :, e * P : (e + 1) * P].rearrange("p t (c i) -> p c t i", i=4), ALU.add)
+
+        def back(c):
+            g_codes = keep.tile([P, P], U32, name=f"g_codes{c}", align_bytes=64)
+            g_scales = keep.tile([P, P], U8, name=f"g_scales{c}", align_bytes=64)
+            nc.vector.quantize_mx(g_codes[:].bitcast(E5M2), g_scales[:], gi[c][:].rearrange("p i t -> p (i t)"))
+            b_banks[c] = psum.tile([P, D], F32, name="b_bank", tag="cb"[c // 2])
+            nc.tensor.matmul_mx(b_banks[c][:], g_codes[:].bitcast(E5M2), g_scales[:],
+                                xr_codes[:].bitcast(E4M3), xr_scales[:], start=True, stop=True)
+
+        lengths(0)
+        v_interleave(0)
+        lengths(1)
+        v_quantise(0)
+        scores(0)
+        v_interleave(1)
+        v_quantise(1)
+        scores(1)
+        nc.vector.scalar_tensor_tensor(m2[:], s[:], -1.0, rl[:], ALU.mult, ALU.mult)
+        plane_turned(3)
+        targets(0)
+        targets(1)
+
+        def along(c):
+            vt_c = vt[:, c, :, :].rearrange("p j m -> p (j m)")
+            prod = ring.tile([P, D], F32, name="prod")
+            nc.vector.scalar_tensor_tensor(prod[:], b_banks[c][:], rl[:, c : c + 1], vt_c, ALU.mult, ALU.mult,
+                                           accum_out=gg[:, c : c + 1])
+            sb[c] = keep.tile([P, D], F32, name=f"sb{c}")
+            nc.scalar.activation(sb[c][:], b_banks[c][:], ACT.Copy, scale=s[:, c : c + 1])
+            kv[c] = keep.tile([P, D], F32, name=f"kv{c}")
+            if c in KV_ON_VECTOR:
+                nc.vector.tensor_scalar(kv[c][:], vt_c, gg[:, c : c + 1], m2[:, c : c + 1], ALU.mult, ALU.mult)
+            else:
+                k = keep.tile([P, 1], F32, name=f"k{c}")
+                nc.scalar.activation(k[:], gg[:, c : c + 1], ACT.Copy, scale=m2[:, c : c + 1])
+                nc.scalar.activation(kv[c][:], vt_c, ACT.Copy, scale=k[:])
+
+        def first_chunk():
+            sb_bank = psum.tile([P, PACK, P], F32, name="sb_bank", tag="a")
+            kv_bank = psum.tile([P, PACK, P], F32, name="kv_bank", tag="n1", bufs=1)
+            for j in range(PACK):
+                turn(sb_bank[:, j, :], sb[0][:, j * P : (j + 1) * P])
+            for j in range(PACK):
+                turn(kv_bank[:, j, :], kv[0][:, j * P : (j + 1) * P])
+            sb_t = keep.tile([P, PACK, P], F32, name="sb_first")
+            kv_t = keep.tile([P, PACK, P], F32, name="kv_first")
+            nc.scalar.copy(sb_t[:], sb_bank[:])
+            for j in range(PACK):
+                nc.scalar.activation(kv_t[:, j, :], kv_bank[:, j, :], ACT.Copy, scale=cs2[:, j : j + 1])
+            firsts.extend([sb_t, kv_t])
+
+        def place_first():
+            for j in range(PACK):
+                nc.vector.tensor_tensor(out_win[j][:].indirect(slots(0, 1)), firsts[0][:, j, :], firsts[1][:, j, :], ALU.add)
+
+        out_planes = out_0.rearrange("(p j) n -> p j n", j=PACK)
+        firsts, done = [], []
+
+        def finish(j, c0, c1):
+            sb_bank = psum.tile([P, c1 - c0, P], F32, name="sb_bank", tag="a")
+            kv_bank = psum.tile([P, c1 - c0, P], F32, name="kv_bank", tag=f"n{len(done) % 2}", bufs=1)
+            done.append(j)
+            for c in range(c0, c1):
+                turn(sb_bank[:, c - c0, :], sb[c][:, j * P : (j + 1) * P])
+            for c in range(c0, c1):
+                turn(kv_bank[:, c - c0, :], kv[c][:, j * P : (j + 1) * P])
+            sb_t = keep.tile([P, (c1 - c0) * P], F32, name=f"sb_t{j}_{c0}")
+            kv_t = keep.tile([P, (c1 - c0) * P], F32, name=f"kv_t{j}_{c0}")
+            nc.scalar.copy(sb_t[:], sb_bank[:].rearrange("p c i -> p (c i)"))
+            nc.scalar.activation(kv_t[:], kv_bank[:].rearrange("p c i -> p (c i)"), ACT.Copy, scale=cs2[:, j : j + 1])
+            nc.vector.tensor_tensor(out_win[j][:].indirect(slots(c0, c1)), sb_t[:], kv_t[:], ALU.add)
+            if c1 == CHUNKS:
+                nc.sync.dma_start(out_planes[:, j, :], out_win[j][:])
+
+        def lengths_gradient():
+            gg_bank = psum.tile([P, P], F32, name="gg_bank", tag="c")
+            turn(gg_bank[:], gg[:])
+            gg_rows = keep.tile([32, P], F32, name="gg_rows")
+            nc.scalar.copy(gg_rows[:], gg_bank[0:32, :])
+            nc.sync.dma_start(out_1.rearrange("o (c i) -> (o c) i", c=CHUNKS), gg_rows[0:CHUNKS, :])
+
+        scaled(0)
+        gradient(0)
+        scaled(1)
+        back(0)
+        back(1)
+        gradient(1)
+        back(2)
+        back(3)
+        along(0)
+        along(1)
+        first_chunk()
+        along(2)
+        along(3)
+        place_first()
+        finish(0, 1, 4)
+        finish(1, 1, 4)
+        lengths_gradient()
+        finish(2, 1, 4)
+        finish(3, 1, 4)

@@ -20,6 +20,7 @@ P = 128
 PACK = 4
 CHUNKS = N // P
 COLS = P // 16
+Y_ON_VECTOR = 8
 KV_ON_VECTOR = (0, 1, 2, 3)
 
 
@@ -40,7 +41,9 @@ def tile_attend_gwnorm_vg_kernel(tc, vT, x, cs, gl, y, us, wt, offs, out_0, out_
         gl_row = keep.tile([1, T], F32, name="gl_row")
         nc.sync.dma_start(gl_row[:], gl[0:1, :])
         xs = keep.tile([P, PACK, D], F32, name="xs")
-        nc.sync.dma_start(xs[:], x.rearrange("(p t) d -> p t d", t=PACK))
+        x_rows = x.rearrange("(p t) d -> p t d", t=PACK)
+        for t in range(0, PACK, 2):
+            nc.sync.dma_start(xs[:, t : t + 2, :], x_rows[:, t : t + 2, :])
         nc.sync.dma_start(offsets[:], offs)
         cs4 = keep.tile([P, PACK], F32, name="cs4")
         nc.sync.dma_start(cs4[:], cs[0:1, :].rearrange("o (p j) -> p (o j)", j=PACK))
@@ -72,7 +75,7 @@ def tile_attend_gwnorm_vg_kernel(tc, vT, x, cs, gl, y, us, wt, offs, out_0, out_
         out_win = []
         for j in range(PACK):
             w = keep.tile([P, T], F32, name=f"out_win{j}")
-            (nc.vector if j == 0 else nc.gpsimd).memset(w[:], 0.0)
+            (nc.vector if j < 2 else nc.gpsimd).memset(w[:], 0.0)
             out_win.append(w)
 
         c2n = keep.tile([P, PACK], F32, name="c2n")
@@ -114,7 +117,7 @@ def tile_attend_gwnorm_vg_kernel(tc, vT, x, cs, gl, y, us, wt, offs, out_0, out_
             if j < PACK - 1:
                 bank = psum.tile([P, CHUNKS, P], F32, name="v_bank", tag="b")
             else:
-                bank = psum.tile([P, CHUNKS, P], F32, name="v_bank", tag="n1", bufs=1)
+                bank = psum.tile([P, CHUNKS, P], F32, name="v_bank", tag="c")
             for c in range(CHUNKS):
                 turn(bank[:, c, :], vg[:, j, c * P : (c + 1) * P])
             nc.scalar.copy(vt[:, :, j, :], bank[:])
@@ -131,7 +134,9 @@ def tile_attend_gwnorm_vg_kernel(tc, vT, x, cs, gl, y, us, wt, offs, out_0, out_
         nc.vector.quantize_mx(xd_codes[:].bitcast(E4M3), xd_scales[:], xd[:].rearrange("m t p j -> m (t p j)"))
         plane(1, 1)
         plane_turned(1)
-        nc.vector.tensor_copy(xr[:].rearrange("p j m t -> p m t j"), xs[:].rearrange("p t (m j) -> p m t j", j=PACK))
+        for m in range(0, P, P // 2):
+            nc.scalar.copy(xr[:].rearrange("p j m t -> p m t j")[:, m : m + P // 2],
+                           xs[:].rearrange("p t (m j) -> p m t j", j=PACK)[:, m : m + P // 2])
         plane(2, 1)
         plane_turned(2)
         nc.vector.quantize_mx(xr_codes[:].bitcast(E4M3), xr_scales[:], xr[:].rearrange("p j m t -> p (j m t)"))
@@ -168,46 +173,39 @@ def tile_attend_gwnorm_vg_kernel(tc, vT, x, cs, gl, y, us, wt, offs, out_0, out_
             nc.scalar.activation(rl[:, two], length[:, two], ACT.Sqrt)
             for c in range(2 * h, 2 * h + 2):
                 nc.scalar.activation(s[:, c : c + 1], rl[:, c : c + 1], ACT.Copy, scale=gl_col[:, c : c + 1])
-            bank = psum.tile([P, 2, P], F32, name="s_bank", tag=f"n{h}", bufs=1)
-            for e in range(2):
-                turn(bank[:, e, :], s[:, 2 * h + e : 2 * h + e + 1].to_broadcast([P, P]))
-            s_row[h] = keep.tile([P, half], F32, name=f"s_row{h}")
-            nc.scalar.copy(s_row[h][:], bank[:].rearrange("p e i -> p (e i)"))
 
         def scores(h):
-            cols = slice(h * half, (h + 1) * half)
-            for t in range(PACK):
-                if t % 2 == 0:
-                    if h == 1 and t == 0:
-                        bank = psum.tile([P, 2, half], F32, name="a_bank", tag="n0", bufs=1)
-                    else:
-                        bank = psum.tile([P, 2, half], F32, name="a_bank", tag="ab"[h])
-                a_banks[h, t] = bank[:, t % 2, :]
-                rows = slice(t * P, (t + 1) * P)
-                nc.tensor.matmul_mx(a_banks[h, t], xd_codes[:, rows].bitcast(E4M3), xd_scales[:, rows],
-                                    v_codes[h][:].bitcast(E4M3), v_scales[:, cols], start=True, stop=True)
+            for c in range(2 * h, 2 * h + 2):
+                cols = slice(c * P, (c + 1) * P)
+                a_banks[c] = psum.tile([P, R], F32, name="a_bank", tag="ab"[h])
+                nc.tensor.matmul_mx(a_banks[c][:], v_codes[h][:, (c % 2) * P : (c % 2 + 1) * P].bitcast(E4M3), v_scales[:, cols],
+                                    xd_codes[:].bitcast(E4M3), xd_scales[:], start=True, stop=True)
 
-        def scaled(h):
-            us_[h] = ring.tile([P, PACK, half], F32, name="u")
+        def scaled(c):
+            u = ring.tile([P, PACK, P], F32, name="u", bufs=CHUNKS)
+            nc.scalar.activation(u[:].rearrange("p t m -> p (t m)"), a_banks[c][:], ACT.Copy, scale=s[:, c : c + 1])
+            if c < 2:
+                us_[c] = psum.tile([P, PACK, P], F32, name="u_bank", tag=f"n{c}", bufs=1)
+            else:
+                us_[c] = psum.tile([P, PACK, P], F32, name="u_bank", tag="a")
             for t in range(PACK):
-                nc.vector.scalar_tensor_tensor(us_[h][:, t, :], a_banks[h, t], c1[:, t : t + 1], s_row[h][:], ALU.mult, ALU.mult)
+                turn(us_[c][:, t, :], u[:, t, :])
 
         def targets(h):
-            gb[h] = keep.tile([P, PACK, half], F32, name=f"y2_{h}", tag="late1" if h else "y2", align_bytes=64)
+            gb[h] = keep.tile([P, PACK, half], F32, name=f"y2_{h}", align_bytes=64)
             for t in range(PACK):
-                if h == 0:
+                if h * PACK + t < Y_ON_VECTOR:
                     nc.vector.tensor_scalar(gb[h][:, t, :], ys[h][:, t, :], c2n[:, t : t + 1], None, ALU.mult)
                 else:
                     nc.scalar.activation(gb[h][:, t, :], ys[h][:, t, :], ACT.Copy, scale=c2n[:, t : t + 1])
 
-        def gradient(h):
-            u = us_[h]
-            for e in range(2):
-                c = 2 * h + e
-                gi[c] = keep.tile([P, P, PACK], BF16, name=f"gi{c}", align_bytes=64)
-                nc.vector.tensor_tensor(gi[c][:].rearrange("p (c i) t -> p c t i", i=4),
-                                        u[:, :, e * P : (e + 1) * P].rearrange("p t (c i) -> p c t i", i=4),
-                                        gb[h][:, :, e * P : (e + 1) * P].rearrange("p t (c i) -> p c t i", i=4), ALU.add)
+        def gradient(c):
+            flat = ring.tile([P, PACK, P], BF16, name="flat", bufs=CHUNKS)
+            for t in range(PACK):
+                nc.vector.scalar_tensor_tensor(flat[:, t, :], us_[c][:, t, :], c1[:, t : t + 1],
+                                               gb[c // 2][:, t, (c % 2) * P : (c % 2 + 1) * P], ALU.mult, ALU.add)
+            gi[c] = keep.tile([P, P, PACK], BF16, name=f"gi{c}", align_bytes=64)
+            nc.scalar.copy(gi[c][:].rearrange("p (c i) t -> p c t i", i=4), flat[:].rearrange("p t (c i) -> p c t i", i=4))
 
         def back(c):
             g_codes = keep.tile([P, P], U32, name=f"g_codes{c}", align_bytes=64)
@@ -246,7 +244,7 @@ def tile_attend_gwnorm_vg_kernel(tc, vT, x, cs, gl, y, us, wt, offs, out_0, out_
                 nc.scalar.activation(kv[c][:], vt_c, ACT.Copy, scale=k[:])
 
         def first_chunk():
-            sb_bank = psum.tile([P, PACK, P], F32, name="sb_bank", tag="a")
+            sb_bank = psum.tile([P, PACK, P], F32, name="sb_bank", tag="n0", bufs=1)
             kv_bank = psum.tile([P, PACK, P], F32, name="kv_bank", tag="n1", bufs=1)
             for j in range(PACK):
                 turn(sb_bank[:, j, :], sb[0][:, j * P : (j + 1) * P])
@@ -290,11 +288,15 @@ def tile_attend_gwnorm_vg_kernel(tc, vT, x, cs, gl, y, us, wt, offs, out_0, out_
             nc.sync.dma_start(out_1.rearrange("o (c i) -> (o c) i", c=CHUNKS), gg_rows[0:CHUNKS, :])
 
         scaled(0)
-        gradient(0)
         scaled(1)
+        scaled(2)
+        scaled(3)
+        gradient(0)
+        gradient(1)
+        gradient(2)
+        gradient(3)
         back(0)
         back(1)
-        gradient(1)
         back(2)
         back(3)
         along(0)

@@ -38,6 +38,10 @@ def tile_attend_gwnorm_vg_kernel(tc, vT, x, cs, gl, y, us, wt, offs, out_0, out_
             return offsets[:, c0 * COLS : c1 * COLS]
 
         offsets = keep.tile([P, N // 16], U16, name="offsets")
+        warm = keep.tile([P, 1], F32, name="warm")
+        nc.vector.memset(warm[:], 1.0)
+        warmed = keep.tile([P, 1], F32, name="warmed")
+        nc.scalar.activation(warmed[:], warm[:], ACT.Abs_reciprocal_sqrt)
         gl_row = keep.tile([1, T], F32, name="gl_row")
         nc.sync.dma_start(gl_row[:], gl[0:1, :])
         xs = keep.tile([P, PACK, D], F32, name="xs")
@@ -53,11 +57,11 @@ def tile_attend_gwnorm_vg_kernel(tc, vT, x, cs, gl, y, us, wt, offs, out_0, out_
         nc.sync.dma_start(wt4[:], wt.rearrange("(p t) o -> p (t o)", t=PACK))
         v_planes = vT.rearrange("(p j) n -> p j n", j=PACK)
         gl_win = keep.tile([P, T], F32, name="gl_win")
-        nc.vector.memset(gl_win[:], 0.0)
+        nc.vector.memset(gl_win[:].bitcast(U32), 0)
         nc.scalar.activation(gl_win[0:1, :], gl_row[:], ACT.Copy)
         v_win = []
         for j in range(PACK):
-            w = keep.tile([P, T], F32, name=f"v_win{j}")
+            w = keep.tile([P, T], F32, name=f"v_win{j}", align_bytes=64)
             nc.sync.dma_start(w[:], v_planes[:, j, :])
             v_win.append(w)
         y_rows = y.rearrange("(p t) i -> p t i", t=PACK)
@@ -75,7 +79,7 @@ def tile_attend_gwnorm_vg_kernel(tc, vT, x, cs, gl, y, us, wt, offs, out_0, out_
         out_win = []
         for j in range(PACK):
             w = keep.tile([P, T], F32, name=f"out_win{j}")
-            (nc.vector if j < 2 else nc.gpsimd).memset(w[:], 0.0)
+            nc.vector.memset(w[:].bitcast(U32), 0)
             out_win.append(w)
 
         c2n = keep.tile([P, PACK], F32, name="c2n")
@@ -92,10 +96,10 @@ def tile_attend_gwnorm_vg_kernel(tc, vT, x, cs, gl, y, us, wt, offs, out_0, out_
             for j in range(PACK):
                 turn(bank[:, j, :], x_by_j[:, t, j, :])
             nc.scalar.copy(xd[:, t, :, :], bank[:].rearrange("m j p -> m p j"))
-        xd_codes = keep.tile([P, R], U32, name="xd_codes", align_bytes=64)
+        xd_codes = keep.tile([P, R], U32, name="xd_codes", tag="v_win1", align_bytes=64)
         xd_scales = keep.tile([P, R], U8, name="xd_scales", align_bytes=64)
         xr = keep.tile([P, PACK, P, PACK], BF16, name="xr", align_bytes=64)
-        xr_codes = keep.tile([P, D], U32, name="xr_codes", align_bytes=64)
+        xr_codes = keep.tile([P, D], U32, name="xr_codes", tag="v_win2", align_bytes=64)
         xr_scales = keep.tile([P, D], U8, name="xr_scales", align_bytes=64)
 
         vg = keep.tile([P, PACK, N], F32, name="vg")
@@ -117,11 +121,14 @@ def tile_attend_gwnorm_vg_kernel(tc, vT, x, cs, gl, y, us, wt, offs, out_0, out_
             if j < PACK - 1:
                 bank = psum.tile([P, CHUNKS, P], F32, name="v_bank", tag="b")
             else:
-                bank = psum.tile([P, CHUNKS, P], F32, name="v_bank", tag="c")
+                bank = psum.tile([P, CHUNKS, P], F32, name="v_bank", tag="a")
             for c in range(CHUNKS):
                 turn(bank[:, c, :], vg[:, j, c * P : (c + 1) * P])
             nc.scalar.copy(vt[:, :, j, :], bank[:])
 
+        for m in range(0, P, P // 2):
+            (nc.scalar.copy if m else nc.vector.tensor_copy)(xr[:].rearrange("p j m t -> p m t j")[:, m : m + P // 2],
+                           xs[:].rearrange("p t (m j) -> p m t j", j=PACK)[:, m : m + P // 2])
         gl_g = keep.tile([P, N], F32, name="gl_g")
         nc.vector.tensor_copy(gl_g[:], gl_win[:].indirect(offsets[:]))
         bank = psum.tile([P, CHUNKS, P], F32, name="gl_bank", tag="b")
@@ -134,15 +141,12 @@ def tile_attend_gwnorm_vg_kernel(tc, vT, x, cs, gl, y, us, wt, offs, out_0, out_
         nc.vector.quantize_mx(xd_codes[:].bitcast(E4M3), xd_scales[:], xd[:].rearrange("m t p j -> m (t p j)"))
         plane(1, 1)
         plane_turned(1)
-        for m in range(0, P, P // 2):
-            nc.scalar.copy(xr[:].rearrange("p j m t -> p m t j")[:, m : m + P // 2],
-                           xs[:].rearrange("p t (m j) -> p m t j", j=PACK)[:, m : m + P // 2])
         plane(2, 1)
         plane_turned(2)
         nc.vector.quantize_mx(xr_codes[:].bitcast(E4M3), xr_scales[:], xr[:].rearrange("p j m t -> p (j m t)"))
         plane(3, 2)
 
-        vi = keep.tile([P, N, PACK], BF16, name="vi", align_bytes=64)
+        vi = {}
         v_codes = [keep.tile([P, N // 2], U32, name=f"v_codes{h}", tag=f"late{h}", align_bytes=64) for h in range(2)]
         v_scales = keep.tile([P, N], U8, name="v_scales", align_bytes=64)
         nn = keep.tile([P, CHUNKS], F32, name="nn")
@@ -150,13 +154,14 @@ def tile_attend_gwnorm_vg_kernel(tc, vT, x, cs, gl, y, us, wt, offs, out_0, out_
 
         def v_interleave(h):
             cols = slice(h * half, (h + 1) * half)
-            (nc.scalar.copy if h else nc.vector.tensor_copy)(vi[:, cols, :].rearrange("p (c i) j -> p c j i", i=4),
+            vi[h] = keep.tile([P, half, PACK], BF16, name="vi", align_bytes=64)
+            nc.vector.tensor_copy(vi[h][:].rearrange("p (c i) j -> p c j i", i=4),
                                   vg[:, :, cols].rearrange("p j (c i) -> p c j i", i=4))
 
         def v_quantise(h):
             cols = slice(h * half, (h + 1) * half)
             nc.vector.quantize_mx(v_codes[h][:].bitcast(E4M3), v_scales[:, cols],
-                                  vi[:, cols, :].rearrange("p i j -> p (i j)"))
+                                  vi[h][:].rearrange("p i j -> p (i j)"))
 
         length = keep.tile([P, CHUNKS], F32, name="length")
         rl = keep.tile([P, CHUNKS], F32, name="rl")
@@ -168,18 +173,18 @@ def tile_attend_gwnorm_vg_kernel(tc, vT, x, cs, gl, y, us, wt, offs, out_0, out_
 
         def lengths(h):
             two = slice(2 * h, 2 * h + 2)
-            nc.vector.tensor_reduce(nn[:, two], nn_bank[h][:], mybir.AxisListType.X, ALU.add)
-            nc.vector.reciprocal(length[:, two], nn[:, two])
-            nc.scalar.activation(rl[:, two], length[:, two], ACT.Sqrt)
+            for e in range(2):
+                terms = ring.tile([P, P], F32, name="terms")
+                nc.scalar.activation(terms[:], nn_bank[h][:, e, :], ACT.Copy, accum_out=nn[:, 2 * h + e : 2 * h + e + 1])
+            nc.scalar.activation(rl[:, two], nn[:, two], ACT.Abs_reciprocal_sqrt)
             for c in range(2 * h, 2 * h + 2):
                 nc.scalar.activation(s[:, c : c + 1], rl[:, c : c + 1], ACT.Copy, scale=gl_col[:, c : c + 1])
 
-        def scores(h):
-            for c in range(2 * h, 2 * h + 2):
-                cols = slice(c * P, (c + 1) * P)
-                a_banks[c] = psum.tile([P, R], F32, name="a_bank", tag="ab"[h])
-                nc.tensor.matmul_mx(a_banks[c][:], v_codes[h][:, (c % 2) * P : (c % 2 + 1) * P].bitcast(E4M3), v_scales[:, cols],
-                                    xd_codes[:].bitcast(E4M3), xd_scales[:], start=True, stop=True)
+        def scores(c):
+            cols = slice(c * P, (c + 1) * P)
+            a_banks[c] = psum.tile([P, R], F32, name="a_bank", tag="b" if c == 2 else "a")
+            nc.tensor.matmul_mx(a_banks[c][:], v_codes[c // 2][:, (c % 2) * P : (c % 2 + 1) * P].bitcast(E4M3), v_scales[:, cols],
+                                xd_codes[:].bitcast(E4M3), xd_scales[:], start=True, stop=True)
 
         def scaled(c):
             u = ring.tile([P, PACK, P], F32, name="u", bufs=CHUNKS)
@@ -187,7 +192,7 @@ def tile_attend_gwnorm_vg_kernel(tc, vT, x, cs, gl, y, us, wt, offs, out_0, out_
             if c < 2:
                 us_[c] = psum.tile([P, PACK, P], F32, name="u_bank", tag=f"n{c}", bufs=1)
             else:
-                us_[c] = psum.tile([P, PACK, P], F32, name="u_bank", tag="a")
+                us_[c] = psum.tile([P, PACK, P], F32, name="u_bank", tag="c")
             for t in range(PACK):
                 turn(us_[c][:, t, :], u[:, t, :])
 
@@ -211,7 +216,7 @@ def tile_attend_gwnorm_vg_kernel(tc, vT, x, cs, gl, y, us, wt, offs, out_0, out_
             g_codes = keep.tile([P, P], U32, name=f"g_codes{c}", align_bytes=64)
             g_scales = keep.tile([P, P], U8, name=f"g_scales{c}", align_bytes=64)
             nc.vector.quantize_mx(g_codes[:].bitcast(E5M2), g_scales[:], gi[c][:].rearrange("p i t -> p (i t)"))
-            b_banks[c] = psum.tile([P, D], F32, name="b_bank", tag="cb"[c // 2])
+            b_banks[c] = psum.tile([P, D], F32, name="b_bank", tag="ba"[c // 2])
             nc.tensor.matmul_mx(b_banks[c][:], g_codes[:].bitcast(E5M2), g_scales[:],
                                 xr_codes[:].bitcast(E4M3), xr_scales[:], start=True, stop=True)
 
@@ -220,11 +225,11 @@ def tile_attend_gwnorm_vg_kernel(tc, vT, x, cs, gl, y, us, wt, offs, out_0, out_
         lengths(1)
         v_quantise(0)
         scores(0)
+        scores(1)
         v_interleave(1)
         v_quantise(1)
-        scores(1)
+        scores(2)
         nc.vector.scalar_tensor_tensor(m2[:], s[:], -1.0, rl[:], ALU.mult, ALU.mult)
-        plane_turned(3)
         targets(0)
         targets(1)
 
@@ -265,7 +270,7 @@ def tile_attend_gwnorm_vg_kernel(tc, vT, x, cs, gl, y, us, wt, offs, out_0, out_
         firsts, done = [], []
 
         def finish(j, c0, c1):
-            sb_bank = psum.tile([P, c1 - c0, P], F32, name="sb_bank", tag="a")
+            sb_bank = psum.tile([P, c1 - c0, P], F32, name="sb_bank", tag="c")
             kv_bank = psum.tile([P, c1 - c0, P], F32, name="kv_bank", tag=f"n{len(done) % 2}", bufs=1)
             done.append(j)
             for c in range(c0, c1):
@@ -281,27 +286,29 @@ def tile_attend_gwnorm_vg_kernel(tc, vT, x, cs, gl, y, us, wt, offs, out_0, out_
                 nc.sync.dma_start(out_planes[:, j, :], out_win[j][:])
 
         def lengths_gradient():
-            gg_bank = psum.tile([P, P], F32, name="gg_bank", tag="c")
+            gg_bank = psum.tile([P, P], F32, name="gg_bank", tag="b")
             turn(gg_bank[:], gg[:])
             gg_rows = keep.tile([32, P], F32, name="gg_rows")
             nc.scalar.copy(gg_rows[:], gg_bank[0:32, :])
             nc.sync.dma_start(out_1.rearrange("o (c i) -> (o c) i", c=CHUNKS), gg_rows[0:CHUNKS, :])
 
         scaled(0)
+        scores(3)
         scaled(1)
         scaled(2)
         scaled(3)
         gradient(0)
-        gradient(1)
-        gradient(2)
-        gradient(3)
+        plane_turned(3)
         back(0)
+        gradient(1)
         back(1)
+        gradient(2)
         back(2)
+        gradient(3)
         back(3)
         along(0)
-        along(1)
         first_chunk()
+        along(1)
         along(2)
         along(3)
         place_first()

@@ -19,9 +19,11 @@ ALU = mybir.AluOpType
 P = 128
 PACK = 4
 CHUNKS = N // P
-COLS = P // 16
-Y_ON_VECTOR = 8
-KV_ON_VECTOR = (0, 1, 2, 3)
+HALF = N // 2
+LIST_COLS = P // 16
+LINE = 4
+QUADRANT = 32
+LAST = PACK - 1
 
 
 def tile_attend_gwnorm_vg_kernel(tc, vT, x, cs, gl, y, us, wt, offs, out_0, out_1):
@@ -31,23 +33,34 @@ def tile_attend_gwnorm_vg_kernel(tc, vT, x, cs, gl, y, us, wt, offs, out_0, out_
         ring = ctx.enter_context(tc.tile_pool(name="ring", bufs=2))
         psum = ctx.enter_context(tc.psum_pool(name="psum", bufs=2))
 
+        def bank(name, group, shape):
+            return psum.tile(shape, F32, name=name, tag=group, bufs=2 if group in ("a", "b", "c") else 1)
+
         def turn(dst, src, start=True, stop=True):
             nc.tensor.matmul(dst, src, ident[:], start=start, stop=stop, is_transpose=True)
 
         def slots(c0, c1):
-            return offsets[:, c0 * COLS : c1 * COLS]
+            return offsets[:, c0 * LIST_COLS : c1 * LIST_COLS]
+
+        def cols(c0, c1):
+            return slice(c0 * P, c1 * P)
+
+        def interleave(copy, dst, src):
+            copy(dst.rearrange("p (c i) j -> p c j i", i=LINE), src.rearrange("p j (c i) -> p c j i", i=LINE))
 
         offsets = keep.tile([P, N // 16], U16, name="offsets")
-        warm = keep.tile([P, 1], F32, name="warm")
-        nc.vector.memset(warm[:], 1.0)
-        warmed = keep.tile([P, 1], F32, name="warmed")
-        nc.scalar.activation(warmed[:], warm[:], ACT.Abs_reciprocal_sqrt)
+
+        warm_in = keep.tile([P, 1], F32, name="warm_in")
+        nc.vector.memset(warm_in[:], 1.0)
+        warm_out = keep.tile([P, 1], F32, name="warm_out")
+        nc.scalar.activation(warm_out[:], warm_in[:], ACT.Abs_reciprocal_sqrt)
+
         gl_row = keep.tile([1, T], F32, name="gl_row")
         nc.sync.dma_start(gl_row[:], gl[0:1, :])
         xs = keep.tile([P, PACK, D], F32, name="xs")
-        x_rows = x.rearrange("(p t) d -> p t d", t=PACK)
+        x_planes = x.rearrange("(p t) d -> p t d", t=PACK)
         for t in range(0, PACK, 2):
-            nc.sync.dma_start(xs[:, t : t + 2, :], x_rows[:, t : t + 2, :])
+            nc.sync.dma_start(xs[:, t : t + 2, :], x_planes[:, t : t + 2, :])
         nc.sync.dma_start(offsets[:], offs)
         cs4 = keep.tile([P, PACK], F32, name="cs4")
         nc.sync.dma_start(cs4[:], cs[0:1, :].rearrange("o (p j) -> p (o j)", j=PACK))
@@ -55,22 +68,19 @@ def tile_attend_gwnorm_vg_kernel(tc, vT, x, cs, gl, y, us, wt, offs, out_0, out_
         nc.sync.dma_start(us4[:], us.rearrange("(p t) o -> p (t o)", t=PACK))
         wt4 = keep.tile([P, PACK], F32, name="wt4")
         nc.sync.dma_start(wt4[:], wt.rearrange("(p t) o -> p (t o)", t=PACK))
-        v_planes = vT.rearrange("(p j) n -> p j n", j=PACK)
         gl_win = keep.tile([P, T], F32, name="gl_win")
         nc.vector.memset(gl_win[:].bitcast(U32), 0)
         nc.scalar.activation(gl_win[0:1, :], gl_row[:], ACT.Copy)
+        v_planes = vT.rearrange("(p j) n -> p j n", j=PACK)
         v_win = []
         for j in range(PACK):
-            w = keep.tile([P, T], F32, name=f"v_win{j}", align_bytes=64)
-            nc.sync.dma_start(w[:], v_planes[:, j, :])
-            v_win.append(w)
-        y_rows = y.rearrange("(p t) i -> p t i", t=PACK)
+            v_win.append(keep.tile([P, T], F32, name=f"v_win{j}", align_bytes=64))
+            nc.sync.dma_start(v_win[j][:], v_planes[:, j, :])
+        y_planes = y.rearrange("(p t) i -> p t i", t=PACK)
         ys = []
         for h in range(2):
-            yh = keep.tile([P, PACK, N // 2], F32, name=f"ys{h}")
-            nc.sync.dma_start(yh[:], y_rows[:, :, h * (N // 2) : (h + 1) * (N // 2)])
-            ys.append(yh)
-
+            ys.append(keep.tile([P, PACK, HALF], F32, name=f"ys{h}"))
+            nc.sync.dma_start(ys[h][:], y_planes[:, :, h * HALF : (h + 1) * HALF])
 
         ident = keep.tile([P, P], F32, name="ident")
         make_identity(nc, ident[:])
@@ -78,9 +88,8 @@ def tile_attend_gwnorm_vg_kernel(tc, vT, x, cs, gl, y, us, wt, offs, out_0, out_
         nc.gpsimd.memset(gg[:], 0.0)
         out_win = []
         for j in range(PACK):
-            w = keep.tile([P, T], F32, name=f"out_win{j}")
-            nc.vector.memset(w[:].bitcast(U32), 0)
-            out_win.append(w)
+            out_win.append(keep.tile([P, T], F32, name=f"out_win{j}"))
+            (nc.gpsimd if j == LAST else nc.vector).memset(out_win[j][:].bitcast(U32), 0)
 
         c2n = keep.tile([P, PACK], F32, name="c2n")
         nc.vector.scalar_tensor_tensor(c2n[:], wt4[:], -1.0, us4[:], ALU.mult, ALU.mult)
@@ -92,228 +101,177 @@ def tile_attend_gwnorm_vg_kernel(tc, vT, x, cs, gl, y, us, wt, offs, out_0, out_
         x_by_j = xs[:].rearrange("p t (m j) -> p t j m", j=PACK)
         xd = keep.tile([P, PACK, P, PACK], BF16, name="xd", align_bytes=64)
         for t in range(PACK):
-            bank = psum.tile([P, PACK, P], F32, name="x_bank", tag="ac"[t // 2])
+            x_bank = bank("x_bank", "a" if t < 2 else "c", [P, PACK, P])
             for j in range(PACK):
-                turn(bank[:, j, :], x_by_j[:, t, j, :])
-            nc.scalar.copy(xd[:, t, :, :], bank[:].rearrange("m j p -> m p j"))
+                turn(x_bank[:, j, :], x_by_j[:, t, j, :])
+            nc.scalar.copy(xd[:, t, :, :], x_bank[:].rearrange("m j p -> m p j"))
+        xr = keep.tile([P, PACK, P, PACK], BF16, name="xr", align_bytes=64)
+        xr_walk = xr[:].rearrange("p j m t -> p m t j")
+        xs_walk = xs[:].rearrange("p t (m j) -> p m t j", j=PACK)
+        nc.vector.tensor_copy(xr_walk[:, : P // 2], xs_walk[:, : P // 2])
+        nc.scalar.copy(xr_walk[:, P // 2 :], xs_walk[:, P // 2 :])
         xd_codes = keep.tile([P, R], U32, name="xd_codes", tag="v_win1", align_bytes=64)
         xd_scales = keep.tile([P, R], U8, name="xd_scales", align_bytes=64)
-        xr = keep.tile([P, PACK, P, PACK], BF16, name="xr", align_bytes=64)
         xr_codes = keep.tile([P, D], U32, name="xr_codes", tag="v_win2", align_bytes=64)
         xr_scales = keep.tile([P, D], U8, name="xr_scales", align_bytes=64)
 
-        vg = keep.tile([P, PACK, N], F32, name="vg")
-        vt = keep.tile([P, CHUNKS, PACK, P], F32, name="vt")
-        nn_bank = [psum.tile([P, 2, P], F32, name=f"nn_bank{h}", tag=f"n{h}", bufs=1) for h in range(2)]
-
-        def plane(j, pieces):
-            sq = ring.tile([P, N], F32, name="sq")
-            step = CHUNKS // pieces
-            for c0 in range(0, CHUNKS, step):
-                cols = slice(c0 * P, (c0 + step) * P)
-                nc.vector.tensor_copy(vg[:, j, cols], v_win[j][:].indirect(slots(c0, c0 + step)))
-                nc.scalar.activation(sq[:, cols], vg[:, j, cols], ACT.Square, scale=cs4[:, j : j + 1])
-                for c in range(c0, c0 + step):
-                    turn(nn_bank[c // 2][:, c % 2, :], sq[:, c * P : (c + 1) * P],
-                         start=(j == 0 and c % 2 == 0), stop=(j == PACK - 1 and c % 2 == 1))
-
-        def plane_turned(j):
-            if j < PACK - 1:
-                bank = psum.tile([P, CHUNKS, P], F32, name="v_bank", tag="b")
-            else:
-                bank = psum.tile([P, CHUNKS, P], F32, name="v_bank", tag="a")
-            for c in range(CHUNKS):
-                turn(bank[:, c, :], vg[:, j, c * P : (c + 1) * P])
-            nc.scalar.copy(vt[:, :, j, :], bank[:])
-
-        for m in range(0, P, P // 2):
-            (nc.scalar.copy if m else nc.vector.tensor_copy)(xr[:].rearrange("p j m t -> p m t j")[:, m : m + P // 2],
-                           xs[:].rearrange("p t (m j) -> p m t j", j=PACK)[:, m : m + P // 2])
         gl_g = keep.tile([P, N], F32, name="gl_g")
         nc.vector.tensor_copy(gl_g[:], gl_win[:].indirect(offsets[:]))
-        bank = psum.tile([P, CHUNKS, P], F32, name="gl_bank", tag="b")
+        gl_bank = bank("gl_bank", "b", [P, CHUNKS, P])
         for c in range(CHUNKS):
-            turn(bank[:, c, :], gl_g[:, c * P : (c + 1) * P])
+            turn(gl_bank[:, c, :], gl_g[:, cols(c, c + 1)])
         gl_col = keep.tile([P, CHUNKS], F32, name="gl_col")
-        nc.scalar.copy(gl_col[:], bank[:, :, 0])
-        plane(0, 1)
-        plane_turned(0)
-        nc.vector.quantize_mx(xd_codes[:].bitcast(E4M3), xd_scales[:], xd[:].rearrange("m t p j -> m (t p j)"))
-        plane(1, 1)
-        plane_turned(1)
-        plane(2, 1)
-        plane_turned(2)
-        nc.vector.quantize_mx(xr_codes[:].bitcast(E4M3), xr_scales[:], xr[:].rearrange("p j m t -> p (j m t)"))
-        plane(3, 2)
+        nc.scalar.copy(gl_col[:], gl_bank[:, :, 0])
 
-        vi = {}
-        v_codes = [keep.tile([P, N // 2], U32, name=f"v_codes{h}", tag=f"late{h}", align_bytes=64) for h in range(2)]
+        vg = keep.tile([P, PACK, N], F32, name="vg")
+        vt = keep.tile([P, CHUNKS, PACK, P], F32, name="vt")
+        nn_bank = [bank(f"nn_bank{h}", f"n{h}", [P, 2, P]) for h in range(2)]
+
+        def gather_plane(j, step):
+            sq = ring.tile([P, N], F32, name="sq")
+            for c0 in range(0, CHUNKS, step):
+                run = cols(c0, c0 + step)
+                nc.vector.tensor_copy(vg[:, j, run], v_win[j][:].indirect(slots(c0, c0 + step)))
+                nc.scalar.activation(sq[:, run], vg[:, j, run], ACT.Square, scale=cs4[:, j : j + 1])
+                for c in range(c0, c0 + step):
+                    turn(nn_bank[c // 2][:, c % 2, :], sq[:, cols(c, c + 1)],
+                         start=(j == 0 and c % 2 == 0), stop=(j == LAST and c % 2 == 1))
+
+        def turn_plane(j, group):
+            v_bank = bank("v_bank", group, [P, CHUNKS, P])
+            for c in range(CHUNKS):
+                turn(v_bank[:, c, :], vg[:, j, cols(c, c + 1)])
+            nc.scalar.copy(vt[:, :, j, :], v_bank[:])
+
+        gather_plane(0, CHUNKS)
+        turn_plane(0, "b")
+        nc.vector.quantize_mx(xd_codes[:].bitcast(E4M3), xd_scales[:], xd[:].rearrange("m t p j -> m (t p j)"))
+        gather_plane(1, CHUNKS)
+        turn_plane(1, "c")
+        gather_plane(2, CHUNKS)
+        turn_plane(2, "b")
+        nc.vector.quantize_mx(xr_codes[:].bitcast(E4M3), xr_scales[:], xr[:].rearrange("p j m t -> p (j m t)"))
+        gather_plane(LAST, 2)
+
+        v_codes = keep.tile([P, N], U32, name="v_codes", align_bytes=64)
         v_scales = keep.tile([P, N], U8, name="v_scales", align_bytes=64)
         nn = keep.tile([P, CHUNKS], F32, name="nn")
-        half = N // 2
-
-        def v_interleave(h):
-            cols = slice(h * half, (h + 1) * half)
-            vi[h] = keep.tile([P, half, PACK], BF16, name="vi", align_bytes=64)
-            nc.vector.tensor_copy(vi[h][:].rearrange("p (c i) j -> p c j i", i=4),
-                                  vg[:, :, cols].rearrange("p j (c i) -> p c j i", i=4))
-
-        def v_quantise(h):
-            cols = slice(h * half, (h + 1) * half)
-            nc.vector.quantize_mx(v_codes[h][:].bitcast(E4M3), v_scales[:, cols],
-                                  vi[h][:].rearrange("p i j -> p (i j)"))
-
-        length = keep.tile([P, CHUNKS], F32, name="length")
         rl = keep.tile([P, CHUNKS], F32, name="rl")
         s = keep.tile([P, CHUNKS], F32, name="s")
-        m2 = keep.tile([P, CHUNKS], F32, name="m2")
-        s_row, a_banks, gb, gi, b_banks, sb, kv = {}, {}, {}, {}, {}, {}, {}
+        srl = keep.tile([P, CHUNKS], F32, name="srl")
+        a_bank, sa_bank, b_bank, y2, gi, sb, kv = {}, {}, {}, {}, {}, {}, {}
 
-        us_ = {}
+        def lengths(c):
+            one = slice(c, c + 1)
+            terms = ring.tile([P, P], F32, name="terms")
+            nc.scalar.activation(terms[:], nn_bank[c // 2][:, c % 2, :], ACT.Copy, accum_out=nn[:, one])
+            nc.scalar.activation(rl[:, one], nn[:, one], ACT.Abs_reciprocal_sqrt)
+            nc.scalar.activation(s[:, one], rl[:, one], ACT.Copy, scale=gl_col[:, one])
 
-        def lengths(h):
-            two = slice(2 * h, 2 * h + 2)
-            for e in range(2):
-                terms = ring.tile([P, P], F32, name="terms")
-                nc.scalar.activation(terms[:], nn_bank[h][:, e, :], ACT.Copy, accum_out=nn[:, 2 * h + e : 2 * h + e + 1])
-            nc.scalar.activation(rl[:, two], nn[:, two], ACT.Abs_reciprocal_sqrt)
-            for c in range(2 * h, 2 * h + 2):
-                nc.scalar.activation(s[:, c : c + 1], rl[:, c : c + 1], ACT.Copy, scale=gl_col[:, c : c + 1])
+        def quantise_v(c):
+            run = cols(c, c + 1)
+            vi = ring.tile([P, P, PACK], BF16, name="vi", align_bytes=64)
+            interleave(nc.vector.tensor_copy, vi[:], vg[:, :, run])
+            nc.vector.quantize_mx(v_codes[:, run].bitcast(E4M3), v_scales[:, run], vi[:].rearrange("p i j -> p (i j)"))
 
-        def scores(c):
-            cols = slice(c * P, (c + 1) * P)
-            a_banks[c] = psum.tile([P, R], F32, name="a_bank", tag="b" if c == 2 else "a")
-            nc.tensor.matmul_mx(a_banks[c][:], v_codes[c // 2][:, (c % 2) * P : (c % 2 + 1) * P].bitcast(E4M3), v_scales[:, cols],
+        def first_product(c, group):
+            run = cols(c, c + 1)
+            a_bank[c] = bank("a_bank", group, [P, R])
+            nc.tensor.matmul_mx(a_bank[c][:], v_codes[:, run].bitcast(E4M3), v_scales[:, run],
                                 xd_codes[:].bitcast(E4M3), xd_scales[:], start=True, stop=True)
 
-        def scaled(c):
-            u = ring.tile([P, PACK, P], F32, name="u", bufs=CHUNKS)
-            nc.scalar.activation(u[:].rearrange("p t m -> p (t m)"), a_banks[c][:], ACT.Copy, scale=s[:, c : c + 1])
-            if c < 2:
-                us_[c] = psum.tile([P, PACK, P], F32, name="u_bank", tag=f"n{c}", bufs=1)
-            else:
-                us_[c] = psum.tile([P, PACK, P], F32, name="u_bank", tag="c")
+        def scale_and_turn(c, group):
+            sa = ring.tile([P, PACK, P], F32, name="sa", bufs=CHUNKS)
+            nc.scalar.activation(sa[:].rearrange("i t p -> i (t p)"), a_bank[c][:], ACT.Copy, scale=s[:, c : c + 1])
+            sa_bank[c] = bank("sa_bank", group, [P, PACK, P])
             for t in range(PACK):
-                turn(us_[c][:, t, :], u[:, t, :])
+                turn(sa_bank[c][:, t, :], sa[:, t, :])
 
         def targets(h):
-            gb[h] = keep.tile([P, PACK, half], F32, name=f"y2_{h}", align_bytes=64)
+            y2[h] = keep.tile([P, PACK, HALF], F32, name=f"y2_{h}", align_bytes=64)
             for t in range(PACK):
-                if h * PACK + t < Y_ON_VECTOR:
-                    nc.vector.tensor_scalar(gb[h][:, t, :], ys[h][:, t, :], c2n[:, t : t + 1], None, ALU.mult)
-                else:
-                    nc.scalar.activation(gb[h][:, t, :], ys[h][:, t, :], ACT.Copy, scale=c2n[:, t : t + 1])
+                nc.vector.tensor_scalar(y2[h][:, t, :], ys[h][:, t, :], c2n[:, t : t + 1], None, ALU.mult)
 
         def gradient(c):
-            flat = ring.tile([P, PACK, P], BF16, name="flat", bufs=CHUNKS)
+            g = ring.tile([P, PACK, P], BF16, name="g", bufs=CHUNKS)
             for t in range(PACK):
-                nc.vector.scalar_tensor_tensor(flat[:, t, :], us_[c][:, t, :], c1[:, t : t + 1],
-                                               gb[c // 2][:, t, (c % 2) * P : (c % 2 + 1) * P], ALU.mult, ALU.add)
+                nc.vector.scalar_tensor_tensor(g[:, t, :], sa_bank[c][:, t, :], c1[:, t : t + 1],
+                                               y2[c // 2][:, t, cols(c % 2, c % 2 + 1)], ALU.mult, ALU.add)
             gi[c] = keep.tile([P, P, PACK], BF16, name=f"gi{c}", align_bytes=64)
-            nc.scalar.copy(gi[c][:].rearrange("p (c i) t -> p c t i", i=4), flat[:].rearrange("p t (c i) -> p c t i", i=4))
+            interleave(nc.scalar.copy, gi[c][:], g[:])
 
-        def back(c):
+        def second_product(c, group):
             g_codes = keep.tile([P, P], U32, name=f"g_codes{c}", align_bytes=64)
             g_scales = keep.tile([P, P], U8, name=f"g_scales{c}", align_bytes=64)
             nc.vector.quantize_mx(g_codes[:].bitcast(E5M2), g_scales[:], gi[c][:].rearrange("p i t -> p (i t)"))
-            b_banks[c] = psum.tile([P, D], F32, name="b_bank", tag="ba"[c // 2])
-            nc.tensor.matmul_mx(b_banks[c][:], g_codes[:].bitcast(E5M2), g_scales[:],
+            b_bank[c] = bank("b_bank", group, [P, D])
+            nc.tensor.matmul_mx(b_bank[c][:], g_codes[:].bitcast(E5M2), g_scales[:],
                                 xr_codes[:].bitcast(E4M3), xr_scales[:], start=True, stop=True)
 
-        lengths(0)
-        v_interleave(0)
-        lengths(1)
-        v_quantise(0)
-        scores(0)
-        scores(1)
-        v_interleave(1)
-        v_quantise(1)
-        scores(2)
-        nc.vector.scalar_tensor_tensor(m2[:], s[:], -1.0, rl[:], ALU.mult, ALU.mult)
-        targets(0)
-        targets(1)
-
-        def along(c):
-            vt_c = vt[:, c, :, :].rearrange("p j m -> p (j m)")
-            prod = ring.tile([P, D], F32, name="prod")
-            nc.vector.scalar_tensor_tensor(prod[:], b_banks[c][:], rl[:, c : c + 1], vt_c, ALU.mult, ALU.mult,
-                                           accum_out=gg[:, c : c + 1])
+        def two_terms(c):
+            one = slice(c, c + 1)
+            vt_c = vt[:, c, :, :].rearrange("i j p -> i (j p)")
+            products = ring.tile([P, D], F32, name="products")
+            nc.vector.scalar_tensor_tensor(products[:], b_bank[c][:], rl[:, one], vt_c, ALU.mult, ALU.mult,
+                                           accum_out=gg[:, one])
             sb[c] = keep.tile([P, D], F32, name=f"sb{c}")
-            nc.scalar.activation(sb[c][:], b_banks[c][:], ACT.Copy, scale=s[:, c : c + 1])
+            nc.scalar.activation(sb[c][:], b_bank[c][:], ACT.Copy, scale=s[:, one])
             kv[c] = keep.tile([P, D], F32, name=f"kv{c}")
-            if c in KV_ON_VECTOR:
-                nc.vector.tensor_scalar(kv[c][:], vt_c, gg[:, c : c + 1], m2[:, c : c + 1], ALU.mult, ALU.mult)
-            else:
-                k = keep.tile([P, 1], F32, name=f"k{c}")
-                nc.scalar.activation(k[:], gg[:, c : c + 1], ACT.Copy, scale=m2[:, c : c + 1])
-                nc.scalar.activation(kv[c][:], vt_c, ACT.Copy, scale=k[:])
+            nc.vector.tensor_scalar(kv[c][:], vt_c, gg[:, one], srl[:, one], ALU.mult, ALU.mult)
 
-        def first_chunk():
-            sb_bank = psum.tile([P, PACK, P], F32, name="sb_bank", tag="n0", bufs=1)
-            kv_bank = psum.tile([P, PACK, P], F32, name="kv_bank", tag="n1", bufs=1)
-            for j in range(PACK):
-                turn(sb_bank[:, j, :], sb[0][:, j * P : (j + 1) * P])
-            for j in range(PACK):
-                turn(kv_bank[:, j, :], kv[0][:, j * P : (j + 1) * P])
-            sb_t = keep.tile([P, PACK, P], F32, name="sb_first")
-            kv_t = keep.tile([P, PACK, P], F32, name="kv_first")
-            nc.scalar.copy(sb_t[:], sb_bank[:])
-            for j in range(PACK):
-                nc.scalar.activation(kv_t[:, j, :], kv_bank[:, j, :], ACT.Copy, scale=cs2[:, j : j + 1])
-            firsts.extend([sb_t, kv_t])
+        for c in range(CHUNKS):
+            lengths(c)
+            quantise_v(c)
+            if c < CHUNKS - 1:
+                first_product(c, "a" if c < 2 else "b")
+        nc.vector.scalar_tensor_tensor(srl[:], s[:], -1.0, rl[:], ALU.mult, ALU.mult)
+        for h in range(2):
+            targets(h)
+        for c in range(CHUNKS):
+            scale_and_turn(c, f"n{c}" if c < 2 else "c")
+            if c == 0:
+                first_product(CHUNKS - 1, "a")
+        for c in range(CHUNKS):
+            gradient(c)
+            if c == 0:
+                turn_plane(LAST, "a")
+            second_product(c, "b" if c < 2 else "a")
 
-        def place_first():
-            for j in range(PACK):
-                nc.vector.tensor_tensor(out_win[j][:].indirect(slots(0, 1)), firsts[0][:, j, :], firsts[1][:, j, :], ALU.add)
+        two_terms(0)
+        sb_bank = bank("sb_bank", "n0", [P, PACK, P])
+        kv_bank = bank("kv_bank", "n1", [P, PACK, P])
+        for j in range(PACK):
+            turn(sb_bank[:, j, :], sb[0][:, cols(j, j + 1)])
+        for j in range(PACK):
+            turn(kv_bank[:, j, :], kv[0][:, cols(j, j + 1)])
+        sb_first = keep.tile([P, PACK, P], F32, name="sb_first")
+        kv_first = keep.tile([P, PACK, P], F32, name="kv_first")
+        nc.scalar.copy(sb_first[:], sb_bank[:])
+        for j in range(PACK):
+            nc.scalar.activation(kv_first[:, j, :], kv_bank[:, j, :], ACT.Copy, scale=cs2[:, j : j + 1])
+        for c in range(1, CHUNKS):
+            two_terms(c)
+        for j in range(PACK):
+            nc.vector.tensor_tensor(out_win[j][:].indirect(slots(0, 1)), sb_first[:, j, :], kv_first[:, j, :], ALU.add)
 
         out_planes = out_0.rearrange("(p j) n -> p j n", j=PACK)
-        firsts, done = [], []
-
-        def finish(j, c0, c1):
-            sb_bank = psum.tile([P, c1 - c0, P], F32, name="sb_bank", tag="c")
-            kv_bank = psum.tile([P, c1 - c0, P], F32, name="kv_bank", tag=f"n{len(done) % 2}", bufs=1)
-            done.append(j)
-            for c in range(c0, c1):
-                turn(sb_bank[:, c - c0, :], sb[c][:, j * P : (j + 1) * P])
-            for c in range(c0, c1):
-                turn(kv_bank[:, c - c0, :], kv[c][:, j * P : (j + 1) * P])
-            sb_t = keep.tile([P, (c1 - c0) * P], F32, name=f"sb_t{j}_{c0}")
-            kv_t = keep.tile([P, (c1 - c0) * P], F32, name=f"kv_t{j}_{c0}")
-            nc.scalar.copy(sb_t[:], sb_bank[:].rearrange("p c i -> p (c i)"))
-            nc.scalar.activation(kv_t[:], kv_bank[:].rearrange("p c i -> p (c i)"), ACT.Copy, scale=cs2[:, j : j + 1])
-            nc.vector.tensor_tensor(out_win[j][:].indirect(slots(c0, c1)), sb_t[:], kv_t[:], ALU.add)
-            if c1 == CHUNKS:
-                nc.sync.dma_start(out_planes[:, j, :], out_win[j][:])
-
-        def lengths_gradient():
-            gg_bank = psum.tile([P, P], F32, name="gg_bank", tag="b")
-            turn(gg_bank[:], gg[:])
-            gg_rows = keep.tile([32, P], F32, name="gg_rows")
-            nc.scalar.copy(gg_rows[:], gg_bank[0:32, :])
-            nc.sync.dma_start(out_1.rearrange("o (c i) -> (o c) i", c=CHUNKS), gg_rows[0:CHUNKS, :])
-
-        scaled(0)
-        scores(3)
-        scaled(1)
-        scaled(2)
-        scaled(3)
-        gradient(0)
-        plane_turned(3)
-        back(0)
-        gradient(1)
-        back(1)
-        gradient(2)
-        back(2)
-        gradient(3)
-        back(3)
-        along(0)
-        first_chunk()
-        along(1)
-        along(2)
-        along(3)
-        place_first()
-        finish(0, 1, 4)
-        finish(1, 1, 4)
-        lengths_gradient()
-        finish(2, 1, 4)
-        finish(3, 1, 4)
+        rest = CHUNKS - 1
+        for j in range(PACK):
+            sb_bank = bank("sb_bank", "c", [P, rest, P])
+            kv_bank = bank("kv_bank", f"n{j % 2}", [P, rest, P])
+            for c in range(1, CHUNKS):
+                turn(sb_bank[:, c - 1, :], sb[c][:, cols(j, j + 1)])
+            for c in range(1, CHUNKS):
+                turn(kv_bank[:, c - 1, :], kv[c][:, cols(j, j + 1)])
+            sb_rest = keep.tile([P, rest * P], F32, name=f"sb_rest{j}")
+            kv_rest = keep.tile([P, rest * P], F32, name=f"kv_rest{j}")
+            nc.scalar.copy(sb_rest[:], sb_bank[:].rearrange("p c i -> p (c i)"))
+            nc.scalar.activation(kv_rest[:], kv_bank[:].rearrange("p c i -> p (c i)"), ACT.Copy, scale=cs2[:, j : j + 1])
+            nc.vector.tensor_tensor(out_win[j][:].indirect(slots(1, CHUNKS)), sb_rest[:], kv_rest[:], ALU.add)
+            nc.sync.dma_start(out_planes[:, j, :], out_win[j][:])
+            if j == 1:
+                gg_bank = bank("gg_bank", "b", [P, P])
+                turn(gg_bank[:], gg[:])
+                gg_rows = keep.tile([QUADRANT, P], F32, name="gg_rows")
+                nc.scalar.copy(gg_rows[:], gg_bank[0:QUADRANT, :])
+                nc.sync.dma_start(out_1.rearrange("o (c i) -> (o c) i", c=CHUNKS), gg_rows[0:CHUNKS, :])

@@ -24,6 +24,7 @@ LIST_COLS = P // 16
 LINE = 4
 QUADRANT = 32
 LAST = PACK - 1
+GL_RUN = T // P
 
 
 def tile_attend_gwnorm_vg_kernel(tc, vT, x, cs, gl, y, us, wt, offs, out_0, out_1):
@@ -31,10 +32,10 @@ def tile_attend_gwnorm_vg_kernel(tc, vT, x, cs, gl, y, us, wt, offs, out_0, out_
     with ExitStack() as ctx:
         keep = ctx.enter_context(tc.tile_pool(name="keep", bufs=1))
         ring = ctx.enter_context(tc.tile_pool(name="ring", bufs=2))
-        psum = ctx.enter_context(tc.psum_pool(name="psum", bufs=2))
+        psum = ctx.enter_context(tc.psum_pool(name="psum", bufs=1))
 
-        def bank(name, group, shape):
-            return psum.tile(shape, F32, name=name, tag=group, bufs=2 if group in ("a", "b", "c") else 1)
+        def bank(name, number, shape):
+            return psum.tile(shape, F32, name=name, tag=f"bank{number}")
 
         def turn(dst, src, start=True, stop=True):
             nc.tensor.matmul(dst, src, ident[:], start=start, stop=stop, is_transpose=True)
@@ -48,6 +49,9 @@ def tile_attend_gwnorm_vg_kernel(tc, vT, x, cs, gl, y, us, wt, offs, out_0, out_
         def interleave(copy, dst, src):
             copy(dst.rearrange("p (c i) j -> p c j i", i=LINE), src.rearrange("p j (c i) -> p c j i", i=LINE))
 
+        def scalar_copy(dst, src):
+            nc.scalar.activation(dst, src, ACT.Copy)
+
         offsets = keep.tile([P, N // 16], U16, name="offsets")
 
         warm_in = keep.tile([P, 1], F32, name="warm_in")
@@ -57,20 +61,20 @@ def tile_attend_gwnorm_vg_kernel(tc, vT, x, cs, gl, y, us, wt, offs, out_0, out_
 
         gl_row = keep.tile([1, T], F32, name="gl_row")
         nc.sync.dma_start(gl_row[:], gl[0:1, :])
+        gl_win = keep.tile([P, T], F32, name="gl_win")
+        nc.vector.memset(gl_win[:].bitcast(U32), 0)
+        scalar_copy(gl_win[0:1, :], gl_row[:])
+        cs4 = keep.tile([P, PACK], F32, name="cs4")
+        nc.sync.dma_start(cs4[:], cs[0:1, :].rearrange("o (p j) -> p (o j)", j=PACK))
         xs = keep.tile([P, PACK, D], F32, name="xs")
         x_planes = x.rearrange("(p t) d -> p t d", t=PACK)
         for t in range(0, PACK, 2):
             nc.sync.dma_start(xs[:, t : t + 2, :], x_planes[:, t : t + 2, :])
         nc.sync.dma_start(offsets[:], offs)
-        cs4 = keep.tile([P, PACK], F32, name="cs4")
-        nc.sync.dma_start(cs4[:], cs[0:1, :].rearrange("o (p j) -> p (o j)", j=PACK))
         us4 = keep.tile([P, PACK], F32, name="us4")
         nc.sync.dma_start(us4[:], us.rearrange("(p t) o -> p (t o)", t=PACK))
         wt4 = keep.tile([P, PACK], F32, name="wt4")
         nc.sync.dma_start(wt4[:], wt.rearrange("(p t) o -> p (t o)", t=PACK))
-        gl_win = keep.tile([P, T], F32, name="gl_win")
-        nc.vector.memset(gl_win[:].bitcast(U32), 0)
-        nc.scalar.activation(gl_win[0:1, :], gl_row[:], ACT.Copy)
         v_planes = vT.rearrange("(p j) n -> p j n", j=PACK)
         v_win = []
         for j in range(PACK):
@@ -86,38 +90,42 @@ def tile_attend_gwnorm_vg_kernel(tc, vT, x, cs, gl, y, us, wt, offs, out_0, out_
         make_identity(nc, ident[:])
         gg = keep.tile([P, P], F32, name="gg")
         nc.gpsimd.memset(gg[:], 0.0)
-        out_win = []
+
+        cs2 = keep.tile([P, PACK], F32, name="cs2")
+        nc.vector.tensor_tensor(cs2[:], cs4[:], cs4[:], ALU.mult)
+        cs2_bank = bank("cs2_bank", 2, [P, PACK, P])
         for j in range(PACK):
-            out_win.append(keep.tile([P, T], F32, name=f"out_win{j}"))
-            (nc.gpsimd if j == LAST else nc.vector).memset(out_win[j][:].bitcast(U32), 0)
+            turn(cs2_bank[:, j, :], cs2[:, j : j + 1].to_broadcast([P, P]))
+        cs2_row = keep.tile([P, PACK, P], F32, name="cs2_row")
+        nc.scalar.copy(cs2_row[:], cs2_bank[:])
+
+        xd = keep.tile([P, PACK, P, PACK], BF16, name="xd", align_bytes=64)
+        xd_words = xd[:].rearrange("m t p j -> m (t p j)").bitcast(F32).rearrange("m (t p u) -> m t p u", t=PACK, u=2)
+        for h in range(2):
+            xb = ring.tile([P, 2, 2, P, 2], BF16, name="xb")
+            nc.vector.tensor_copy(xb[:], xs[:, 2 * h : 2 * h + 2, :].rearrange("p t (m u e) -> p t u m e", u=2, e=2))
+            xb_words = xb[:].rearrange("p t u m e -> p (t u m e)").bitcast(F32)
+            x_bank = bank("x_bank", h, [P, 2, 2, P])
+            for t in range(2):
+                for u in range(2):
+                    turn(x_bank[:, t, u, :], xb_words[:, cols(2 * t + u, 2 * t + u + 1)])
+            nc.scalar.copy(xd_words[:, 2 * h : 2 * h + 2, :, :], x_bank[:].rearrange("m t u p -> m t p u"))
+        xr = keep.tile([P, PACK, P, PACK], BF16, name="xr", align_bytes=64)
+        nc.vector.tensor_copy(xr[:].rearrange("p j m t -> p m t j"), xs[:].rearrange("p t (m j) -> p m t j", j=PACK))
+        xd_codes = keep.tile([P, R], U32, name="xd_codes", align_bytes=64)
+        xd_scales = keep.tile([P, R], U8, name="xd_scales", align_bytes=64)
+        xr_codes = keep.tile([P, D], U32, name="xr_codes", align_bytes=64)
+        xr_scales = keep.tile([P, D], U8, name="xr_scales", align_bytes=64)
+        nc.vector.quantize_mx(xr_codes[:].bitcast(E4M3), xr_scales[:], xr[:].rearrange("p j m t -> p (j m t)"))
+        nc.vector.quantize_mx(xd_codes[:].bitcast(E4M3), xd_scales[:], xd[:].rearrange("m t p j -> m (t p j)"))
 
         c2n = keep.tile([P, PACK], F32, name="c2n")
         nc.vector.scalar_tensor_tensor(c2n[:], wt4[:], -1.0, us4[:], ALU.mult, ALU.mult)
         c1 = keep.tile([P, PACK], F32, name="c1")
         nc.vector.scalar_tensor_tensor(c1[:], c2n[:], -1.0, us4[:], ALU.mult, ALU.mult)
-        cs2 = keep.tile([P, PACK], F32, name="cs2")
-        nc.vector.tensor_tensor(cs2[:], cs4[:], cs4[:], ALU.mult)
-
-        x_by_j = xs[:].rearrange("p t (m j) -> p t j m", j=PACK)
-        xd = keep.tile([P, PACK, P, PACK], BF16, name="xd", align_bytes=64)
-        for t in range(PACK):
-            x_bank = bank("x_bank", "a" if t < 2 else "c", [P, PACK, P])
-            for j in range(PACK):
-                turn(x_bank[:, j, :], x_by_j[:, t, j, :])
-            nc.scalar.copy(xd[:, t, :, :], x_bank[:].rearrange("m j p -> m p j"))
-        xr = keep.tile([P, PACK, P, PACK], BF16, name="xr", align_bytes=64)
-        xr_walk = xr[:].rearrange("p j m t -> p m t j")
-        xs_walk = xs[:].rearrange("p t (m j) -> p m t j", j=PACK)
-        nc.vector.tensor_copy(xr_walk[:, : P // 2], xs_walk[:, : P // 2])
-        nc.scalar.copy(xr_walk[:, P // 2 :], xs_walk[:, P // 2 :])
-        xd_codes = keep.tile([P, R], U32, name="xd_codes", tag="v_win1", align_bytes=64)
-        xd_scales = keep.tile([P, R], U8, name="xd_scales", align_bytes=64)
-        xr_codes = keep.tile([P, D], U32, name="xr_codes", tag="v_win2", align_bytes=64)
-        xr_scales = keep.tile([P, D], U8, name="xr_scales", align_bytes=64)
-
         gl_g = keep.tile([P, N], F32, name="gl_g")
-        nc.vector.tensor_copy(gl_g[:], gl_win[:].indirect(offsets[:]))
-        gl_bank = bank("gl_bank", "b", [P, CHUNKS, P])
+        scalar_copy(gl_g[:], gl_win[:].indirect(offsets[:]))
+        gl_bank = bank("gl_bank", 3, [P, CHUNKS, P])
         for c in range(CHUNKS):
             turn(gl_bank[:, c, :], gl_g[:, cols(c, c + 1)])
         gl_col = keep.tile([P, CHUNKS], F32, name="gl_col")
@@ -125,33 +133,44 @@ def tile_attend_gwnorm_vg_kernel(tc, vT, x, cs, gl, y, us, wt, offs, out_0, out_
 
         vg = keep.tile([P, PACK, N], F32, name="vg")
         vt = keep.tile([P, CHUNKS, PACK, P], F32, name="vt")
-        nn_bank = [bank(f"nn_bank{h}", f"n{h}", [P, 2, P]) for h in range(2)]
+        vc = {}
+        nn_bank = [bank(f"nn_bank{c}", 4 + c, [P, P]) for c in range(CHUNKS)]
 
-        def gather_plane(j, step):
-            sq = ring.tile([P, N], F32, name="sq")
-            for c0 in range(0, CHUNKS, step):
-                run = cols(c0, c0 + step)
-                nc.vector.tensor_copy(vg[:, j, run], v_win[j][:].indirect(slots(c0, c0 + step)))
-                nc.scalar.activation(sq[:, run], vg[:, j, run], ACT.Square, scale=cs4[:, j : j + 1])
-                for c in range(c0, c0 + step):
-                    turn(nn_bank[c // 2][:, c % 2, :], sq[:, cols(c, c + 1)],
-                         start=(j == 0 and c % 2 == 0), stop=(j == LAST and c % 2 == 1))
+        def square(j, c0, c1):
+            sq = ring.tile([P, N], F32, name="sq", bufs=CHUNKS)
+            run = cols(c0, c1)
+            nc.scalar.activation(sq[:, run], vg[:, j, run], ACT.Square, scale=cs4[:, j : j + 1])
+            for c in range(c0, c1):
+                turn(nn_bank[c][:], sq[:, cols(c, c + 1)], start=(j == 0), stop=(j == LAST))
 
-        def turn_plane(j, group):
-            v_bank = bank("v_bank", group, [P, CHUNKS, P])
+        def turn_plane(j, number):
+            v_bank = bank("v_bank", number, [P, CHUNKS, P])
             for c in range(CHUNKS):
                 turn(v_bank[:, c, :], vg[:, j, cols(c, c + 1)])
-            nc.scalar.copy(vt[:, :, j, :], v_bank[:])
+            (nc.scalar.copy if j < LAST else nc.vector.tensor_copy)(vt[:, :, j, :], v_bank[:])
 
-        gather_plane(0, CHUNKS)
-        turn_plane(0, "b")
-        nc.vector.quantize_mx(xd_codes[:].bitcast(E4M3), xd_scales[:], xd[:].rearrange("m t p j -> m (t p j)"))
-        gather_plane(1, CHUNKS)
-        turn_plane(1, "c")
-        gather_plane(2, CHUNKS)
-        turn_plane(2, "b")
-        nc.vector.quantize_mx(xr_codes[:].bitcast(E4M3), xr_scales[:], xr[:].rearrange("p j m t -> p (j m t)"))
-        gather_plane(LAST, 2)
+        def weigh(j0, j1, window):
+            part = keep.tile([P, CHUNKS, j1 - j0, P], F32, name=f"vc{j0}", tag=f"v_win{window}", align_bytes=64)
+            nc.vector.tensor_tensor(part[:], vt[:, :, j0:j1, :],
+                                    cs2_row[:, j0:j1, :].unsqueeze(1).to_broadcast([P, CHUNKS, j1 - j0, P]), ALU.mult)
+            vc[j0, j1] = part
+
+        def gather(j, c0, c1):
+            nc.vector.tensor_copy(vg[:, j, cols(c0, c1)], v_win[j][:].indirect(slots(c0, c1)))
+
+        for j in range(LAST):
+            for h in range(2):
+                gather(j, 2 * h, 2 * h + 2)
+            if j > 0:
+                weigh(j - 1, j, j)
+            turn_plane(j, 2 + j % 2)
+            square(j, 0, CHUNKS)
+        out_win = []
+        for j in range(PACK):
+            out_win.append(keep.tile([P, T], F32, name=f"out_win{j}"))
+            (nc.gpsimd if j == LAST else nc.vector).memset(out_win[j][:].bitcast(U32), 0)
+        for h in range(2):
+            gather(LAST, 2 * h, 2 * h + 2)
 
         v_codes = keep.tile([P, N], U32, name="v_codes", align_bytes=64)
         v_scales = keep.tile([P, N], U8, name="v_scales", align_bytes=64)
@@ -164,26 +183,30 @@ def tile_attend_gwnorm_vg_kernel(tc, vT, x, cs, gl, y, us, wt, offs, out_0, out_
         def lengths(c):
             one = slice(c, c + 1)
             terms = ring.tile([P, P], F32, name="terms")
-            nc.scalar.activation(terms[:], nn_bank[c // 2][:, c % 2, :], ACT.Copy, accum_out=nn[:, one])
+            nc.scalar.activation(terms[:], nn_bank[c][:], ACT.Copy, accum_out=nn[:, one])
             nc.scalar.activation(rl[:, one], nn[:, one], ACT.Abs_reciprocal_sqrt)
             nc.scalar.activation(s[:, one], rl[:, one], ACT.Copy, scale=gl_col[:, one])
 
+        vi = {}
+
+        def weave_v(c):
+            vi[c] = keep.tile([P, P, PACK], BF16, name=f"vi{c}", align_bytes=64)
+            interleave(nc.vector.tensor_copy, vi[c][:], vg[:, :, cols(c, c + 1)])
+
         def quantise_v(c):
             run = cols(c, c + 1)
-            vi = ring.tile([P, P, PACK], BF16, name="vi", align_bytes=64)
-            interleave(nc.vector.tensor_copy, vi[:], vg[:, :, run])
-            nc.vector.quantize_mx(v_codes[:, run].bitcast(E4M3), v_scales[:, run], vi[:].rearrange("p i j -> p (i j)"))
+            nc.vector.quantize_mx(v_codes[:, run].bitcast(E4M3), v_scales[:, run], vi[c][:].rearrange("p i j -> p (i j)"))
 
-        def first_product(c, group):
+        def first_product(c):
             run = cols(c, c + 1)
-            a_bank[c] = bank("a_bank", group, [P, R])
+            a_bank[c] = bank("a_bank", (0, 1, 3, 4)[c], [P, R])
             nc.tensor.matmul_mx(a_bank[c][:], v_codes[:, run].bitcast(E4M3), v_scales[:, run],
                                 xd_codes[:].bitcast(E4M3), xd_scales[:], start=True, stop=True)
 
-        def scale_and_turn(c, group):
+        def scale_and_turn(c):
             sa = ring.tile([P, PACK, P], F32, name="sa", bufs=CHUNKS)
             nc.scalar.activation(sa[:].rearrange("i t p -> i (t p)"), a_bank[c][:], ACT.Copy, scale=s[:, c : c + 1])
-            sa_bank[c] = bank("sa_bank", group, [P, PACK, P])
+            sa_bank[c] = bank("sa_bank", (5, 6, 7, 2)[c], [P, PACK, P])
             for t in range(PACK):
                 turn(sa_bank[c][:, t, :], sa[:, t, :])
 
@@ -200,78 +223,88 @@ def tile_attend_gwnorm_vg_kernel(tc, vT, x, cs, gl, y, us, wt, offs, out_0, out_
             gi[c] = keep.tile([P, P, PACK], BF16, name=f"gi{c}", align_bytes=64)
             interleave(nc.scalar.copy, gi[c][:], g[:])
 
-        def second_product(c, group):
+        def second_product(c):
             g_codes = keep.tile([P, P], U32, name=f"g_codes{c}", align_bytes=64)
             g_scales = keep.tile([P, P], U8, name=f"g_scales{c}", align_bytes=64)
             nc.vector.quantize_mx(g_codes[:].bitcast(E5M2), g_scales[:], gi[c][:].rearrange("p i t -> p (i t)"))
-            b_bank[c] = bank("b_bank", group, [P, D])
-            nc.tensor.matmul_mx(b_bank[c][:], g_codes[:].bitcast(E5M2), g_scales[:],
+            b_bank[c] = bank("b_bank", (0, 1, 3, 4)[c], [P, PACK, P])
+            nc.tensor.matmul_mx(b_bank[c][:].rearrange("i j p -> i (j p)"), g_codes[:].bitcast(E5M2), g_scales[:],
                                 xr_codes[:].bitcast(E4M3), xr_scales[:], start=True, stop=True)
+
+        def projection(c):
+            products = ring.tile([P, PACK, P], F32, name="products")
+            nc.vector.scalar_tensor_tensor(products[:], b_bank[c][:], rl[:, c : c + 1], vt[:, c, :, :], ALU.mult, ALU.mult,
+                                           accum_out=gg[:, c : c + 1])
 
         def two_terms(c):
             one = slice(c, c + 1)
-            vt_c = vt[:, c, :, :].rearrange("i j p -> i (j p)")
-            products = ring.tile([P, D], F32, name="products")
-            nc.vector.scalar_tensor_tensor(products[:], b_bank[c][:], rl[:, one], vt_c, ALU.mult, ALU.mult,
-                                           accum_out=gg[:, one])
-            sb[c] = keep.tile([P, D], F32, name=f"sb{c}")
+            sb[c] = keep.tile([P, PACK, P], F32, name=f"sb{c}")
             nc.scalar.activation(sb[c][:], b_bank[c][:], ACT.Copy, scale=s[:, one])
-            kv[c] = keep.tile([P, D], F32, name=f"kv{c}")
-            nc.vector.tensor_scalar(kv[c][:], vt_c, gg[:, one], srl[:, one], ALU.mult, ALU.mult)
+            kv[c] = keep.tile([P, PACK, P], F32, name=f"kv{c}")
+            for (j0, j1), part in vc.items():
+                nc.vector.tensor_scalar(kv[c][:, j0:j1, :], part[:, c, :, :], gg[:, one], srl[:, one], ALU.mult, ALU.mult)
 
-        for c in range(CHUNKS):
-            lengths(c)
-            quantise_v(c)
-            if c < CHUNKS - 1:
-                first_product(c, "a" if c < 2 else "b")
-        nc.vector.scalar_tensor_tensor(srl[:], s[:], -1.0, rl[:], ALU.mult, ALU.mult)
-        for h in range(2):
-            targets(h)
-        for c in range(CHUNKS):
-            scale_and_turn(c, f"n{c}" if c < 2 else "c")
-            if c == 0:
-                first_product(CHUNKS - 1, "a")
-        for c in range(CHUNKS):
-            gradient(c)
-            if c == 0:
-                turn_plane(LAST, "a")
-            second_product(c, "b" if c < 2 else "a")
-
-        two_terms(0)
-        sb_bank = bank("sb_bank", "n0", [P, PACK, P])
-        kv_bank = bank("kv_bank", "n1", [P, PACK, P])
-        for j in range(PACK):
-            turn(sb_bank[:, j, :], sb[0][:, cols(j, j + 1)])
-        for j in range(PACK):
-            turn(kv_bank[:, j, :], kv[0][:, cols(j, j + 1)])
-        sb_first = keep.tile([P, PACK, P], F32, name="sb_first")
-        kv_first = keep.tile([P, PACK, P], F32, name="kv_first")
-        nc.scalar.copy(sb_first[:], sb_bank[:])
-        for j in range(PACK):
-            nc.scalar.activation(kv_first[:, j, :], kv_bank[:, j, :], ACT.Copy, scale=cs2[:, j : j + 1])
-        for c in range(1, CHUNKS):
-            two_terms(c)
-        for j in range(PACK):
-            nc.vector.tensor_tensor(out_win[j][:].indirect(slots(0, 1)), sb_first[:, j, :], kv_first[:, j, :], ALU.add)
+        def turn_back(j, c0, c1, number, copy):
+            dv_bank = bank("dv_bank", number, [P, c1 - c0, P])
+            for c in range(c0, c1):
+                turn(dv_bank[:, c - c0, :], sb[c][:, j, :], start=(c == c0), stop=False)
+            for c in range(c0, c1):
+                turn(dv_bank[:, c - c0, :], kv[c][:, j, :], start=False, stop=(c == c1 - 1))
+            dv = keep.tile([P, (c1 - c0) * P], F32, name=f"dv{j}_{c0}")
+            copy(dv[:], dv_bank[:].rearrange("p c i -> p (c i)"))
+            return dv
 
         out_planes = out_0.rearrange("(p j) n -> p j n", j=PACK)
-        rest = CHUNKS - 1
-        for j in range(PACK):
-            sb_bank = bank("sb_bank", "c", [P, rest, P])
-            kv_bank = bank("kv_bank", f"n{j % 2}", [P, rest, P])
-            for c in range(1, CHUNKS):
-                turn(sb_bank[:, c - 1, :], sb[c][:, cols(j, j + 1)])
-            for c in range(1, CHUNKS):
-                turn(kv_bank[:, c - 1, :], kv[c][:, cols(j, j + 1)])
-            sb_rest = keep.tile([P, rest * P], F32, name=f"sb_rest{j}")
-            kv_rest = keep.tile([P, rest * P], F32, name=f"kv_rest{j}")
-            nc.scalar.copy(sb_rest[:], sb_bank[:].rearrange("p c i -> p (c i)"))
-            nc.scalar.activation(kv_rest[:], kv_bank[:].rearrange("p c i -> p (c i)"), ACT.Copy, scale=cs2[:, j : j + 1])
-            nc.vector.tensor_tensor(out_win[j][:].indirect(slots(1, CHUNKS)), sb_rest[:], kv_rest[:], ALU.add)
+
+        def store(j):
             nc.sync.dma_start(out_planes[:, j, :], out_win[j][:])
-            if j == 1:
-                gg_bank = bank("gg_bank", "b", [P, P])
-                turn(gg_bank[:], gg[:])
-                gg_rows = keep.tile([QUADRANT, P], F32, name="gg_rows")
-                nc.scalar.copy(gg_rows[:], gg_bank[0:QUADRANT, :])
-                nc.sync.dma_start(out_1.rearrange("o (c i) -> (o c) i", c=CHUNKS), gg_rows[0:CHUNKS, :])
+
+        for c in range(2):
+            square(LAST, c, c + 1)
+        square(LAST, 2, 4)
+        for c in range(CHUNKS):
+            weave_v(c)
+            quantise_v(c)
+            first_product(c)
+            lengths(c)
+            scale_and_turn(c)
+            if c == 0:
+                turn_plane(LAST, 2)
+        targets(0)
+        gradient(0)
+        second_product(0)
+        gradient(1)
+        second_product(1)
+        targets(1)
+        nc.vector.scalar_tensor_tensor(srl[:], s[:], -1.0, rl[:], ALU.mult, ALU.mult)
+        gradient(2)
+        second_product(2)
+        gradient(3)
+        second_product(3)
+        weigh(2, 4, LAST)
+        for c in range(2):
+            projection(c)
+            two_terms(c)
+        dv = turn_back(0, 0, 2, 5, nc.scalar.copy)
+        scalar_copy(out_win[0][:].indirect(slots(0, 2)), dv[:])
+        for c in range(2, CHUNKS):
+            projection(c)
+            two_terms(c)
+        dv = turn_back(0, 2, 4, 6, nc.scalar.copy)
+        scalar_copy(out_win[0][:].indirect(slots(2, 4)), dv[:])
+        store(0)
+        dv1 = turn_back(1, 0, 4, 7, nc.vector.tensor_copy)
+        nc.vector.tensor_copy(out_win[1][:].indirect(offsets[:]), dv1[:])
+        store(1)
+        dv2 = turn_back(2, 0, 4, 2, nc.scalar.copy)
+        for h in range(2):
+            scalar_copy(out_win[2][:].indirect(slots(2 * h, 2 * h + 2)), dv2[:, cols(2 * h, 2 * h + 2)])
+        store(2)
+        dv3 = turn_back(3, 0, 4, 5, nc.vector.tensor_copy)
+        nc.vector.tensor_copy(out_win[3][:].indirect(offsets[:]), dv3[:])
+        store(3)
+        gg_bank = bank("gg_bank", 6, [P, P])
+        turn(gg_bank[:], gg[:])
+        gg_rows = keep.tile([QUADRANT, P], F32, name="gg_rows")
+        nc.scalar.copy(gg_rows[:], gg_bank[0:QUADRANT, :])
+        nc.sync.dma_start(out_1.rearrange("o (c i) -> (o c) i", c=CHUNKS), gg_rows[0:CHUNKS, :])

@@ -111,7 +111,9 @@ def tile_attend_gwnorm_vg_kernel(tc, vT, x, cs, gl, y, us, wt, offs, out_0, out_
                     turn(x_bank[:, t, u, :], xb_words[:, cols(2 * t + u, 2 * t + u + 1)])
             nc.scalar.copy(xd_words[:, 2 * h : 2 * h + 2, :, :], x_bank[:].rearrange("m t u p -> m t p u"))
         xr = keep.tile([P, PACK, P, PACK], BF16, name="xr", align_bytes=64)
-        nc.vector.tensor_copy(xr[:].rearrange("p j m t -> p m t j"), xs[:].rearrange("p t (m j) -> p m t j", j=PACK))
+        xr_walk = xr[:].rearrange("p j m t -> p m t j")
+        xs_walk = xs[:].rearrange("p t (m j) -> p m t j", j=PACK)
+        nc.vector.tensor_copy(xr_walk, xs_walk)
         xd_codes = keep.tile([P, R], U32, name="xd_codes", align_bytes=64)
         xd_scales = keep.tile([P, R], U8, name="xd_scales", align_bytes=64)
         xr_codes = keep.tile([P, D], U32, name="xr_codes", align_bytes=64)
@@ -128,47 +130,54 @@ def tile_attend_gwnorm_vg_kernel(tc, vT, x, cs, gl, y, us, wt, offs, out_0, out_
         gl_bank = bank("gl_bank", 3, [P, CHUNKS, P])
         for c in range(CHUNKS):
             turn(gl_bank[:, c, :], gl_g[:, cols(c, c + 1)])
-        gl_col = keep.tile([P, CHUNKS], F32, name="gl_col")
+        gl_col = keep.tile([P, CHUNKS], F32, name="gl_col", align_bytes=64)
         nc.scalar.copy(gl_col[:], gl_bank[:, :, 0])
 
         vg = keep.tile([P, PACK, N], F32, name="vg")
-        vt = keep.tile([P, CHUNKS, PACK, P], F32, name="vt")
+        vt = keep.tile([P, CHUNKS, PACK, P], F32, name="vt", align_bytes=64)
         vc = {}
-        nn_bank = [bank(f"nn_bank{c}", 4 + c, [P, P]) for c in range(CHUNKS)]
+        nn_bank = [bank(f"nn_bank{h}", 6 + h, [P, 2, P]) for h in range(2)]
 
         def square(j, c0, c1):
             sq = ring.tile([P, N], F32, name="sq", bufs=CHUNKS)
             run = cols(c0, c1)
             nc.scalar.activation(sq[:, run], vg[:, j, run], ACT.Square, scale=cs4[:, j : j + 1])
             for c in range(c0, c1):
-                turn(nn_bank[c][:], sq[:, cols(c, c + 1)], start=(j == 0), stop=(j == LAST))
+                turn(nn_bank[c // 2][:, c % 2, :], sq[:, cols(c, c + 1)],
+                     start=(j == 0 and c % 2 == 0), stop=(j == LAST and c % 2 == 1))
 
         def turn_plane(j, number):
             v_bank = bank("v_bank", number, [P, CHUNKS, P])
             for c in range(CHUNKS):
                 turn(v_bank[:, c, :], vg[:, j, cols(c, c + 1)])
-            (nc.scalar.copy if j < LAST else nc.vector.tensor_copy)(vt[:, :, j, :], v_bank[:])
+            return v_bank
 
-        def weigh(j0, j1, window):
-            part = keep.tile([P, CHUNKS, j1 - j0, P], F32, name=f"vc{j0}", tag=f"v_win{window}", align_bytes=64)
-            nc.vector.tensor_tensor(part[:], vt[:, :, j0:j1, :],
-                                    cs2_row[:, j0:j1, :].unsqueeze(1).to_broadcast([P, CHUNKS, j1 - j0, P]), ALU.mult)
-            vc[j0, j1] = part
+        def weigh(dst, src, j):
+            nc.vector.tensor_tensor(dst, src, cs2_row[:, j : j + 1, :].to_broadcast([P, CHUNKS, P]), ALU.mult)
+
+        def weighed(j0, j1, tag):
+            vc[j0, j1] = keep.tile([P, CHUNKS, j1 - j0, P], F32, name=f"vc{j0}", tag=tag, align_bytes=64)
+            return vc[j0, j1]
 
         def gather(j, c0, c1):
-            nc.vector.tensor_copy(vg[:, j, cols(c0, c1)], v_win[j][:].indirect(slots(c0, c1)))
+            (scalar_copy if j == 0 else nc.vector.tensor_copy)(vg[:, j, cols(c0, c1)], v_win[j][:].indirect(slots(c0, c1)))
 
         for j in range(LAST):
             for h in range(2):
                 gather(j, 2 * h, 2 * h + 2)
             if j > 0:
-                weigh(j - 1, j, j)
-            turn_plane(j, 2 + j % 2)
+                weigh(weighed(j - 1, (1, PACK)[j - 1], f"v_win{j}")[:, :, 0, :], vt[:, :, j - 1, :], j - 1)
+            nc.scalar.copy(vt[:, :, j, :], turn_plane(j, 2 + j % 2)[:])
             square(j, 0, CHUNKS)
-        out_win = []
+        out_win = {}
+
+        def clear(j, engine, tag, pieces):
+            out_win[j] = keep.tile([P, T], F32, name=f"out_win{j}", tag=tag, align_bytes=64)
+            for q in range(0, T, T // pieces):
+                engine.memset(out_win[j][:, q : q + T // pieces].bitcast(U32), 0)
+
         for j in range(PACK):
-            out_win.append(keep.tile([P, T], F32, name=f"out_win{j}"))
-            (nc.gpsimd if j == LAST else nc.vector).memset(out_win[j][:].bitcast(U32), 0)
+            clear(j, nc.vector, f"out_win{j}", 2)
         for h in range(2):
             gather(LAST, 2 * h, 2 * h + 2)
 
@@ -178,12 +187,12 @@ def tile_attend_gwnorm_vg_kernel(tc, vT, x, cs, gl, y, us, wt, offs, out_0, out_
         rl = keep.tile([P, CHUNKS], F32, name="rl")
         s = keep.tile([P, CHUNKS], F32, name="s")
         srl = keep.tile([P, CHUNKS], F32, name="srl")
-        a_bank, sa_bank, b_bank, y2, gi, sb, kv = {}, {}, {}, {}, {}, {}, {}
+        a_bank, sa_bank, b_bank, y2, gi, sb, kv, kv_part, whole = {}, {}, {}, {}, {}, {}, {}, {}, {}
 
         def lengths(c):
             one = slice(c, c + 1)
             terms = ring.tile([P, P], F32, name="terms")
-            nc.scalar.activation(terms[:], nn_bank[c][:], ACT.Copy, accum_out=nn[:, one])
+            nc.scalar.activation(terms[:], nn_bank[c // 2][:, c % 2, :], ACT.Copy, accum_out=nn[:, one])
             nc.scalar.activation(rl[:, one], nn[:, one], ACT.Abs_reciprocal_sqrt)
             nc.scalar.activation(s[:, one], rl[:, one], ACT.Copy, scale=gl_col[:, one])
 
@@ -199,14 +208,18 @@ def tile_attend_gwnorm_vg_kernel(tc, vT, x, cs, gl, y, us, wt, offs, out_0, out_
 
         def first_product(c):
             run = cols(c, c + 1)
-            a_bank[c] = bank("a_bank", (0, 1, 3, 4)[c], [P, R])
+            a_bank[c] = bank("a_bank", (0, 1, 4, 5)[c], [P, R])
             nc.tensor.matmul_mx(a_bank[c][:], v_codes[:, run].bitcast(E4M3), v_scales[:, run],
                                 xd_codes[:].bitcast(E4M3), xd_scales[:], start=True, stop=True)
 
         def scale_and_turn(c):
             sa = ring.tile([P, PACK, P], F32, name="sa", bufs=CHUNKS)
-            nc.scalar.activation(sa[:].rearrange("i t p -> i (t p)"), a_bank[c][:], ACT.Copy, scale=s[:, c : c + 1])
-            sa_bank[c] = bank("sa_bank", (5, 6, 7, 2)[c], [P, PACK, P])
+            if c == 0:
+                nc.vector.tensor_scalar(sa[:].rearrange("i t p -> i (t p)"), a_bank[c][:], rl[:, 0:1], gl_col[:, 0:1],
+                                        ALU.mult, ALU.mult)
+            else:
+                nc.scalar.activation(sa[:].rearrange("i t p -> i (t p)"), a_bank[c][:], ACT.Copy, scale=s[:, c : c + 1])
+            sa_bank[c] = bank("sa_bank", (2, 6, 7, 0)[c], [P, PACK, P])
             for t in range(PACK):
                 turn(sa_bank[c][:, t, :], sa[:, t, :])
 
@@ -216,7 +229,7 @@ def tile_attend_gwnorm_vg_kernel(tc, vT, x, cs, gl, y, us, wt, offs, out_0, out_
                 nc.vector.tensor_scalar(y2[h][:, t, :], ys[h][:, t, :], c2n[:, t : t + 1], None, ALU.mult)
 
         def gradient(c):
-            g = ring.tile([P, PACK, P], BF16, name="g", bufs=CHUNKS)
+            g = keep.tile([P, PACK, P], BF16, name=f"g{c}")
             for t in range(PACK):
                 nc.vector.scalar_tensor_tensor(g[:, t, :], sa_bank[c][:, t, :], c1[:, t : t + 1],
                                                y2[c // 2][:, t, cols(c % 2, c % 2 + 1)], ALU.mult, ALU.add)
@@ -227,7 +240,7 @@ def tile_attend_gwnorm_vg_kernel(tc, vT, x, cs, gl, y, us, wt, offs, out_0, out_
             g_codes = keep.tile([P, P], U32, name=f"g_codes{c}", align_bytes=64)
             g_scales = keep.tile([P, P], U8, name=f"g_scales{c}", align_bytes=64)
             nc.vector.quantize_mx(g_codes[:].bitcast(E5M2), g_scales[:], gi[c][:].rearrange("p i t -> p (i t)"))
-            b_bank[c] = bank("b_bank", (0, 1, 3, 4)[c], [P, PACK, P])
+            b_bank[c] = bank("b_bank", (1, 4, 3, 5)[c], [P, PACK, P])
             nc.tensor.matmul_mx(b_bank[c][:].rearrange("i j p -> i (j p)"), g_codes[:].bitcast(E5M2), g_scales[:],
                                 xr_codes[:].bitcast(E4M3), xr_scales[:], start=True, stop=True)
 
@@ -236,74 +249,96 @@ def tile_attend_gwnorm_vg_kernel(tc, vT, x, cs, gl, y, us, wt, offs, out_0, out_
             nc.vector.scalar_tensor_tensor(products[:], b_bank[c][:], rl[:, c : c + 1], vt[:, c, :, :], ALU.mult, ALU.mult,
                                            accum_out=gg[:, c : c + 1])
 
-        def two_terms(c):
-            one = slice(c, c + 1)
-            sb[c] = keep.tile([P, PACK, P], F32, name=f"sb{c}")
-            nc.scalar.activation(sb[c][:], b_bank[c][:], ACT.Copy, scale=s[:, one])
-            kv[c] = keep.tile([P, PACK, P], F32, name=f"kv{c}")
-            for (j0, j1), part in vc.items():
-                nc.vector.tensor_scalar(kv[c][:, j0:j1, :], part[:, c, :, :], gg[:, one], srl[:, one], ALU.mult, ALU.mult)
+        def weigh_on_gpsimd(j):
+            for c in range(CHUNKS):
+                nc.gpsimd.tensor_tensor(vc[1, PACK][:, c, j - 1, :], vt[:, c, j, :], cs2_row[:, j, :], ALU.mult)
+
+        def first_term(c, j0):
+            part = keep.tile([P, PACK - j0, P], F32, name=f"sb{c}")
+            nc.scalar.activation(part[:], b_bank[c][:, j0:, :], ACT.Copy, scale=s[:, c : c + 1])
+            for j in range(j0, PACK):
+                sb[c, j] = part[:, j - j0, :]
+
+        def second_term(c, j0, j1):
+            part = keep.tile([P, j1 - j0, P], F32, name=f"kv{c}_{j0}")
+            nc.vector.tensor_scalar(part[:], vc[j0, j1][:, c, :, :], gg[:, c : c + 1], srl[:, c : c + 1], ALU.mult, ALU.mult)
+            kv_part[c, j0] = part
+            for j in range(j0, j1):
+                kv[c, j] = part[:, j - j0, :]
+
+        def both_terms(c, j0, j1):
+            part = keep.tile([P, j1 - j0, P], F32, name=f"whole{c}_{j0}")
+            nc.vector.scalar_tensor_tensor(part[:], b_bank[c][:, j0:j1, :], s[:, c : c + 1], kv_part[c, j0][:], ALU.mult, ALU.add)
+            for j in range(j0, j1):
+                whole[c, j] = part[:, j - j0, :]
 
         def turn_back(j, c0, c1, number, copy):
             dv_bank = bank("dv_bank", number, [P, c1 - c0, P])
             for c in range(c0, c1):
-                turn(dv_bank[:, c - c0, :], sb[c][:, j, :], start=(c == c0), stop=False)
-            for c in range(c0, c1):
-                turn(dv_bank[:, c - c0, :], kv[c][:, j, :], start=False, stop=(c == c1 - 1))
+                if (c, j) in whole:
+                    turn(dv_bank[:, c - c0, :], whole[c, j], start=(c == c0), stop=(c == c1 - 1))
+                else:
+                    turn(dv_bank[:, c - c0, :], sb[c, j], start=(c == c0), stop=False)
+                    turn(dv_bank[:, c - c0, :], kv[c, j], start=False, stop=(c == c1 - 1))
             dv = keep.tile([P, (c1 - c0) * P], F32, name=f"dv{j}_{c0}")
             copy(dv[:], dv_bank[:].rearrange("p c i -> p (c i)"))
             return dv
 
         out_planes = out_0.rearrange("(p j) n -> p j n", j=PACK)
 
-        def store(j):
-            nc.sync.dma_start(out_planes[:, j, :], out_win[j][:])
+        def store(j, queue=nc.sync):
+            queue.dma_start(out_planes[:, j, :], out_win[j][:])
 
-        for c in range(2):
-            square(LAST, c, c + 1)
-        square(LAST, 2, 4)
+        for h in range(2):
+            square(LAST, 2 * h, 2 * h + 2)
+        v_bank = turn_plane(LAST, 3)
         for c in range(CHUNKS):
             weave_v(c)
             quantise_v(c)
-            first_product(c)
+        for c in range(CHUNKS):
             lengths(c)
+        for c in range(LAST):
+            first_product(c)
+        scale_and_turn(0)
+        first_product(LAST)
+        for c in range(1, CHUNKS):
             scale_and_turn(c)
-            if c == 0:
-                turn_plane(LAST, 2)
         targets(0)
         gradient(0)
         second_product(0)
-        gradient(1)
-        second_product(1)
+        nc.vector.tensor_copy(vt[:, :, LAST, :], v_bank[:])
+        for j in range(2, PACK):
+            weigh_on_gpsimd(j)
         targets(1)
+        for c in range(1, CHUNKS):
+            gradient(c)
+            second_product(c)
         nc.vector.scalar_tensor_tensor(srl[:], s[:], -1.0, rl[:], ALU.mult, ALU.mult)
-        gradient(2)
-        second_product(2)
-        gradient(3)
-        second_product(3)
-        weigh(2, 4, LAST)
-        for c in range(2):
+        for c in range(CHUNKS):
             projection(c)
-            two_terms(c)
-        dv = turn_back(0, 0, 2, 5, nc.scalar.copy)
-        scalar_copy(out_win[0][:].indirect(slots(0, 2)), dv[:])
-        for c in range(2, CHUNKS):
-            projection(c)
-            two_terms(c)
-        dv = turn_back(0, 2, 4, 6, nc.scalar.copy)
-        scalar_copy(out_win[0][:].indirect(slots(2, 4)), dv[:])
+            second_term(c, 0, 1)
+            both_terms(c, 0, 1)
+            if c % 2 == 1:
+                dv = turn_back(0, c - 1, c + 1, (2, 6)[c // 2], nc.scalar.copy)
+                scalar_copy(out_win[0][:].indirect(slots(c - 1, c + 1)), dv[:])
         store(0)
+        for c in range(CHUNKS):
+            second_term(c, 1, PACK)
+            if c < 2:
+                first_term(c, 1)
+            else:
+                both_terms(c, 1, PACK)
         dv1 = turn_back(1, 0, 4, 7, nc.vector.tensor_copy)
         nc.vector.tensor_copy(out_win[1][:].indirect(offsets[:]), dv1[:])
         store(1)
-        dv2 = turn_back(2, 0, 4, 2, nc.scalar.copy)
-        for h in range(2):
-            scalar_copy(out_win[2][:].indirect(slots(2 * h, 2 * h + 2)), dv2[:, cols(2 * h, 2 * h + 2)])
-        store(2)
-        dv3 = turn_back(3, 0, 4, 5, nc.vector.tensor_copy)
+        dv2 = turn_back(2, 0, 4, 0, nc.scalar.copy)
+        scalar_copy(out_win[2][:].indirect(slots(0, 2)), dv2[:, cols(0, 2)])
+        dv3 = turn_back(3, 0, 4, 1, nc.scalar.copy)
+        scalar_copy(out_win[2][:].indirect(slots(2, 4)), dv2[:, cols(2, 4)])
+        store(2, nc.scalar)
         nc.vector.tensor_copy(out_win[3][:].indirect(offsets[:]), dv3[:])
         store(3)
-        gg_bank = bank("gg_bank", 6, [P, P])
+        gg_bank = bank("gg_bank", 2, [P, P])
         turn(gg_bank[:], gg[:])
         gg_rows = keep.tile([QUADRANT, P], F32, name="gg_rows")
         nc.scalar.copy(gg_rows[:], gg_bank[0:QUADRANT, :])

@@ -214,11 +214,7 @@ def tile_attend_gwnorm_vg_kernel(tc, vT, x, cs, gl, y, us, wt, offs, out_0, out_
 
         def scale_and_turn(c):
             sa = ring.tile([P, PACK, P], F32, name="sa", bufs=CHUNKS)
-            if c == 0:
-                nc.vector.tensor_scalar(sa[:].rearrange("i t p -> i (t p)"), a_bank[c][:], rl[:, 0:1], gl_col[:, 0:1],
-                                        ALU.mult, ALU.mult)
-            else:
-                nc.scalar.activation(sa[:].rearrange("i t p -> i (t p)"), a_bank[c][:], ACT.Copy, scale=s[:, c : c + 1])
+            nc.scalar.activation(sa[:].rearrange("i t p -> i (t p)"), a_bank[c][:], ACT.Copy, scale=s[:, c : c + 1])
             sa_bank[c] = bank("sa_bank", (2, 6, 7, 0)[c], [P, PACK, P])
             for t in range(PACK):
                 turn(sa_bank[c][:, t, :], sa[:, t, :])
@@ -249,10 +245,6 @@ def tile_attend_gwnorm_vg_kernel(tc, vT, x, cs, gl, y, us, wt, offs, out_0, out_
             nc.vector.scalar_tensor_tensor(products[:], b_bank[c][:], rl[:, c : c + 1], vt[:, c, :, :], ALU.mult, ALU.mult,
                                            accum_out=gg[:, c : c + 1])
 
-        def weigh_on_gpsimd(j):
-            for c in range(CHUNKS):
-                nc.gpsimd.tensor_tensor(vc[1, PACK][:, c, j - 1, :], vt[:, c, j, :], cs2_row[:, j, :], ALU.mult)
-
         def first_term(c, j0):
             part = keep.tile([P, PACK - j0, P], F32, name=f"sb{c}")
             nc.scalar.activation(part[:], b_bank[c][:, j0:, :], ACT.Copy, scale=s[:, c : c + 1])
@@ -266,24 +258,18 @@ def tile_attend_gwnorm_vg_kernel(tc, vT, x, cs, gl, y, us, wt, offs, out_0, out_
             for j in range(j0, j1):
                 kv[c, j] = part[:, j - j0, :]
 
-        def both_terms(c, j0, j1):
-            part = keep.tile([P, j1 - j0, P], F32, name=f"whole{c}_{j0}")
-            nc.vector.scalar_tensor_tensor(part[:], b_bank[c][:, j0:j1, :], s[:, c : c + 1], kv_part[c, j0][:], ALU.mult, ALU.add)
-            for j in range(j0, j1):
-                whole[c, j] = part[:, j - j0, :]
+        def turn_back(j, h, number, copy, tag):
+            dv_bank = bank("dv_bank", number, [P, 2, P])
+            for c in range(2 * h, 2 * h + 2):
+                turn(dv_bank[:, c % 2, :], sb[c, j], start=(c % 2 == 0), stop=False)
+                turn(dv_bank[:, c % 2, :], kv[c, j], start=False, stop=(c % 2 == 1))
+            dv[j, h] = keep.tile([P, HALF], F32, name=f"dv{j}_{h}", tag=tag)
+            copy(dv[j, h][:], dv_bank[:].rearrange("p c i -> p (c i)"))
 
-        def turn_back(j, c0, c1, number, copy):
-            dv_bank = bank("dv_bank", number, [P, c1 - c0, P])
-            for c in range(c0, c1):
-                if (c, j) in whole:
-                    turn(dv_bank[:, c - c0, :], whole[c, j], start=(c == c0), stop=(c == c1 - 1))
-                else:
-                    turn(dv_bank[:, c - c0, :], sb[c, j], start=(c == c0), stop=False)
-                    turn(dv_bank[:, c - c0, :], kv[c, j], start=False, stop=(c == c1 - 1))
-            dv = keep.tile([P, (c1 - c0) * P], F32, name=f"dv{j}_{c0}")
-            copy(dv[:], dv_bank[:].rearrange("p c i -> p (c i)"))
-            return dv
+        def put(copy, j, h):
+            copy(out_win[j][:].indirect(slots(2 * h, 2 * h + 2)), dv[j, h][:])
 
+        dv = {}
         out_planes = out_0.rearrange("(p j) n -> p j n", j=PACK)
 
         def store(j, queue=nc.sync):
@@ -307,39 +293,45 @@ def tile_attend_gwnorm_vg_kernel(tc, vT, x, cs, gl, y, us, wt, offs, out_0, out_
         gradient(0)
         second_product(0)
         nc.vector.tensor_copy(vt[:, :, LAST, :], v_bank[:])
-        for j in range(2, PACK):
-            weigh_on_gpsimd(j)
         targets(1)
+        nc.vector.tensor_tensor(vc[1, PACK][:, :, 1:, :], vt[:, :, 2:, :],
+                                cs2_row[:, 2:, :].unsqueeze(1).to_broadcast([P, CHUNKS, 2, P]), ALU.mult)
         for c in range(1, CHUNKS):
             gradient(c)
             second_product(c)
         nc.vector.scalar_tensor_tensor(srl[:], s[:], -1.0, rl[:], ALU.mult, ALU.mult)
-        for c in range(CHUNKS):
+        for c in range(2):
             projection(c)
+            first_term(c, 0)
             second_term(c, 0, 1)
-            both_terms(c, 0, 1)
-            if c % 2 == 1:
-                dv = turn_back(0, c - 1, c + 1, (2, 6)[c // 2], nc.scalar.copy)
-                scalar_copy(out_win[0][:].indirect(slots(c - 1, c + 1)), dv[:])
-        store(0)
-        for c in range(CHUNKS):
             second_term(c, 1, PACK)
-            if c < 2:
-                first_term(c, 1)
-            else:
-                both_terms(c, 1, PACK)
-        dv1 = turn_back(1, 0, 4, 7, nc.vector.tensor_copy)
-        nc.vector.tensor_copy(out_win[1][:].indirect(offsets[:]), dv1[:])
+        turn_back(0, 0, 2, nc.scalar.copy, "dv_a")
+        for c in range(2, CHUNKS):
+            projection(c)
+            first_term(c, 0)
+            second_term(c, 0, 1)
+            second_term(c, 1, PACK)
+        put(nc.vector.tensor_copy, 0, 0)
+        turn_back(0, 1, 0, nc.vector.tensor_copy, "dv_b")
+        turn_back(1, 0, 6, nc.scalar.copy, "dv_s0")
+        turn_back(2, 0, 7, nc.scalar.copy, "dv_s1")
+        put(scalar_copy, 1, 0)
+        put(nc.vector.tensor_copy, 0, 1)
+        store(0)
+        turn_back(1, 1, 1, nc.vector.tensor_copy, "dv_a")
+        turn_back(3, 0, 2, nc.vector.tensor_copy, "dv_b")
+        put(nc.vector.tensor_copy, 1, 1)
         store(1)
-        dv2 = turn_back(2, 0, 4, 0, nc.scalar.copy)
-        scalar_copy(out_win[2][:].indirect(slots(0, 2)), dv2[:, cols(0, 2)])
-        dv3 = turn_back(3, 0, 4, 1, nc.scalar.copy)
-        scalar_copy(out_win[2][:].indirect(slots(2, 4)), dv2[:, cols(2, 4)])
-        store(2, nc.scalar)
-        nc.vector.tensor_copy(out_win[3][:].indirect(offsets[:]), dv3[:])
+        put(scalar_copy, 2, 0)
+        turn_back(2, 1, 3, nc.vector.tensor_copy, "dv_a")
+        put(nc.vector.tensor_copy, 3, 0)
+        turn_back(3, 1, 5, nc.scalar.copy, "dv_b")
+        put(nc.vector.tensor_copy, 2, 1)
+        store(2)
+        put(nc.vector.tensor_copy, 3, 1)
         store(3)
-        gg_bank = bank("gg_bank", 2, [P, P])
+        gg_bank = bank("gg_bank", 5, [P, P])
         turn(gg_bank[:], gg[:])
         gg_rows = keep.tile([QUADRANT, P], F32, name="gg_rows")
         nc.scalar.copy(gg_rows[:], gg_bank[0:QUADRANT, :])
-        nc.sync.dma_start(out_1.rearrange("o (c i) -> (o c) i", c=CHUNKS), gg_rows[0:CHUNKS, :])
+        nc.scalar.dma_start(out_1.rearrange("o (c i) -> (o c) i", c=CHUNKS), gg_rows[0:CHUNKS, :])

@@ -30,8 +30,10 @@ GL_RUN = T // P
 def tile_attend_gwnorm_vg_kernel(tc, vT, x, cs, gl, y, us, wt, offs, out_0, out_1):
     nc = tc.nc
     with ExitStack() as ctx:
+        low = ctx.enter_context(tc.tile_pool(name="low", bufs=1))
         keep = ctx.enter_context(tc.tile_pool(name="keep", bufs=1))
         ring = ctx.enter_context(tc.tile_pool(name="ring", bufs=2))
+        high = ctx.enter_context(tc.tile_pool(name="high", bufs=1))
         psum = ctx.enter_context(tc.psum_pool(name="psum", bufs=1))
 
         def bank(name, number, shape):
@@ -172,7 +174,7 @@ def tile_attend_gwnorm_vg_kernel(tc, vT, x, cs, gl, y, us, wt, offs, out_0, out_
         out_win = {}
 
         def clear(j, engine, tag, pieces):
-            out_win[j] = keep.tile([P, T], F32, name=f"out_win{j}", tag=tag, align_bytes=64)
+            out_win[j] = (low if j % 2 else high).tile([P, T], F32, name=f"out_win{j}", tag=tag, align_bytes=64)
             for q in range(0, T, T // pieces):
                 engine.memset(out_win[j][:, q : q + T // pieces].bitcast(U32), 0)
 
@@ -258,16 +260,19 @@ def tile_attend_gwnorm_vg_kernel(tc, vT, x, cs, gl, y, us, wt, offs, out_0, out_
             for j in range(j0, j1):
                 kv[c, j] = part[:, j - j0, :]
 
-        def turn_back(j, h, number, copy, tag):
-            dv_bank = bank("dv_bank", number, [P, 2, P])
-            for c in range(2 * h, 2 * h + 2):
-                turn(dv_bank[:, c % 2, :], sb[c, j], start=(c % 2 == 0), stop=False)
-                turn(dv_bank[:, c % 2, :], kv[c, j], start=False, stop=(c % 2 == 1))
-            dv[j, h] = keep.tile([P, HALF], F32, name=f"dv{j}_{h}", tag=tag)
-            copy(dv[j, h][:], dv_bank[:].rearrange("p c i -> p (c i)"))
+        def turn_back(j, c0, c1, number, copy, tag):
+            dv_bank = bank("dv_bank", number, [P, c1 - c0, P])
+            for c in range(c0, c1):
+                turn(dv_bank[:, c - c0, :], sb[c, j], start=(c == c0), stop=False)
+                turn(dv_bank[:, c - c0, :], kv[c, j], start=False, stop=(c == c1 - 1))
+            part = keep.tile([P, c1 - c0, P], F32, name=f"dv{j}_{c0}", tag=tag)
+            copy(part[:], dv_bank[:])
+            for c in range(c0, c1):
+                dv[j, c] = (part, c - c0)
 
-        def put(copy, j, h):
-            copy(out_win[j][:].indirect(slots(2 * h, 2 * h + 2)), dv[j, h][:])
+        def put(copy, j, c0, c1):
+            part, first = dv[j, c0]
+            copy(out_win[j][:].indirect(slots(c0, c1)), part[:, first : first + c1 - c0, :].rearrange("p c i -> p (c i)"))
 
         dv = {}
         out_planes = out_0.rearrange("(p j) n -> p j n", j=PACK)
@@ -305,33 +310,28 @@ def tile_attend_gwnorm_vg_kernel(tc, vT, x, cs, gl, y, us, wt, offs, out_0, out_
             first_term(c, 0)
             second_term(c, 0, 1)
             second_term(c, 1, PACK)
-        turn_back(0, 0, 2, nc.scalar.copy, "dv_a")
+        turn_back(0, 0, 2, 2, nc.scalar.copy, "dv_s0")
         for c in range(2, CHUNKS):
             projection(c)
             first_term(c, 0)
             second_term(c, 0, 1)
             second_term(c, 1, PACK)
-        put(nc.vector.tensor_copy, 0, 0)
-        turn_back(0, 1, 0, nc.vector.tensor_copy, "dv_b")
-        turn_back(1, 0, 6, nc.scalar.copy, "dv_s0")
-        turn_back(2, 0, 7, nc.scalar.copy, "dv_s1")
-        put(scalar_copy, 1, 0)
-        put(nc.vector.tensor_copy, 0, 1)
+        put(scalar_copy, 0, 0, 2)
+        turn_back(0, 2, 4, 0, nc.vector.tensor_copy, "dv_s1")
+        turn_back(1, 0, 4, 6, nc.vector.tensor_copy, "dv_v")
+        put(scalar_copy, 0, 2, 4)
         store(0)
-        turn_back(1, 1, 1, nc.vector.tensor_copy, "dv_a")
-        turn_back(3, 0, 2, nc.vector.tensor_copy, "dv_b")
-        put(nc.vector.tensor_copy, 1, 1)
+        put(nc.vector.tensor_copy, 1, 0, 4)
         store(1)
-        put(scalar_copy, 2, 0)
-        turn_back(2, 1, 3, nc.vector.tensor_copy, "dv_a")
-        put(nc.vector.tensor_copy, 3, 0)
-        turn_back(3, 1, 5, nc.scalar.copy, "dv_b")
-        put(nc.vector.tensor_copy, 2, 1)
-        store(2)
-        put(nc.vector.tensor_copy, 3, 1)
+        turn_back(2, 0, 4, 0, nc.scalar.copy, "dv_s0")
+        turn_back(3, 0, 4, 6, nc.scalar.copy, "dv_d")
+        put(scalar_copy, 2, 0, 2)
+        put(scalar_copy, 2, 2, 4)
+        store(2, nc.scalar)
+        put(nc.vector.tensor_copy, 3, 0, 4)
         store(3)
-        gg_bank = bank("gg_bank", 5, [P, P])
+        gg_bank = bank("gg_bank", 6, [P, P])
         turn(gg_bank[:], gg[:])
         gg_rows = keep.tile([QUADRANT, P], F32, name="gg_rows")
         nc.scalar.copy(gg_rows[:], gg_bank[0:QUADRANT, :])
-        nc.scalar.dma_start(out_1.rearrange("o (c i) -> (o c) i", c=CHUNKS), gg_rows[0:CHUNKS, :])
+        nc.sync.dma_start(out_1.rearrange("o (c i) -> (o c) i", c=CHUNKS), gg_rows[0:CHUNKS, :])

@@ -30,10 +30,8 @@ GL_RUN = T // P
 def tile_attend_gwnorm_vg_kernel(tc, vT, x, cs, gl, y, us, wt, offs, out_0, out_1):
     nc = tc.nc
     with ExitStack() as ctx:
-        low = ctx.enter_context(tc.tile_pool(name="low", bufs=1))
         keep = ctx.enter_context(tc.tile_pool(name="keep", bufs=1))
         ring = ctx.enter_context(tc.tile_pool(name="ring", bufs=2))
-        high = ctx.enter_context(tc.tile_pool(name="high", bufs=1))
         psum = ctx.enter_context(tc.psum_pool(name="psum", bufs=1))
 
         def bank(name, number, shape):
@@ -85,7 +83,7 @@ def tile_attend_gwnorm_vg_kernel(tc, vT, x, cs, gl, y, us, wt, offs, out_0, out_
         y_planes = y.rearrange("(p t) i -> p t i", t=PACK)
         ys = []
         for h in range(2):
-            ys.append(keep.tile([P, PACK, HALF], F32, name=f"ys{h}"))
+            ys.append(keep.tile([P, PACK, HALF], F32, name=f"ys{h}", align_bytes=64))
             nc.sync.dma_start(ys[h][:], y_planes[:, :, h * HALF : (h + 1) * HALF])
 
         ident = keep.tile([P, P], F32, name="ident")
@@ -174,12 +172,11 @@ def tile_attend_gwnorm_vg_kernel(tc, vT, x, cs, gl, y, us, wt, offs, out_0, out_
         out_win = {}
 
         def clear(j, engine, tag, pieces):
-            out_win[j] = (low if j % 2 else high).tile([P, T], F32, name=f"out_win{j}", tag=tag, align_bytes=64)
+            out_win[j] = keep.tile([P, T], F32, name=f"out_win{j}", tag=tag, align_bytes=64)
             for q in range(0, T, T // pieces):
                 engine.memset(out_win[j][:, q : q + T // pieces].bitcast(U32), 0)
 
-        for j in range(PACK):
-            clear(j, nc.vector, f"out_win{j}", 2)
+        clear(0, nc.vector, "out_win0", 2)
         for h in range(2):
             gather(LAST, 2 * h, 2 * h + 2)
 
@@ -299,6 +296,8 @@ def tile_attend_gwnorm_vg_kernel(tc, vT, x, cs, gl, y, us, wt, offs, out_0, out_
         second_product(0)
         nc.vector.tensor_copy(vt[:, :, LAST, :], v_bank[:])
         targets(1)
+        for j, tag in ((1, "vi3"), (2, "ys0"), (3, "ys1")):
+            clear(j, nc.gpsimd, tag, 8)
         nc.vector.tensor_tensor(vc[1, PACK][:, :, 1:, :], vt[:, :, 2:, :],
                                 cs2_row[:, 2:, :].unsqueeze(1).to_broadcast([P, CHUNKS, 2, P]), ALU.mult)
         for c in range(1, CHUNKS):

@@ -88,6 +88,8 @@ def tile_attend_gwnorm_vg_kernel(tc, vT, x, cs, gl, y, us, wt, offs, out_0, out_
 
         ident = keep.tile([P, P], F32, name="ident")
         make_identity(nc, ident[:])
+        zeros = keep.tile([P, P], F32, name="zeros")
+        nc.gpsimd.memset(zeros[:], 0.0)
         gg = keep.tile([P, P], F32, name="gg")
         nc.gpsimd.memset(gg[:], 0.0)
 
@@ -99,21 +101,18 @@ def tile_attend_gwnorm_vg_kernel(tc, vT, x, cs, gl, y, us, wt, offs, out_0, out_
         cs2_row = keep.tile([P, PACK, P], F32, name="cs2_row")
         nc.scalar.copy(cs2_row[:], cs2_bank[:])
 
+        x_by_j = xs[:].rearrange("p t (m j) -> p t j m", j=PACK)
         xd = keep.tile([P, PACK, P, PACK], BF16, name="xd", align_bytes=64)
-        xd_words = xd[:].rearrange("m t p j -> m (t p j)").bitcast(F32).rearrange("m (t p u) -> m t p u", t=PACK, u=2)
-        for h in range(2):
-            xb = ring.tile([P, 2, 2, P, 2], BF16, name="xb")
-            nc.vector.tensor_copy(xb[:], xs[:, 2 * h : 2 * h + 2, :].rearrange("p t (m u e) -> p t u m e", u=2, e=2))
-            xb_words = xb[:].rearrange("p t u m e -> p (t u m e)").bitcast(F32)
-            x_bank = bank("x_bank", h, [P, 2, 2, P])
-            for t in range(2):
-                for u in range(2):
-                    turn(x_bank[:, t, u, :], xb_words[:, cols(2 * t + u, 2 * t + u + 1)])
-            nc.scalar.copy(xd_words[:, 2 * h : 2 * h + 2, :, :], x_bank[:].rearrange("m t u p -> m t p u"))
+        for t in range(PACK):
+            x_bank = bank("x_bank", (0, 1, 4, 5)[t], [P, PACK, P])
+            for j in range(PACK):
+                turn(x_bank[:, j, :], x_by_j[:, t, j, :])
+            nc.scalar.copy(xd[:, t, :, :], x_bank[:].rearrange("m j p -> m p j"))
         xr = keep.tile([P, PACK, P, PACK], BF16, name="xr", align_bytes=64)
         xr_walk = xr[:].rearrange("p j m t -> p m t j")
         xs_walk = xs[:].rearrange("p t (m j) -> p m t j", j=PACK)
-        nc.vector.tensor_copy(xr_walk, xs_walk)
+        nc.vector.tensor_copy(xr_walk[:, : P // 2], xs_walk[:, : P // 2])
+        nc.scalar.copy(xr_walk[:, P // 2 :], xs_walk[:, P // 2 :])
         xd_codes = keep.tile([P, R], U32, name="xd_codes", align_bytes=64)
         xd_scales = keep.tile([P, R], U8, name="xd_scales", align_bytes=64)
         xr_codes = keep.tile([P, D], U32, name="xr_codes", align_bytes=64)
@@ -126,7 +125,7 @@ def tile_attend_gwnorm_vg_kernel(tc, vT, x, cs, gl, y, us, wt, offs, out_0, out_
         c1 = keep.tile([P, PACK], F32, name="c1")
         nc.vector.scalar_tensor_tensor(c1[:], c2n[:], -1.0, us4[:], ALU.mult, ALU.mult)
         gl_g = keep.tile([P, N], F32, name="gl_g")
-        scalar_copy(gl_g[:], gl_win[:].indirect(offsets[:]))
+        nc.vector.tensor_copy(gl_g[:], gl_win[:].indirect(offsets[:]))
         gl_bank = bank("gl_bank", 3, [P, CHUNKS, P])
         for c in range(CHUNKS):
             turn(gl_bank[:, c, :], gl_g[:, cols(c, c + 1)])
@@ -160,7 +159,7 @@ def tile_attend_gwnorm_vg_kernel(tc, vT, x, cs, gl, y, us, wt, offs, out_0, out_
             return vc[j0, j1]
 
         def gather(j, c0, c1):
-            (scalar_copy if j == 0 else nc.vector.tensor_copy)(vg[:, j, cols(c0, c1)], v_win[j][:].indirect(slots(c0, c1)))
+            nc.vector.tensor_copy(vg[:, j, cols(c0, c1)], v_win[j][:].indirect(slots(c0, c1)))
 
         for j in range(LAST):
             for h in range(2):
@@ -176,7 +175,8 @@ def tile_attend_gwnorm_vg_kernel(tc, vT, x, cs, gl, y, us, wt, offs, out_0, out_
             for q in range(0, T, T // pieces):
                 engine.memset(out_win[j][:, q : q + T // pieces].bitcast(U32), 0)
 
-        clear(0, nc.vector, "out_win0", 2)
+        for j in range(PACK):
+            clear(j, nc.gpsimd if j == LAST else nc.vector, f"out_win{j}", 1 if j == LAST else 2)
         for h in range(2):
             gather(LAST, 2 * h, 2 * h + 2)
 
@@ -186,6 +186,7 @@ def tile_attend_gwnorm_vg_kernel(tc, vT, x, cs, gl, y, us, wt, offs, out_0, out_
         rl = keep.tile([P, CHUNKS], F32, name="rl")
         s = keep.tile([P, CHUNKS], F32, name="s")
         srl = keep.tile([P, CHUNKS], F32, name="srl")
+        k = keep.tile([P, CHUNKS], F32, name="k")
         a_bank, sa_bank, b_bank, y2, gi, sb, kv, kv_part, whole = {}, {}, {}, {}, {}, {}, {}, {}, {}
 
         def lengths(c):
@@ -229,7 +230,7 @@ def tile_attend_gwnorm_vg_kernel(tc, vT, x, cs, gl, y, us, wt, offs, out_0, out_
                 nc.vector.scalar_tensor_tensor(g[:, t, :], sa_bank[c][:, t, :], c1[:, t : t + 1],
                                                y2[c // 2][:, t, cols(c % 2, c % 2 + 1)], ALU.mult, ALU.add)
             gi[c] = keep.tile([P, P, PACK], BF16, name=f"gi{c}", align_bytes=64)
-            interleave(nc.scalar.copy, gi[c][:], g[:])
+            interleave(nc.vector.tensor_copy if c == LAST else nc.scalar.copy, gi[c][:], g[:])
 
         def second_product(c):
             g_codes = keep.tile([P, P], U32, name=f"g_codes{c}", align_bytes=64)
@@ -244,15 +245,20 @@ def tile_attend_gwnorm_vg_kernel(tc, vT, x, cs, gl, y, us, wt, offs, out_0, out_
             nc.vector.scalar_tensor_tensor(products[:], b_bank[c][:], rl[:, c : c + 1], vt[:, c, :, :], ALU.mult, ALU.mult,
                                            accum_out=gg[:, c : c + 1])
 
-        def first_term(c, j0):
-            part = keep.tile([P, PACK - j0, P], F32, name=f"sb{c}")
-            nc.scalar.activation(part[:], b_bank[c][:, j0:, :], ACT.Copy, scale=s[:, c : c + 1])
-            for j in range(j0, PACK):
+        def first_term(c, j0, j1):
+            part = keep.tile([P, j1 - j0, P], F32, name=f"sb{c}_{j0}")
+            nc.scalar.activation(part[:], b_bank[c][:, j0:j1, :], ACT.Copy, scale=s[:, c : c + 1])
+            for j in range(j0, j1):
                 sb[c, j] = part[:, j - j0, :]
 
         def second_term(c, j0, j1):
             part = keep.tile([P, j1 - j0, P], F32, name=f"kv{c}_{j0}")
-            nc.vector.tensor_scalar(part[:], vc[j0, j1][:, c, :, :], gg[:, c : c + 1], srl[:, c : c + 1], ALU.mult, ALU.mult)
+            if c < 2:
+                nc.vector.tensor_scalar(part[:], vc[j0, j1][:, c, :, :], gg[:, c : c + 1], srl[:, c : c + 1], ALU.mult, ALU.mult)
+            else:
+                if j0 == 0:
+                    nc.scalar.activation(k[:, c : c + 1], gg[:, c : c + 1], ACT.Copy, scale=srl[:, c : c + 1])
+                nc.scalar.activation(part[:], vc[j0, j1][:, c, :, :], ACT.Copy, scale=k[:, c : c + 1])
             kv_part[c, j0] = part
             for j in range(j0, j1):
                 kv[c, j] = part[:, j - j0, :]
@@ -270,6 +276,9 @@ def tile_attend_gwnorm_vg_kernel(tc, vT, x, cs, gl, y, us, wt, offs, out_0, out_
         def put(copy, j, c0, c1):
             part, first = dv[j, c0]
             copy(out_win[j][:].indirect(slots(c0, c1)), part[:, first : first + c1 - c0, :].rearrange("p c i -> p (c i)"))
+
+        def add_put(dst, src):
+            nc.vector.tensor_tensor(dst, src, zeros[:], ALU.add)
 
         dv = {}
         out_planes = out_0.rearrange("(p j) n -> p j n", j=PACK)
@@ -296,40 +305,36 @@ def tile_attend_gwnorm_vg_kernel(tc, vT, x, cs, gl, y, us, wt, offs, out_0, out_
         second_product(0)
         nc.vector.tensor_copy(vt[:, :, LAST, :], v_bank[:])
         targets(1)
-        for j, tag in ((1, "vi3"), (2, "ys0"), (3, "ys1")):
-            clear(j, nc.gpsimd, tag, 8)
         nc.vector.tensor_tensor(vc[1, PACK][:, :, 1:, :], vt[:, :, 2:, :],
                                 cs2_row[:, 2:, :].unsqueeze(1).to_broadcast([P, CHUNKS, 2, P]), ALU.mult)
         for c in range(1, CHUNKS):
             gradient(c)
             second_product(c)
         nc.vector.scalar_tensor_tensor(srl[:], s[:], -1.0, rl[:], ALU.mult, ALU.mult)
-        for c in range(2):
-            projection(c)
-            first_term(c, 0)
-            second_term(c, 0, 1)
-            second_term(c, 1, PACK)
-        turn_back(0, 0, 2, 2, nc.scalar.copy, "dv_s0")
+        projection(0)
+        first_term(0, 0, 1)
+        second_term(0, 0, 1)
+        turn_back(0, 0, 1, 2, nc.scalar.copy, "dv00")
+        first_term(0, 1, PACK)
+        projection(1)
+        second_term(0, 1, PACK)
+        for j in range(1, PACK):
+            turn_back(j, 0, 1, (2, 6, 7, 0)[j], nc.scalar.copy, f"dv0{j}")
         for c in range(2, CHUNKS):
             projection(c)
-            first_term(c, 0)
+        for c in range(1, CHUNKS):
+            first_term(c, 0, 1)
             second_term(c, 0, 1)
+        for c in range(1, CHUNKS):
+            first_term(c, 1, PACK)
             second_term(c, 1, PACK)
-        put(scalar_copy, 0, 0, 2)
-        turn_back(0, 2, 4, 0, nc.vector.tensor_copy, "dv_s1")
-        turn_back(1, 0, 4, 6, nc.vector.tensor_copy, "dv_v")
-        put(scalar_copy, 0, 2, 4)
-        store(0)
-        put(nc.vector.tensor_copy, 1, 0, 4)
-        store(1)
-        turn_back(2, 0, 4, 0, nc.scalar.copy, "dv_s0")
-        turn_back(3, 0, 4, 6, nc.scalar.copy, "dv_d")
-        put(scalar_copy, 2, 0, 2)
-        put(scalar_copy, 2, 2, 4)
-        store(2, nc.scalar)
-        put(nc.vector.tensor_copy, 3, 0, 4)
-        store(3)
-        gg_bank = bank("gg_bank", 6, [P, P])
+        for j in range(PACK):
+            put(add_put, j, 0, 1)
+        for j in range(PACK):
+            turn_back(j, 1, CHUNKS, (2, 6, 7, 0)[j], nc.scalar.copy, f"dv1{j}")
+            put(nc.vector.tensor_copy, j, 1, CHUNKS)
+            store(j)
+        gg_bank = bank("gg_bank", 1, [P, P])
         turn(gg_bank[:], gg[:])
         gg_rows = keep.tile([QUADRANT, P], F32, name="gg_rows")
         nc.scalar.copy(gg_rows[:], gg_bank[0:QUADRANT, :])

@@ -88,19 +88,11 @@ def tile_attend_gwnorm_vg_kernel(tc, vT, x, cs, gl, y, us, wt, offs, out_0, out_
 
         ident = keep.tile([P, P], F32, name="ident")
         make_identity(nc, ident[:])
-        zeros = keep.tile([P, P], F32, name="zeros")
-        nc.gpsimd.memset(zeros[:], 0.0)
         gg = keep.tile([P, P], F32, name="gg")
         nc.gpsimd.memset(gg[:], 0.0)
 
         cs2 = keep.tile([P, PACK], F32, name="cs2")
         nc.vector.tensor_tensor(cs2[:], cs4[:], cs4[:], ALU.mult)
-        cs2_bank = bank("cs2_bank", 2, [P, PACK, P])
-        for j in range(PACK):
-            turn(cs2_bank[:, j, :], cs2[:, j : j + 1].to_broadcast([P, P]))
-        cs2_row = keep.tile([P, PACK, P], F32, name="cs2_row")
-        nc.scalar.copy(cs2_row[:], cs2_bank[:])
-
         x_by_j = xs[:].rearrange("p t (m j) -> p t j m", j=PACK)
         xd = keep.tile([P, PACK, P, PACK], BF16, name="xd", align_bytes=64)
         for t in range(PACK):
@@ -113,12 +105,10 @@ def tile_attend_gwnorm_vg_kernel(tc, vT, x, cs, gl, y, us, wt, offs, out_0, out_
         xs_walk = xs[:].rearrange("p t (m j) -> p m t j", j=PACK)
         nc.vector.tensor_copy(xr_walk[:, : P // 2], xs_walk[:, : P // 2])
         nc.scalar.copy(xr_walk[:, P // 2 :], xs_walk[:, P // 2 :])
-        xd_codes = keep.tile([P, R], U32, name="xd_codes", align_bytes=64)
         xd_scales = keep.tile([P, R], U8, name="xd_scales", align_bytes=64)
         xr_codes = keep.tile([P, D], U32, name="xr_codes", align_bytes=64)
         xr_scales = keep.tile([P, D], U8, name="xr_scales", align_bytes=64)
         nc.vector.quantize_mx(xr_codes[:].bitcast(E4M3), xr_scales[:], xr[:].rearrange("p j m t -> p (j m t)"))
-        nc.vector.quantize_mx(xd_codes[:].bitcast(E4M3), xd_scales[:], xd[:].rearrange("m t p j -> m (t p j)"))
 
         c2n = keep.tile([P, PACK], F32, name="c2n")
         nc.vector.scalar_tensor_tensor(c2n[:], wt4[:], -1.0, us4[:], ALU.mult, ALU.mult)
@@ -134,7 +124,6 @@ def tile_attend_gwnorm_vg_kernel(tc, vT, x, cs, gl, y, us, wt, offs, out_0, out_
 
         vg = keep.tile([P, PACK, N], F32, name="vg")
         vt = keep.tile([P, CHUNKS, PACK, P], F32, name="vt", align_bytes=64)
-        vc = {}
         nn_bank = [bank(f"nn_bank{h}", 6 + h, [P, 2, P]) for h in range(2)]
 
         def square(j, c0, c1):
@@ -151,21 +140,15 @@ def tile_attend_gwnorm_vg_kernel(tc, vT, x, cs, gl, y, us, wt, offs, out_0, out_
                 turn(v_bank[:, c, :], vg[:, j, cols(c, c + 1)])
             return v_bank
 
-        def weigh(dst, src, j):
-            nc.vector.tensor_tensor(dst, src, cs2_row[:, j : j + 1, :].to_broadcast([P, CHUNKS, P]), ALU.mult)
-
-        def weighed(j0, j1, tag):
-            vc[j0, j1] = keep.tile([P, CHUNKS, j1 - j0, P], F32, name=f"vc{j0}", tag=tag, align_bytes=64)
-            return vc[j0, j1]
-
         def gather(j, c0, c1):
             nc.vector.tensor_copy(vg[:, j, cols(c0, c1)], v_win[j][:].indirect(slots(c0, c1)))
 
         for j in range(LAST):
             for h in range(2):
                 gather(j, 2 * h, 2 * h + 2)
-            if j > 0:
-                weigh(weighed(j - 1, (1, PACK)[j - 1], f"v_win{j}")[:, :, 0, :], vt[:, :, j - 1, :], j - 1)
+            if j == 1:
+                xd_codes = keep.tile([P, R], U32, name="xd_codes", tag="v_win1", align_bytes=64)
+                nc.vector.quantize_mx(xd_codes[:].bitcast(E4M3), xd_scales[:], xd[:].rearrange("m t p j -> m (t p j)"))
             nc.scalar.copy(vt[:, :, j, :], turn_plane(j, 2 + j % 2)[:])
             square(j, 0, CHUNKS)
         out_win = {}
@@ -176,7 +159,7 @@ def tile_attend_gwnorm_vg_kernel(tc, vT, x, cs, gl, y, us, wt, offs, out_0, out_
                 engine.memset(out_win[j][:, q : q + T // pieces].bitcast(U32), 0)
 
         for j in range(PACK):
-            clear(j, nc.gpsimd if j == LAST else nc.vector, f"out_win{j}", 1 if j == LAST else 2)
+            clear(j, nc.vector, f"out_win{j}", 2)
         for h in range(2):
             gather(LAST, 2 * h, 2 * h + 2)
 
@@ -253,32 +236,32 @@ def tile_attend_gwnorm_vg_kernel(tc, vT, x, cs, gl, y, us, wt, offs, out_0, out_
 
         def second_term(c, j0, j1):
             part = keep.tile([P, j1 - j0, P], F32, name=f"kv{c}_{j0}")
-            if c < 2:
-                nc.vector.tensor_scalar(part[:], vc[j0, j1][:, c, :, :], gg[:, c : c + 1], srl[:, c : c + 1], ALU.mult, ALU.mult)
+            src = vt[:, c, j0:j1, :]
+            if c == 0:
+                nc.vector.tensor_scalar(part[:], src, gg[:, c : c + 1], srl[:, c : c + 1], ALU.mult, ALU.mult)
             else:
                 if j0 == 0:
                     nc.scalar.activation(k[:, c : c + 1], gg[:, c : c + 1], ACT.Copy, scale=srl[:, c : c + 1])
-                nc.scalar.activation(part[:], vc[j0, j1][:, c, :, :], ACT.Copy, scale=k[:, c : c + 1])
+                nc.scalar.activation(part[:], src, ACT.Copy, scale=k[:, c : c + 1])
             kv_part[c, j0] = part
             for j in range(j0, j1):
                 kv[c, j] = part[:, j - j0, :]
 
-        def turn_back(j, c0, c1, number, copy, tag):
+        def turn_terms(j, c0, c1, terms, number):
             dv_bank = bank("dv_bank", number, [P, c1 - c0, P])
             for c in range(c0, c1):
-                turn(dv_bank[:, c - c0, :], sb[c, j], start=(c == c0), stop=False)
-                turn(dv_bank[:, c - c0, :], kv[c, j], start=False, stop=(c == c1 - 1))
-            part = keep.tile([P, c1 - c0, P], F32, name=f"dv{j}_{c0}", tag=tag)
-            copy(part[:], dv_bank[:])
-            for c in range(c0, c1):
-                dv[j, c] = (part, c - c0)
+                turn(dv_bank[:, c - c0, :], terms[c, j])
+            return dv_bank[:].rearrange("p c i -> p (c i)")
 
-        def put(copy, j, c0, c1):
-            part, first = dv[j, c0]
-            copy(out_win[j][:].indirect(slots(c0, c1)), part[:, first : first + c1 - c0, :].rearrange("p c i -> p (c i)"))
+        def turn_back(j, c0, c1, number, spare):
+            first = keep.tile([P, (c1 - c0) * P], F32, name=f"dv{j}_{c0}")
+            second = keep.tile([P, (c1 - c0) * P], F32, name=f"dw{j}_{c0}")
+            nc.scalar.copy(first[:], turn_terms(j, c0, c1, sb, number))
+            nc.scalar.activation(second[:], turn_terms(j, c0, c1, kv, spare), ACT.Copy, scale=cs2[:, j : j + 1])
+            dv[j, c0] = (first[:], second[:])
 
-        def add_put(dst, src):
-            nc.vector.tensor_tensor(dst, src, zeros[:], ALU.add)
+        def put(j, c0, c1):
+            nc.vector.tensor_tensor(out_win[j][:].indirect(slots(c0, c1)), *dv[j, c0], ALU.add)
 
         dv = {}
         out_planes = out_0.rearrange("(p j) n -> p j n", j=PACK)
@@ -305,8 +288,6 @@ def tile_attend_gwnorm_vg_kernel(tc, vT, x, cs, gl, y, us, wt, offs, out_0, out_
         second_product(0)
         nc.vector.tensor_copy(vt[:, :, LAST, :], v_bank[:])
         targets(1)
-        nc.vector.tensor_tensor(vc[1, PACK][:, :, 1:, :], vt[:, :, 2:, :],
-                                cs2_row[:, 2:, :].unsqueeze(1).to_broadcast([P, CHUNKS, 2, P]), ALU.mult)
         for c in range(1, CHUNKS):
             gradient(c)
             second_product(c)
@@ -314,27 +295,31 @@ def tile_attend_gwnorm_vg_kernel(tc, vT, x, cs, gl, y, us, wt, offs, out_0, out_
         projection(0)
         first_term(0, 0, 1)
         second_term(0, 0, 1)
-        turn_back(0, 0, 1, 2, nc.scalar.copy, "dv00")
+        turn_back(0, 0, 1, 2, 6)
         first_term(0, 1, PACK)
         projection(1)
         second_term(0, 1, PACK)
-        for j in range(1, PACK):
-            turn_back(j, 0, 1, (2, 6, 7, 0)[j], nc.scalar.copy, f"dv0{j}")
+        turn_back(1, 0, 1, 7, 0)
+        turn_back(2, 0, 1, 2, 6)
+        turn_back(3, 0, 1, 7, 0)
         for c in range(2, CHUNKS):
             projection(c)
         for c in range(1, CHUNKS):
             first_term(c, 0, 1)
             second_term(c, 0, 1)
+        for j in range(PACK):
+            put(j, 0, 1)
+        turn_back(0, 1, CHUNKS, 1, 2)
         for c in range(1, CHUNKS):
             first_term(c, 1, PACK)
             second_term(c, 1, PACK)
-        for j in range(PACK):
-            put(add_put, j, 0, 1)
-        for j in range(PACK):
-            turn_back(j, 1, CHUNKS, (2, 6, 7, 0)[j], nc.scalar.copy, f"dv1{j}")
-            put(nc.vector.tensor_copy, j, 1, CHUNKS)
+        put(0, 1, CHUNKS)
+        store(0)
+        for j in range(1, PACK):
+            turn_back(j, 1, CHUNKS, (None, 6, 0, 1)[j], (None, 7, 2, 6)[j])
+            put(j, 1, CHUNKS)
             store(j)
-        gg_bank = bank("gg_bank", 1, [P, P])
+        gg_bank = bank("gg_bank", 7, [P, P])
         turn(gg_bank[:], gg[:])
         gg_rows = keep.tile([QUADRANT, P], F32, name="gg_rows")
         nc.scalar.copy(gg_rows[:], gg_bank[0:QUADRANT, :])

@@ -93,6 +93,12 @@ def tile_attend_gwnorm_vg_kernel(tc, vT, x, cs, gl, y, us, wt, offs, out_0, out_
 
         cs2 = keep.tile([P, PACK], F32, name="cs2")
         nc.vector.tensor_tensor(cs2[:], cs4[:], cs4[:], ALU.mult)
+        cs2_bank = bank("cs2_bank", 2, [P, 2, P])
+        for j in range(2):
+            turn(cs2_bank[:, j, :], cs2[:, j : j + 1].to_broadcast([P, P]))
+        cs2_row = keep.tile([P, 2, P], F32, name="cs2_row")
+        nc.scalar.copy(cs2_row[:], cs2_bank[:])
+
         x_by_j = xs[:].rearrange("p t (m j) -> p t j m", j=PACK)
         xd = keep.tile([P, PACK, P, PACK], BF16, name="xd", align_bytes=64)
         for t in range(PACK):
@@ -140,6 +146,12 @@ def tile_attend_gwnorm_vg_kernel(tc, vT, x, cs, gl, y, us, wt, offs, out_0, out_
                 turn(v_bank[:, c, :], vg[:, j, cols(c, c + 1)])
             return v_bank
 
+        vc = {}
+
+        def weigh(j, tag):
+            vc[j] = keep.tile([P, CHUNKS, P], F32, name=f"vc{j}", tag=tag, align_bytes=64)
+            nc.vector.tensor_tensor(vc[j][:], vt[:, :, j, :], cs2_row[:, j : j + 1, :].to_broadcast([P, CHUNKS, P]), ALU.mult)
+
         def gather(j, c0, c1):
             nc.vector.tensor_copy(vg[:, j, cols(c0, c1)], v_win[j][:].indirect(slots(c0, c1)))
 
@@ -151,6 +163,7 @@ def tile_attend_gwnorm_vg_kernel(tc, vT, x, cs, gl, y, us, wt, offs, out_0, out_
                 nc.vector.quantize_mx(xd_codes[:].bitcast(E4M3), xd_scales[:], xd[:].rearrange("m t p j -> m (t p j)"))
             nc.scalar.copy(vt[:, :, j, :], turn_plane(j, 2 + j % 2)[:])
             square(j, 0, CHUNKS)
+        weigh(0, "v_win2")
         out_win = {}
 
         def clear(j, engine, tag, pieces):
@@ -169,7 +182,6 @@ def tile_attend_gwnorm_vg_kernel(tc, vT, x, cs, gl, y, us, wt, offs, out_0, out_
         rl = keep.tile([P, CHUNKS], F32, name="rl")
         s = keep.tile([P, CHUNKS], F32, name="s")
         srl = keep.tile([P, CHUNKS], F32, name="srl")
-        k = keep.tile([P, CHUNKS], F32, name="k")
         a_bank, sa_bank, b_bank, y2, gi, sb, kv, kv_part, whole = {}, {}, {}, {}, {}, {}, {}, {}, {}
 
         def lengths(c):
@@ -236,34 +248,34 @@ def tile_attend_gwnorm_vg_kernel(tc, vT, x, cs, gl, y, us, wt, offs, out_0, out_
 
         def second_term(c, j0, j1):
             part = keep.tile([P, j1 - j0, P], F32, name=f"kv{c}_{j0}")
-            src = vt[:, c, j0:j1, :]
-            if c == 0:
-                nc.vector.tensor_scalar(part[:], src, gg[:, c : c + 1], srl[:, c : c + 1], ALU.mult, ALU.mult)
-            else:
-                if j0 == 0:
-                    nc.scalar.activation(k[:, c : c + 1], gg[:, c : c + 1], ACT.Copy, scale=srl[:, c : c + 1])
-                nc.scalar.activation(part[:], src, ACT.Copy, scale=k[:, c : c + 1])
-            kv_part[c, j0] = part
+            src = vc[j0][:, c : c + 1, :] if j0 in vc else vt[:, c, j0:j1, :]
+            nc.vector.tensor_scalar(part[:], src, gg[:, c : c + 1], srl[:, c : c + 1], ALU.mult, ALU.mult)
             for j in range(j0, j1):
                 kv[c, j] = part[:, j - j0, :]
 
         def turn_terms(j, c0, c1, terms, number):
             dv_bank = bank("dv_bank", number, [P, c1 - c0, P])
             for c in range(c0, c1):
-                turn(dv_bank[:, c - c0, :], terms[c, j])
+                for n, term in enumerate(terms):
+                    turn(dv_bank[:, c - c0, :], term[c, j], start=(c == c0 and n == 0),
+                         stop=(c == c1 - 1 and n == len(terms) - 1))
             return dv_bank[:].rearrange("p c i -> p (c i)")
 
-        def turn_back(j, c0, c1, number, spare):
-            first = keep.tile([P, (c1 - c0) * P], F32, name=f"dv{j}_{c0}")
-            second = keep.tile([P, (c1 - c0) * P], F32, name=f"dw{j}_{c0}")
-            nc.scalar.copy(first[:], turn_terms(j, c0, c1, sb, number))
-            nc.scalar.activation(second[:], turn_terms(j, c0, c1, kv, spare), ACT.Copy, scale=cs2[:, j : j + 1])
-            dv[j, c0] = (first[:], second[:])
+        def leave(copy, j, c0, c1, terms, number, name):
+            part = keep.tile([P, (c1 - c0) * P], F32, name=name)
+            copy(part[:], turn_terms(j, c0, c1, terms, number))
+            return part
 
-        def put(j, c0, c1):
-            nc.vector.tensor_tensor(out_win[j][:].indirect(slots(c0, c1)), *dv[j, c0], ALU.add)
+        def times_cs2(j):
+            return lambda dst, src: nc.scalar.activation(dst, src, ACT.Copy, scale=cs2[:, j : j + 1])
 
-        dv = {}
+        def vector_put(j, c0, c1, first, second):
+            nc.vector.tensor_tensor(out_win[j][:].indirect(slots(c0, c1)), first[:], second[:], ALU.add)
+
+        def scalar_put(j, whole):
+            for c in range(0, CHUNKS, 2):
+                scalar_copy(out_win[j][:].indirect(slots(c, c + 2)), whole[:, cols(c, c + 2)])
+
         out_planes = out_0.rearrange("(p j) n -> p j n", j=PACK)
 
         def store(j, queue=nc.sync):
@@ -288,37 +300,41 @@ def tile_attend_gwnorm_vg_kernel(tc, vT, x, cs, gl, y, us, wt, offs, out_0, out_
         second_product(0)
         nc.vector.tensor_copy(vt[:, :, LAST, :], v_bank[:])
         targets(1)
+        weigh(1, "vi3")
         for c in range(1, CHUNKS):
             gradient(c)
             second_product(c)
         nc.vector.scalar_tensor_tensor(srl[:], s[:], -1.0, rl[:], ALU.mult, ALU.mult)
-        projection(0)
-        first_term(0, 0, 1)
-        second_term(0, 0, 1)
-        turn_back(0, 0, 1, 2, 6)
-        first_term(0, 1, PACK)
-        projection(1)
-        second_term(0, 1, PACK)
-        turn_back(1, 0, 1, 7, 0)
-        turn_back(2, 0, 1, 2, 6)
-        turn_back(3, 0, 1, 7, 0)
-        for c in range(2, CHUNKS):
+        for c in range(CHUNKS):
             projection(c)
-        for c in range(1, CHUNKS):
-            first_term(c, 0, 1)
+            first_term(c, 2, 3)
+            second_term(c, 2, 3)
+            if c == 0:
+                a0_first = leave(nc.scalar.copy, 2, 0, 1, (sb,), 2, "a0_first")
+                a0_second = leave(times_cs2(2), 2, 0, 1, (kv,), 6, "a0_second")
+        a_first = leave(nc.scalar.copy, 2, 1, CHUNKS, (sb,), 7, "a_first")
+        a_second = leave(times_cs2(2), 2, 1, CHUNKS, (kv,), 0, "a_second")
+        for c in range(CHUNKS):
+            first_term(c, 0, 2)
             second_term(c, 0, 1)
-        for j in range(PACK):
-            put(j, 0, 1)
-        turn_back(0, 1, CHUNKS, 1, 2)
-        for c in range(1, CHUNKS):
-            first_term(c, 1, PACK)
-            second_term(c, 1, PACK)
-        put(0, 1, CHUNKS)
+        vector_put(2, 0, 1, a0_first, a0_second)
+        b_whole = leave(nc.scalar.copy, 0, 0, CHUNKS, (sb, kv), 2, "b_whole")
+        for c in range(CHUNKS):
+            first_term(c, 3, 4)
+            second_term(c, 3, 4)
+        for c in range(CHUNKS):
+            second_term(c, 1, 2)
+        vector_put(2, 1, CHUNKS, a_first, a_second)
+        store(2)
+        c_second = leave(times_cs2(3), 3, 0, CHUNKS, (kv,), 6, "c_second")
+        scalar_put(0, b_whole)
         store(0)
-        for j in range(1, PACK):
-            turn_back(j, 1, CHUNKS, (None, 6, 0, 1)[j], (None, 7, 2, 6)[j])
-            put(j, 1, CHUNKS)
-            store(j)
+        c_first = leave(nc.vector.tensor_copy, 3, 0, CHUNKS, (sb,), 7, "c_first")
+        vector_put(3, 0, CHUNKS, c_first, c_second)
+        store(3)
+        d_whole = leave(nc.scalar.copy, 1, 0, CHUNKS, (sb, kv), 6, "d_whole")
+        scalar_put(1, d_whole)
+        store(1, nc.scalar)
         gg_bank = bank("gg_bank", 7, [P, P])
         turn(gg_bank[:], gg[:])
         gg_rows = keep.tile([QUADRANT, P], F32, name="gg_rows")

@@ -93,12 +93,6 @@ def tile_attend_gwnorm_vg_kernel(tc, vT, x, cs, gl, y, us, wt, offs, out_0, out_
 
         cs2 = keep.tile([P, PACK], F32, name="cs2")
         nc.vector.tensor_tensor(cs2[:], cs4[:], cs4[:], ALU.mult)
-        cs2_bank = bank("cs2_bank", 2, [P, 2, P])
-        for j in range(2):
-            turn(cs2_bank[:, j, :], cs2[:, j : j + 1].to_broadcast([P, P]))
-        cs2_row = keep.tile([P, 2, P], F32, name="cs2_row")
-        nc.scalar.copy(cs2_row[:], cs2_bank[:])
-
         x_by_j = xs[:].rearrange("p t (m j) -> p t j m", j=PACK)
         xd = keep.tile([P, PACK, P, PACK], BF16, name="xd", align_bytes=64)
         for t in range(PACK):
@@ -120,6 +114,11 @@ def tile_attend_gwnorm_vg_kernel(tc, vT, x, cs, gl, y, us, wt, offs, out_0, out_
         nc.vector.scalar_tensor_tensor(c2n[:], wt4[:], -1.0, us4[:], ALU.mult, ALU.mult)
         c1 = keep.tile([P, PACK], F32, name="c1")
         nc.vector.scalar_tensor_tensor(c1[:], c2n[:], -1.0, us4[:], ALU.mult, ALU.mult)
+        cs2_bank = bank("cs2_bank", 0, [P, 1, P])
+        turn(cs2_bank[:, 0, :], cs2[:, 1:2].to_broadcast([P, P]))
+        cs2_row = keep.tile([P, 1, P], F32, name="cs2_row")
+        nc.scalar.copy(cs2_row[:], cs2_bank[:])
+
         gl_g = keep.tile([P, N], F32, name="gl_g")
         nc.vector.tensor_copy(gl_g[:], gl_win[:].indirect(offsets[:]))
         gl_bank = bank("gl_bank", 3, [P, CHUNKS, P])
@@ -150,7 +149,16 @@ def tile_attend_gwnorm_vg_kernel(tc, vT, x, cs, gl, y, us, wt, offs, out_0, out_
 
         def weigh(j, tag):
             vc[j] = keep.tile([P, CHUNKS, P], F32, name=f"vc{j}", tag=tag, align_bytes=64)
-            nc.vector.tensor_tensor(vc[j][:], vt[:, :, j, :], cs2_row[:, j : j + 1, :].to_broadcast([P, CHUNKS, P]), ALU.mult)
+            nc.vector.tensor_tensor(vc[j][:], vt[:, :, j, :], cs2_row[:].to_broadcast([P, CHUNKS, P]), ALU.mult)
+
+        def weigh_turned(j, number):
+            cv = ring.tile([P, N], F32, name="cv")
+            nc.scalar.activation(cv[:], vg[:, j, :], ACT.Copy, scale=cs2[:, j : j + 1])
+            cv_bank = bank("cv_bank", number, [P, CHUNKS, P])
+            for c in range(CHUNKS):
+                turn(cv_bank[:, c, :], cv[:, cols(c, c + 1)])
+            vc[j] = keep.tile([P, CHUNKS, P], F32, name=f"vc{j}")
+            nc.scalar.copy(vc[j][:], cv_bank[:])
 
         def gather(j, c0, c1):
             nc.vector.tensor_copy(vg[:, j, cols(c0, c1)], v_win[j][:].indirect(slots(c0, c1)))
@@ -163,7 +171,7 @@ def tile_attend_gwnorm_vg_kernel(tc, vT, x, cs, gl, y, us, wt, offs, out_0, out_
                 nc.vector.quantize_mx(xd_codes[:].bitcast(E4M3), xd_scales[:], xd[:].rearrange("m t p j -> m (t p j)"))
             nc.scalar.copy(vt[:, :, j, :], turn_plane(j, 2 + j % 2)[:])
             square(j, 0, CHUNKS)
-        weigh(0, "v_win2")
+        weigh_turned(0, 0)
         out_win = {}
 
         def clear(j, engine, tag, pieces):
@@ -236,7 +244,7 @@ def tile_attend_gwnorm_vg_kernel(tc, vT, x, cs, gl, y, us, wt, offs, out_0, out_
                                 xr_codes[:].bitcast(E4M3), xr_scales[:], start=True, stop=True)
 
         def projection(c):
-            products = ring.tile([P, PACK, P], F32, name="products")
+            products = (keep if c == 0 else ring).tile([P, PACK, P], F32, name="g3" if c == 0 else "products")
             nc.vector.scalar_tensor_tensor(products[:], b_bank[c][:], rl[:, c : c + 1], vt[:, c, :, :], ALU.mult, ALU.mult,
                                            accum_out=gg[:, c : c + 1])
 

@@ -71,15 +71,15 @@ def tile_attend_gwnorm_vg_kernel(tc, vT, x, cs, gl, y, us, wt, offs, out_0, out_
         for t in range(0, PACK, 2):
             nc.sync.dma_start(xs[:, t : t + 2, :], x_planes[:, t : t + 2, :])
         nc.sync.dma_start(offsets[:], offs)
-        us4 = keep.tile([P, PACK], F32, name="us4")
-        nc.sync.dma_start(us4[:], us.rearrange("(p t) o -> p (t o)", t=PACK))
-        wt4 = keep.tile([P, PACK], F32, name="wt4")
-        nc.sync.dma_start(wt4[:], wt.rearrange("(p t) o -> p (t o)", t=PACK))
         v_planes = vT.rearrange("(p j) n -> p j n", j=PACK)
         v_win = []
         for j in range(PACK):
             v_win.append(keep.tile([P, T], F32, name=f"v_win{j}", align_bytes=64))
             nc.sync.dma_start(v_win[j][:], v_planes[:, j, :])
+        us4 = keep.tile([P, PACK], F32, name="us4")
+        nc.sync.dma_start(us4[:], us.rearrange("(p t) o -> p (t o)", t=PACK))
+        wt4 = keep.tile([P, PACK], F32, name="wt4")
+        nc.sync.dma_start(wt4[:], wt.rearrange("(p t) o -> p (t o)", t=PACK))
         y_planes = y.rearrange("(p t) i -> p t i", t=PACK)
         ys = []
         for h in range(2):

@@ -24,7 +24,7 @@ LIST_COLS = P // 16
 LINE = 4
 QUADRANT = 32
 LAST = PACK - 1
-GL_RUN = T // P
+GL_ROW = P - 1
 
 
 def tile_attend_gwnorm_vg_kernel(tc, vT, x, cs, gl, y, us, wt, offs, out_0, out_1):
@@ -59,17 +59,15 @@ def tile_attend_gwnorm_vg_kernel(tc, vT, x, cs, gl, y, us, wt, offs, out_0, out_
         warm_out = keep.tile([P, 1], F32, name="warm_out")
         nc.scalar.activation(warm_out[:], warm_in[:], ACT.Abs_reciprocal_sqrt)
 
-        gl_row = keep.tile([1, T], F32, name="gl_row")
-        nc.sync.dma_start(gl_row[:], gl[0:1, :])
-        gl_win = keep.tile([P, T], F32, name="gl_win")
-        nc.vector.memset(gl_win[:].bitcast(U32), 0)
-        scalar_copy(gl_win[0:1, :], gl_row[:])
-        cs4 = keep.tile([P, PACK], F32, name="cs4")
-        nc.sync.dma_start(cs4[:], cs[0:1, :].rearrange("o (p j) -> p (o j)", j=PACK))
         xs = keep.tile([P, PACK, D], F32, name="xs")
         x_planes = x.rearrange("(p t) d -> p t d", t=PACK)
         for t in range(0, PACK, 2):
             nc.sync.dma_start(xs[:, t : t + 2, :], x_planes[:, t : t + 2, :])
+        gl_win = keep.tile([P, T], F32, name="gl_win")
+        nc.sync.dma_start(gl_win[GL_ROW:P, :], gl[0:1, :])
+        nc.vector.memset(gl_win[0:GL_ROW, :].bitcast(U32), 0)
+        cs4 = keep.tile([P, PACK], F32, name="cs4")
+        nc.sync.dma_start(cs4[:], cs[0:1, :].rearrange("o (p j) -> p (o j)", j=PACK))
         nc.sync.dma_start(offsets[:], offs)
         v_planes = vT.rearrange("(p j) n -> p j n", j=PACK)
         v_win = []
@@ -120,12 +118,12 @@ def tile_attend_gwnorm_vg_kernel(tc, vT, x, cs, gl, y, us, wt, offs, out_0, out_
         nc.scalar.copy(cs2_row[:], cs2_bank[:])
 
         gl_g = keep.tile([P, N], F32, name="gl_g")
-        nc.vector.tensor_copy(gl_g[:], gl_win[:].indirect(offsets[:]))
+        scalar_copy(gl_g[:], gl_win[:].indirect(offsets[:]))
         gl_bank = bank("gl_bank", 3, [P, CHUNKS, P])
         for c in range(CHUNKS):
             turn(gl_bank[:, c, :], gl_g[:, cols(c, c + 1)])
         gl_col = keep.tile([P, CHUNKS], F32, name="gl_col", align_bytes=64)
-        nc.scalar.copy(gl_col[:], gl_bank[:, :, 0])
+        nc.scalar.copy(gl_col[:], gl_bank[:, :, GL_ROW])
 
         vg = keep.tile([P, PACK, N], F32, name="vg")
         vt = keep.tile([P, CHUNKS, PACK, P], F32, name="vt", align_bytes=64)

@@ -89,6 +89,8 @@ def tile_attend_gwnorm_vg_kernel(tc, vT, x, cs, gl, y, us, wt, offs, out_0, out_
         gg = keep.tile([P, P], F32, name="gg")
         nc.gpsimd.memset(gg[:], 0.0)
 
+        unit = keep.tile([P, 1], F32, name="unit")
+        nc.vector.memset(unit[:], 1.0)
         cs2 = keep.tile([P, PACK], F32, name="cs2")
         nc.vector.tensor_tensor(cs2[:], cs4[:], cs4[:], ALU.mult)
         x_by_j = xs[:].rearrange("p t (m j) -> p t j m", j=PACK)
@@ -279,8 +281,7 @@ def tile_attend_gwnorm_vg_kernel(tc, vT, x, cs, gl, y, us, wt, offs, out_0, out_
             nc.vector.tensor_tensor(out_win[j][:].indirect(slots(c0, c1)), first[:], second[:], ALU.add)
 
         def scalar_put(j, whole):
-            for c in range(0, CHUNKS, 2):
-                scalar_copy(out_win[j][:].indirect(slots(c, c + 2)), whole[:, cols(c, c + 2)])
+            nc.scalar.activation(out_win[j][:].indirect(offsets[:]), whole[:], ACT.Copy, scale=unit[:])
 
         out_planes = out_0.rearrange("(p j) n -> p j n", j=PACK)
 
@@ -311,6 +312,8 @@ def tile_attend_gwnorm_vg_kernel(tc, vT, x, cs, gl, y, us, wt, offs, out_0, out_
             gradient(c)
             second_product(c)
         nc.vector.scalar_tensor_tensor(srl[:], s[:], -1.0, rl[:], ALU.mult, ALU.mult)
+        a_first = keep.tile([P, LAST * P], F32, name="a_first")
+        a_second = keep.tile([P, LAST * P], F32, name="a_second")
         for c in range(CHUNKS):
             projection(c)
             first_term(c, 2, 3)
@@ -318,13 +321,16 @@ def tile_attend_gwnorm_vg_kernel(tc, vT, x, cs, gl, y, us, wt, offs, out_0, out_
             if c == 0:
                 a0_first = leave(nc.scalar.copy, 2, 0, 1, (sb,), 2, "a0_first")
                 a0_second = leave(times_cs2(2), 2, 0, 1, (kv,), 6, "a0_second")
-        a_first = leave(nc.scalar.copy, 2, 1, CHUNKS, (sb,), 7, "a_first")
-        a_second = leave(times_cs2(2), 2, 1, CHUNKS, (kv,), 0, "a_second")
+            if c == 2:
+                nc.scalar.copy(a_first[:, cols(0, 2)], turn_terms(2, 1, LAST, (sb,), 7))
+                times_cs2(2)(a_second[:, cols(0, 2)], turn_terms(2, 1, LAST, (kv,), 0))
+        nc.scalar.copy(a_first[:, cols(2, LAST)], turn_terms(2, LAST, CHUNKS, (sb,), 2))
+        times_cs2(2)(a_second[:, cols(2, LAST)], turn_terms(2, LAST, CHUNKS, (kv,), 6))
         for c in range(CHUNKS):
             first_term(c, 0, 2)
             second_term(c, 0, 1)
         vector_put(2, 0, 1, a0_first, a0_second)
-        b_whole = leave(nc.scalar.copy, 0, 0, CHUNKS, (sb, kv), 2, "b_whole")
+        b_whole = leave(nc.scalar.copy, 0, 0, CHUNKS, (sb, kv), 1, "b_whole")
         for c in range(CHUNKS):
             first_term(c, 3, 4)
             second_term(c, 3, 4)

@@ -201,13 +201,13 @@ def tile_attend_gwnorm_vg_kernel(tc, vT, x, cs, gl, y, us, wt, offs, out_0, out_
 
         vi = {}
 
-        def weave_v(c):
-            vi[c] = keep.tile([P, P, PACK], BF16, name=f"vi{c}", align_bytes=64)
-            interleave(nc.vector.tensor_copy, vi[c][:], vg[:, :, cols(c, c + 1)])
+        def weave_v(h):
+            vi[h] = keep.tile([P, HALF, PACK], BF16, name=f"vi{h}", align_bytes=64)
+            interleave(nc.vector.tensor_copy, vi[h][:], vg[:, :, cols(2 * h, 2 * h + 2)])
 
-        def quantise_v(c):
-            run = cols(c, c + 1)
-            nc.vector.quantize_mx(v_codes[:, run].bitcast(E4M3), v_scales[:, run], vi[c][:].rearrange("p i j -> p (i j)"))
+        def quantise_v(h):
+            run = cols(2 * h, 2 * h + 2)
+            nc.vector.quantize_mx(v_codes[:, run].bitcast(E4M3), v_scales[:, run], vi[h][:].rearrange("p i j -> p (i j)"))
 
         def first_product(c):
             run = cols(c, c + 1)
@@ -291,9 +291,9 @@ def tile_attend_gwnorm_vg_kernel(tc, vT, x, cs, gl, y, us, wt, offs, out_0, out_
         for h in range(2):
             square(LAST, 2 * h, 2 * h + 2)
         v_bank = turn_plane(LAST, 3)
-        for c in range(CHUNKS):
-            weave_v(c)
-            quantise_v(c)
+        for h in range(2):
+            weave_v(h)
+            quantise_v(h)
         for c in range(CHUNKS):
             lengths(c)
         for c in range(LAST):
@@ -307,7 +307,7 @@ def tile_attend_gwnorm_vg_kernel(tc, vT, x, cs, gl, y, us, wt, offs, out_0, out_
         second_product(0)
         nc.vector.tensor_copy(vt[:, :, LAST, :], v_bank[:])
         targets(1)
-        weigh(1, "vi3")
+        weigh(1, "vi1")
         for c in range(1, CHUNKS):
             gradient(c)
             second_product(c)
@@ -317,7 +317,7 @@ def tile_attend_gwnorm_vg_kernel(tc, vT, x, cs, gl, y, us, wt, offs, out_0, out_
         for c in range(CHUNKS):
             projection(c)
             first_term(c, 2, 3)
-            second_term(c, 2, 3)
+            second_term(c, 2, PACK if c < LAST else LAST)
             if c == 0:
                 a0_first = leave(nc.scalar.copy, 2, 0, 1, (sb,), 2, "a0_first")
                 a0_second = leave(times_cs2(2), 2, 0, 1, (kv,), 6, "a0_second")
@@ -333,7 +333,7 @@ def tile_attend_gwnorm_vg_kernel(tc, vT, x, cs, gl, y, us, wt, offs, out_0, out_
         b_whole = leave(nc.scalar.copy, 0, 0, CHUNKS, (sb, kv), 1, "b_whole")
         for c in range(CHUNKS):
             first_term(c, 3, 4)
-            second_term(c, 3, 4)
+        second_term(LAST, LAST, PACK)
         for c in range(CHUNKS):
             second_term(c, 1, 2)
         vector_put(2, 1, CHUNKS, a_first, a_second)

from contextlib import ExitStack

import concourse.mybir as mybir
from concourse.masks import make_identity

D, R, N, T = 512, 512, 512, 2048
FLOPS = 2 * 2 * D * R * N

F32 = mybir.dt.float32
BF16 = mybir.dt.bfloat16
U32 = mybir.dt.uint32
U16 = mybir.dt.uint16
U8 = mybir.dt.uint8
E4M3 = mybir.dt.float8_e4m3fn_x4
E5M2 = mybir.dt.float8_e5m2_x4
ACT = mybir.ActivationFunctionType
ALU = mybir.AluOpType

P = 128
PACK = 4
CHUNKS = N // P
HALF = N // 2
LIST_COLS = P // 16
LINE = 4
QUADRANT = 32
LAST = PACK - 1
GL_ROW = P - 1


def tile_attend_gwnorm_vg_kernel(tc, vT, x, cs, gl, y, us, wt, offs, out_0, out_1):
    nc = tc.nc
    with ExitStack() as ctx:
        keep = ctx.enter_context(tc.tile_pool(name="keep", bufs=1))
        ring = ctx.enter_context(tc.tile_pool(name="ring", bufs=2))
        psum = ctx.enter_context(tc.psum_pool(name="psum", bufs=1))

        def bank(name, number, shape):
            return psum.tile(shape, F32, name=name, tag=f"bank{number}")

        def turn(dst, src, start=True, stop=True):
            nc.tensor.matmul(dst, src, ident[:], start=start, stop=stop, is_transpose=True)

        def slots(c0, c1):
            return offsets[:, c0 * LIST_COLS : c1 * LIST_COLS]

        def cols(c0, c1):
            return slice(c0 * P, c1 * P)

        def interleave(copy, dst, src):
            copy(dst.rearrange("p (c i) j -> p c j i", i=LINE), src.rearrange("p j (c i) -> p c j i", i=LINE))

        def scalar_copy(dst, src):
            nc.scalar.activation(dst, src, ACT.Copy)

        offsets = keep.tile([P, N // 16], U16, name="offsets")

        warm_in = keep.tile([P, 1], F32, name="warm_in")
        nc.vector.memset(warm_in[:], 1.0)
        warm_out = keep.tile([P, 1], F32, name="warm_out")
        nc.scalar.activation(warm_out[:], warm_in[:], ACT.Abs_reciprocal_sqrt)

        xs = keep.tile([P, PACK, D], F32, name="xs")
        x_planes = x.rearrange("(p t) d -> p t d", t=PACK)
        for t in range(0, PACK, 2):
            nc.sync.dma_start(xs[:, t : t + 2, :], x_planes[:, t : t + 2, :])
        gl_win = keep.tile([P, T], F32, name="gl_win")
        nc.sync.dma_start(gl_win[GL_ROW:P, :], gl[0:1, :])
        nc.vector.memset(gl_win[0:GL_ROW, :].bitcast(U32), 0)
        cs4 = keep.tile([P, PACK], F32, name="cs4")
        nc.sync.dma_start(cs4[:], cs[0:1, :].rearrange("o (p j) -> p (o j)", j=PACK))
        nc.sync.dma_start(offsets[:], offs)
        v_planes = vT.rearrange("(p j) n -> p j n", j=PACK)
        v_win = []
        for j in range(PACK):
            v_win.append(keep.tile([P, T], F32, name=f"v_win{j}", align_bytes=64))
            nc.sync.dma_start(v_win[j][:], v_planes[:, j, :])
        us4 = keep.tile([P, PACK], F32, name="us4")
        nc.sync.dma_start(us4[:], us.rearrange("(p t) o -> p (t o)", t=PACK))
        wt4 = keep.tile([P, PACK], F32, name="wt4")
        nc.sync.dma_start(wt4[:], wt.rearrange("(p t) o -> p (t o)", t=PACK))
        y_planes = y.rearrange("(p t) i -> p t i", t=PACK)
        ys = []
        for h in range(2):
            ys.append(keep.tile([P, PACK, HALF], F32, name=f"ys{h}", align_bytes=64))
            nc.sync.dma_start(ys[h][:], y_planes[:, :, h * HALF : (h + 1) * HALF])

        ident = keep.tile([P, P], F32, name="ident")
        make_identity(nc, ident[:])
        gg = keep.tile([P, P], F32, name="gg")
        nc.gpsimd.memset(gg[:], 0.0)

        unit = keep.tile([P, 1], F32, name="unit")
        nc.vector.memset(unit[:], 1.0)
        cs2 = keep.tile([P, PACK], F32, name="cs2")
        nc.vector.tensor_tensor(cs2[:], cs4[:], cs4[:], ALU.mult)
        x_by_j = xs[:].rearrange("p t (m j) -> p t j m", j=PACK)
        xd = keep.tile([P, PACK, P, PACK], BF16, name="xd", align_bytes=64)
        for t in range(PACK):
            x_bank = bank("x_bank", (0, 1, 4, 5)[t], [P, PACK, P])
            for j in range(PACK):
                turn(x_bank[:, j, :], x_by_j[:, t, j, :])
            nc.scalar.copy(xd[:, t, :, :], x_bank[:].rearrange("m j p -> m p j"))
        xr = keep.tile([P, PACK, P, PACK], BF16, name="xr", align_bytes=64)
        xr_walk = xr[:].rearrange("p j m t -> p m t j")
        xs_walk = xs[:].rearrange("p t (m j) -> p m t j", j=PACK)
        nc.vector.tensor_copy(xr_walk[:, : P // 2], xs_walk[:, : P // 2])
        nc.scalar.copy(xr_walk[:, P // 2 :], xs_walk[:, P // 2 :])
        xd_scales = keep.tile([P, R], U8, name="xd_scales", align_bytes=64)
        xr_codes = keep.tile([P, D], U32, name="xr_codes", align_bytes=64)
        xr_scales = keep.tile([P, D], U8, name="xr_scales", align_bytes=64)
        nc.vector.quantize_mx(xr_codes[:].bitcast(E4M3), xr_scales[:], xr[:].rearrange("p j m t -> p (j m t)"))

        c2n = keep.tile([P, PACK], F32, name="c2n")
        nc.vector.scalar_tensor_tensor(c2n[:], wt4[:], -1.0, us4[:], ALU.mult, ALU.mult)
        c1 = keep.tile([P, PACK], F32, name="c1")
        nc.vector.scalar_tensor_tensor(c1[:], c2n[:], -1.0, us4[:], ALU.mult, ALU.mult)
        cs2_bank = bank("cs2_bank", 0, [P, 1, P])
        turn(cs2_bank[:, 0, :], cs2[:, 1:2].to_broadcast([P, P]))
        cs2_row = keep.tile([P, 1, P], F32, name="cs2_row")
        nc.scalar.copy(cs2_row[:], cs2_bank[:])

        gl_g = keep.tile([P, N], F32, name="gl_g")
        scalar_copy(gl_g[:], gl_win[:].indirect(offsets[:]))
        gl_bank = bank("gl_bank", 3, [P, CHUNKS, P])
        for c in range(CHUNKS):
            turn(gl_bank[:, c, :], gl_g[:, cols(c, c + 1)])
        gl_col = keep.tile([P, CHUNKS], F32, name="gl_col", align_bytes=64)
        nc.scalar.copy(gl_col[:], gl_bank[:, :, GL_ROW])

        vg = keep.tile([P, PACK, N], F32, name="vg")
        vt = keep.tile([P, CHUNKS, PACK, P], F32, name="vt", align_bytes=64)
        nn_bank = [bank(f"nn_bank{h}", 6 + h, [P, 2, P]) for h in range(2)]

        def square(j, c0, c1):
            sq = ring.tile([P, N], F32, name="sq", bufs=CHUNKS)
            run = cols(c0, c1)
            nc.scalar.activation(sq[:, run], vg[:, j, run], ACT.Square, scale=cs4[:, j : j + 1])
            for c in range(c0, c1):
                turn(nn_bank[c // 2][:, c % 2, :], sq[:, cols(c, c + 1)],
                     start=(j == 0 and c % 2 == 0), stop=(j == LAST and c % 2 == 1))

        def turn_plane(j, number):
            v_bank = bank("v_bank", number, [P, CHUNKS, P])
            for c in range(CHUNKS):
                turn(v_bank[:, c, :], vg[:, j, cols(c, c + 1)])
            return v_bank

        vc = {}

        def weigh(j, tag):
            vc[j] = keep.tile([P, CHUNKS, P], F32, name=f"vc{j}", tag=tag, align_bytes=64)
            nc.vector.tensor_tensor(vc[j][:], vt[:, :, j, :], cs2_row[:].to_broadcast([P, CHUNKS, P]), ALU.mult)

        def weigh_turned(j, number):
            cv = ring.tile([P, N], F32, name="cv")
            nc.scalar.activation(cv[:], vg[:, j, :], ACT.Copy, scale=cs2[:, j : j + 1])
            cv_bank = bank("cv_bank", number, [P, CHUNKS, P])
            for c in range(CHUNKS):
                turn(cv_bank[:, c, :], cv[:, cols(c, c + 1)])
            vc[j] = keep.tile([P, CHUNKS, P], F32, name=f"vc{j}")
            nc.scalar.copy(vc[j][:], cv_bank[:])

        def gather(j, c0, c1):
            nc.vector.tensor_copy(vg[:, j, cols(c0, c1)], v_win[j][:].indirect(slots(c0, c1)))

        for j in range(LAST):
            for h in range(2):
                gather(j, 2 * h, 2 * h + 2)
            if j == 1:
                xd_codes = keep.tile([P, R], U32, name="xd_codes", tag="v_win1", align_bytes=64)
                nc.vector.quantize_mx(xd_codes[:].bitcast(E4M3), xd_scales[:], xd[:].rearrange("m t p j -> m (t p j)"))
            nc.scalar.copy(vt[:, :, j, :], turn_plane(j, 2 + j % 2)[:])
            square(j, 0, CHUNKS)
        weigh_turned(0, 0)
        out_win = {}

        def clear(j, engine, tag, pieces):
            out_win[j] = keep.tile([P, T], F32, name=f"out_win{j}", tag=tag, align_bytes=64)
            for q in range(0, T, T // pieces):
                engine.memset(out_win[j][:, q : q + T // pieces].bitcast(U32), 0)

        for j in range(PACK):
            clear(j, nc.vector, f"out_win{j}", 2)
        for h in range(2):
            gather(LAST, 2 * h, 2 * h + 2)

        v_codes = keep.tile([P, N], U32, name="v_codes", align_bytes=64)
        v_scales = keep.tile([P, N], U8, name="v_scales", align_bytes=64)
        nn = keep.tile([P, CHUNKS], F32, name="nn")
        rl = keep.tile([P, CHUNKS], F32, name="rl")
        s = keep.tile([P, CHUNKS], F32, name="s")
        srl = keep.tile([P, CHUNKS], F32, name="srl")
        a_bank, sa_bank, b_bank, y2, gi, sb, kv, kv_part, whole = {}, {}, {}, {}, {}, {}, {}, {}, {}

        def lengths(c):
            one = slice(c, c + 1)
            terms = ring.tile([P, P], F32, name="terms")
            nc.scalar.activation(terms[:], nn_bank[c // 2][:, c % 2, :], ACT.Copy, accum_out=nn[:, one])
            nc.scalar.activation(rl[:, one], nn[:, one], ACT.Abs_reciprocal_sqrt)
            nc.scalar.activation(s[:, one], rl[:, one], ACT.Copy, scale=gl_col[:, one])

        vi = {}

        def weave_v(h):
            vi[h] = keep.tile([P, HALF, PACK], BF16, name=f"vi{h}", align_bytes=64)
            interleave(nc.vector.tensor_copy, vi[h][:], vg[:, :, cols(2 * h, 2 * h + 2)])

        def quantise_v(h):
            run = cols(2 * h, 2 * h + 2)
            nc.vector.quantize_mx(v_codes[:, run].bitcast(E4M3), v_scales[:, run], vi[h][:].rearrange("p i j -> p (i j)"))

        def first_product(c):
            run = cols(c, c + 1)
            a_bank[c] = bank("a_bank", (0, 1, 4, 5)[c], [P, R])
            nc.tensor.matmul_mx(a_bank[c][:], v_codes[:, run].bitcast(E4M3), v_scales[:, run],
                                xd_codes[:].bitcast(E4M3), xd_scales[:], start=True, stop=True)

        def scale_and_turn(c):
            sa = ring.tile([P, PACK, P], F32, name="sa", bufs=CHUNKS)
            nc.scalar.activation(sa[:].rearrange("i t p -> i (t p)"), a_bank[c][:], ACT.Copy, scale=s[:, c : c + 1])
            sa_bank[c] = bank("sa_bank", (2, 6, 7, 0)[c], [P, PACK, P])
            for t in range(PACK):
                turn(sa_bank[c][:, t, :], sa[:, t, :])

        def targets(h):
            y2[h] = keep.tile([P, PACK, HALF], F32, name=f"y2_{h}", align_bytes=64)
            for t in range(PACK):
                nc.vector.tensor_scalar(y2[h][:, t, :], ys[h][:, t, :], c2n[:, t : t + 1], None, ALU.mult)

        def gradient(c):
            g = keep.tile([P, PACK, P], BF16, name=f"g{c}")
            for t in range(PACK):
                nc.vector.scalar_tensor_tensor(g[:, t, :], sa_bank[c][:, t, :], c1[:, t : t + 1],
                                               y2[c // 2][:, t, cols(c % 2, c % 2 + 1)], ALU.mult, ALU.add)
            gi[c] = keep.tile([P, P, PACK], BF16, name=f"gi{c}", align_bytes=64)
            interleave(nc.vector.tensor_copy if c == LAST else nc.scalar.copy, gi[c][:], g[:])

        def second_product(c):
            g_codes = keep.tile([P, P], U32, name=f"g_codes{c}", align_bytes=64)
            g_scales = keep.tile([P, P], U8, name=f"g_scales{c}", align_bytes=64)
            nc.vector.quantize_mx(g_codes[:].bitcast(E5M2), g_scales[:], gi[c][:].rearrange("p i t -> p (i t)"))
            b_bank[c] = bank("b_bank", (1, 4, 3, 5)[c], [P, PACK, P])
            nc.tensor.matmul_mx(b_bank[c][:].rearrange("i j p -> i (j p)"), g_codes[:].bitcast(E5M2), g_scales[:],
                                xr_codes[:].bitcast(E4M3), xr_scales[:], start=True, stop=True)

        def projection(c):
            products = (keep if c == 0 else ring).tile([P, PACK, P], F32, name="g3" if c == 0 else "products")
            nc.vector.scalar_tensor_tensor(products[:], b_bank[c][:], rl[:, c : c + 1], vt[:, c, :, :], ALU.mult, ALU.mult,
                                           accum_out=gg[:, c : c + 1])

        def first_term(c, j0, j1):
            part = keep.tile([P, j1 - j0, P], F32, name=f"sb{c}_{j0}")
            nc.scalar.activation(part[:], b_bank[c][:, j0:j1, :], ACT.Copy, scale=s[:, c : c + 1])
            for j in range(j0, j1):
                sb[c, j] = part[:, j - j0, :]

        def second_term(c, j0, j1):
            part = keep.tile([P, j1 - j0, P], F32, name=f"kv{c}_{j0}")
            src = vc[j0][:, c : c + 1, :] if j0 in vc else vt[:, c, j0:j1, :]
            nc.vector.tensor_scalar(part[:], src, gg[:, c : c + 1], srl[:, c : c + 1], ALU.mult, ALU.mult)
            for j in range(j0, j1):
                kv[c, j] = part[:, j - j0, :]

        def turn_terms(j, c0, c1, terms, number):
            dv_bank = bank("dv_bank", number, [P, c1 - c0, P])
            for c in range(c0, c1):
                for n, term in enumerate(terms):
                    turn(dv_bank[:, c - c0, :], term[c, j], start=(c == c0 and n == 0),
                         stop=(c == c1 - 1 and n == len(terms) - 1))
            return dv_bank[:].rearrange("p c i -> p (c i)")

        def leave(copy, j, c0, c1, terms, number, name):
            part = keep.tile([P, (c1 - c0) * P], F32, name=name)
            copy(part[:], turn_terms(j, c0, c1, terms, number))
            return part

        def times_cs2(j):
            return lambda dst, src: nc.scalar.activation(dst, src, ACT.Copy, scale=cs2[:, j : j + 1])

        def vector_put(j, c0, c1, first, second):
            nc.vector.tensor_tensor(out_win[j][:].indirect(slots(c0, c1)), first[:], second[:], ALU.add)

        def scalar_put(j, whole):
            nc.scalar.activation(out_win[j][:].indirect(offsets[:]), whole[:], ACT.Copy, scale=unit[:])

        out_planes = out_0.rearrange("(p j) n -> p j n", j=PACK)

        def store(j, queue=nc.sync):
            queue.dma_start(out_planes[:, j, :], out_win[j][:])

        for h in range(2):
            square(LAST, 2 * h, 2 * h + 2)
        v_bank = turn_plane(LAST, 3)
        for h in range(2):
            weave_v(h)
            quantise_v(h)
        for c in range(CHUNKS):
            lengths(c)
        for c in range(LAST):
            first_product(c)
        scale_and_turn(0)
        first_product(LAST)
        for c in range(1, CHUNKS):
            scale_and_turn(c)
        targets(0)
        gradient(0)
        second_product(0)
        nc.vector.tensor_copy(vt[:, :, LAST, :], v_bank[:])
        targets(1)
        weigh(1, "vi1")
        for c in range(1, CHUNKS):
            gradient(c)
            second_product(c)
        nc.vector.scalar_tensor_tensor(srl[:], s[:], -1.0, rl[:], ALU.mult, ALU.mult)
        a_first = keep.tile([P, LAST * P], F32, name="a_first")
        a_second = keep.tile([P, LAST * P], F32, name="a_second")
        for c in range(CHUNKS):
            projection(c)
            first_term(c, 2, 3)
            second_term(c, 2, PACK if c < LAST else LAST)
            if c == 0:
                a0_first = leave(nc.scalar.copy, 2, 0, 1, (sb,), 2, "a0_first")
                a0_second = leave(times_cs2(2), 2, 0, 1, (kv,), 6, "a0_second")
            if c == 2:
                nc.scalar.copy(a_first[:, cols(0, 2)], turn_terms(2, 1, LAST, (sb,), 7))
                times_cs2(2)(a_second[:, cols(0, 2)], turn_terms(2, 1, LAST, (kv,), 0))
        nc.scalar.copy(a_first[:, cols(2, LAST)], turn_terms(2, LAST, CHUNKS, (sb,), 2))
        times_cs2(2)(a_second[:, cols(2, LAST)], turn_terms(2, LAST, CHUNKS, (kv,), 6))
        for c in range(CHUNKS):
            first_term(c, 0, 2)
            second_term(c, 0, 1)
        vector_put(2, 0, 1, a0_first, a0_second)
        b_whole = leave(nc.scalar.copy, 0, 0, CHUNKS, (sb, kv), 1, "b_whole")
        for c in range(CHUNKS):
            first_term(c, 3, 4)
        second_term(LAST, LAST, PACK)
        for c in range(CHUNKS):
            second_term(c, 1, 2)
        vector_put(2, 1, CHUNKS, a_first, a_second)
        store(2)
        c_second = leave(times_cs2(3), 3, 0, CHUNKS, (kv,), 6, "c_second")
        scalar_put(0, b_whole)
        store(0)
        c_first = leave(nc.vector.tensor_copy, 3, 0, CHUNKS, (sb,), 7, "c_first")
        vector_put(3, 0, CHUNKS, c_first, c_second)
        store(3)
        d_whole = leave(nc.scalar.copy, 1, 0, CHUNKS, (sb, kv), 6, "d_whole")
        scalar_put(1, d_whole)
        store(1, nc.scalar)
        gg_bank = bank("gg_bank", 7, [P, P])
        turn(gg_bank[:], gg[:])
        gg_rows = keep.tile([QUADRANT, P], F32, name="gg_rows")
        nc.scalar.copy(gg_rows[:], gg_bank[0:QUADRANT, :])
        nc.sync.dma_start(out_1.rearrange("o (c i) -> (o c) i", c=CHUNKS), gg_rows[0:CHUNKS, :])
